import numpy as np, ml_dtypes
CORES = [113,118,241,246]
N = 4
BF = ml_dtypes.bfloat16
def gentries(a):
    return np.ascontiguousarray(a.reshape(8, 16, -1).transpose(0, 2, 1)).reshape(8, -1)
def gtable(e):
    e = np.asarray(e); return np.ascontiguousarray(e.reshape(8, -1, 16).transpose(0, 2, 1)).reshape(128, -1).astype(np.int32)
V, B, T, S, LH = 2048, 256, 192, 7, 2
M = V + T * S
def rows_of(rng, u):
    y = np.sort((u * (V - 15)).astype(np.int64), axis=-1) + np.arange(16)
    return rng.permuted(y, axis=-1)
def homes(rng, sb):
    he = rng.integers(0, B, (N, 8, V))
    for r in range(N):
        for g in range(8):
            o = rng.permutation(16 * B); he[r, g, sb[r, g].reshape(-1)[o]] = o >> 4
    return he
def parts(rng):
    sb = rows_of(rng, rng.random((N, 8, B, 16))); he = homes(rng, sb)
    x = rng.integers(0, 64, (N, 8, 16, V)); z = rng.integers(0, 64, (N, 8, 16, T))
    pe = (B * rng.random((N, 8, V)) ** 2).astype(np.int64); bx = (B * rng.random((N, 8, T)) ** 2).astype(np.int64)
    lim = np.stack([rng.integers(100, 450, (N, 8)), rng.integers(180, 320, (N, 8))], axis=-1)
    return x, sb, pe, he, bx, z, lim
def pack(x, sb, pe, he, bx, z, lim):
    w = lambda a: np.ascontiguousarray(a).astype(np.int32)
    return {"xs": x.reshape(N, 128, V).astype(np.float32).astype(BF), "sb": np.stack([gtable(a.reshape(8, -1)) for a in sb]), "pe": w(pe), "he": w(he),
            "bx": w(bx), "zs": z.reshape(N, 128, T).astype(np.float32).astype(BF), "lim": w(lim)}
def setup_inputs(rng):
    return pack(*parts(rng))
def setup_inputs_spread(rng):
    x, sb, pe, he, bx, z, lim = parts(rng)
    sb = rows_of(rng, rng.random((N, 8, B, 16)) ** rng.choice(np.array([1.0, 2.0, 4.0]), (N, 8, 1, 1))); he = homes(rng, sb)
    x = (64 * rng.random(x.shape) * np.exp2(-rng.integers(0, 6, (N, 8, 1, V)))).astype(np.int64)
    z = (64 * rng.random(z.shape) * np.exp2(-rng.integers(0, 6, (N, 8, 1, T)))).astype(np.int64)
    bx = (B * rng.random((N, 8, T)) ** rng.choice(np.array([1.0, 2.0, 4.0]), (N, 8, 1))).astype(np.int64)
    lim = np.minimum((np.exp2(10 * rng.random((N, 8, 2)))).astype(np.int64), 1023); lim[:, 0, 0] = 0; lim[:, 1, 0] = 1023; lim[:, 2, 1] = 0; lim[:, 3, 1] = 1023
    return pack(x, sb, pe, he, bx, z, lim)
def setup_inputs_ends(rng):
    base = np.concatenate([np.arange(8), np.arange(V - 8, V)])
    sb = rng.permuted(np.broadcast_to(base, (N, 8, B, 16)).copy(), axis=-1)
    pe = (B - 1) * rng.integers(0, 2, (N, 8, V)); he = (B - 1) * rng.integers(0, 2, (N, 8, V)); bx = (B - 1) * rng.integers(0, 2, (N, 8, T))
    m = rng.integers(0, 3, (N, 8, 1, V)); x = 63 * np.where(m == 2, rng.integers(0, 2, (N, 8, 16, V)), m)
    m = rng.integers(0, 3, (N, 8, 1, T)); z = 63 * np.where(m == 2, rng.integers(0, 2, (N, 8, 16, T)), m)
    x[:, 2][:, :, base] = 63; z[:, 2] = 63
    for g in (3, 7):
        x[:, g][:, :, base] = 0; z[:, g] = 63
    for g in (1, 5):
        x[:, g][:, :, base] = 63; x[:, g][:, :, V - 1] = 0; z[:, g] = 0; he[:, g][:, base] = B - 1
    he[:, 7][:, base] = B - 1
    for g in (4, 7):
        bx[:, g] = 0; bx[:, g, T - 1] = B - 1
    h = (np.arange(8)[None, :] + N - 1 - np.arange(N)[:, None]) & 7
    lim = 1023 * np.stack([h & 1, (h >> 1) & 1], axis=-1)
    return pack(x, sb, pe, he, bx, z, lim)
def setup_inputs_corners(rng):
    x, sb, pe, he, bx, z, lim = parts(rng)
    for r in range(N):
        for g in range(8):
            k = g & 3
            if k == 0:
                m = int(rng.integers(100, 400)); extra = (rng.random(V) < 0.85).astype(np.int64)
                x[r, g] = (m >> 4) + (np.argsort(rng.random((16, V)), axis=0) < (m & 15) + extra[None, :])
                z[r, g] = 0; lim[r, g] = (1000, m)
            elif k == 1:
                i, j = rng.permutation(16)[:2]; x[r, g] = 20; x[r, g, i] += rng.integers(0, 16, V); x[r, g, j] += rng.integers(0, 16, V)
                z[r, g] = 20; lim[r, g] = (int(rng.integers(4, 9)), 1023)
            elif k == 2:
                sec = np.concatenate([np.array([0, V - 1]), 1 + rng.permutation(V - 2)[:14]])
                sb[r, g] = rng.permuted(np.tile(sec, (B, 1)), axis=-1)
                for j in range(8):
                    sb[r, g, B - 1 - j] = np.concatenate([sec[2 * j:2 * j + 2], rng.permutation(np.delete(sec, [2 * j, 2 * j + 1]))])
                he[r, g, sec] = B - 1 - (np.arange(16) >> 1)
                if r % 2 == 0: he[r, g, sec[2:]] = np.arange(14)
                x[r, g][:, sec] = 31; bx[r, g] = rng.integers(0, B, T); o = rng.permutation(T)[:32]; bx[r, g, o] = B - 1 - (np.arange(32) & 7)
                lim[r, g] = (1023, 1023)
            else:
                pe[r, g] = np.where(rng.random(V) < 0.5, he[r, g], pe[r, g])
                x[r, g] = 63 * rng.integers(0, 2, (1, V)); z[r, g] = 63 * rng.integers(0, 2, (1, T))
                bx[r, g] = rng.choice(np.array([0, 1, B - 2, B - 1]), T)
                lim[r, g] = (int(rng.choice(np.array([1, 8, 1023]))), int(rng.choice(np.array([0, 1007, 1008, 1023]))))
    return pack(x, sb, pe, he, bx, z, lim)
def setup_inputs_crowd(rng):
    x, sb, pe, he, bx, z, lim = parts(rng)
    at = (0, B - 1, B >> 1, B - 1, 5, B - 2, 1, B - 1)
    for r in range(N):
        for g in range(8):
            a = at[g]; bx[r, g] = a
            if g != 6: z[r, g] = z[r, g, :, :1]
            if g == 2: bx[r, g, 0] = 0
            if g == 3: bx[r, g, T - 1] = 3
            if g in (4, 5):
                sb[r, g, a - 1] = rng.permutation(sb[r, g, a])
                if g == 4: bx[r, g, rng.permutation(T)[:T >> 1]] = a - 1
                else: bx[r, g, int(rng.integers(0, T))] = a - 1
            if g == 6: bx[r, g] = rng.integers(0, 4, T)
            if g == 7:
                x[r, g][:, sb[r, g, a]] = x[r, g][:, sb[r, g, a, :1]] & 3; z[r, g] = z[r, g] & 3
                far = rng.permutation(sb[r, g, a])[2 * S - 2:]; x[r, g][:, far] = rng.integers(40, 64, (16, far.size))
                pe[r, g, sb[r, g, a]] = a
            he[r, g, sb[r, g, a]] = a; lim[r, g, 0] = (300, 500, 700, 1000)[g & 3]
            if g != 0: lim[r, g, 1] = int(rng.integers(250, 500))
    return pack(x, sb, pe, he, bx, z, lim)
def setup_inputs_busy(rng):
    x, sb, pe, he, bx, z, lim = parts(rng); K = V >> 4; z = 0 * z + 8
    for g in range(8):
        H = rng.permutation(B)[:K]
        for r in range(N):
            o = rng.permutation(V); own = o.reshape(K, 16); he[r, g, o] = np.repeat(H, 16)
            nx = np.arange(K); nx[0:8:2] += 1; nx[1:8:2] -= 1
            if g & 1:
                src = np.concatenate([np.arange(1, 8, 2), np.arange(8, K)]); nx[src] = rng.permutation(nx[src])
            pe[r, g, o] = np.repeat(H[nx], 16)
            sb[r, g, H] = own; sb[r, g, H[1:8:2], 0] = own[0:8:2, 1]
            far = (np.arange(K) >= 16) & (rng.random(K) < 0.25)
            w = np.where(far, rng.integers(14, 51, K), 0); c = np.where(far, 3, rng.integers(0, 7, K)); c[:16] = 0
            x[r, g][:, o] = 8 + np.repeat(w, 16) * rng.integers(0, 2, (16, V)) + (rng.random((16, V)) * (np.repeat(c, 16) + 1)).astype(np.int64)
            first = np.arange(1, K)
            if S & 1: first = np.delete(first, 7)
            mid = np.concatenate([first, np.arange(16, K)])[:T - 2]
            bx[r, g] = H[np.concatenate([np.array([0]), rng.permutation(mid), np.array([8 if S & 1 else 0])])]
            lim[r, g] = (int(rng.integers(97, 130)), 300 if g == 5 else 1023)
    H = rng.permutation(B)[:K]
    for r in range(N):
        o = rng.permutation(V); own = o.reshape(K, 16); sb[r, 6, H] = own
        ex = np.concatenate([31 + rng.permutation(31), rng.permutation(31), np.arange(62, K)])
        ho = np.concatenate([np.arange(62), np.roll(np.arange(62, K), 1)])
        pe[r, 6, o] = np.repeat(H[ex], 16); he[r, 6, o] = np.repeat(H[ho], 16)
        x[r, 6] = rng.integers(0, 64, (16, V))
        x[r, 6][:, own[:31].reshape(-1)] = rng.integers(8, 10, (16, 31 * 16))
        x[r, 6][:, own[31:62].reshape(-1)] = rng.integers(40, 64, (16, 31 * 16))
        two = np.argsort(rng.random((31, 16)), axis=1)[:, :2]; b = 31 + np.arange(31)
        m = int(lim[r, 6, 0]) + 240 + rng.permutation(31) - 8
        x[r, 6][:, own[b, two[:, 0]]] = 8
        x[r, 6][:, own[b, two[:, 1]]] = 8 + (m >> 4) + (np.argsort(rng.random((16, 31)), axis=0) < (m & 15))
        i = rng.permutation(T); bx[r, 6, i[:31]] = H[:31]; bx[r, 6, i[31:]] = H[rng.integers(62, K, T - 31)]
        z[r, 6] = rng.integers(0, 64, (16, T)); z[r, 6][:, i[:31]] = 8
    return pack(x, sb, pe, he, bx, z, lim)
def check_inputs(d):
    bad = []
    for k, lo, hi in (("xs", 0, 63), ("sb", 0, V - 1), ("pe", 0, B - 1), ("he", 0, B - 1), ("bx", 0, B - 1), ("zs", 0, 63), ("lim", 0, 1023)):
        v = np.asarray(d[k]).astype(np.float64)
        if not (np.min(v) >= lo and np.max(v) <= hi): bad.append("range of " + k)
        elif np.any(v != np.floor(v)): bad.append("whole numbers in " + k)
    w = np.sort(np.stack([gentries(a) for a in np.asarray(d["sb"])]).reshape(N, 8, B, 16), axis=-1)
    if np.any(w[..., 1:] == w[..., :-1]): bad.append("16 different entries of every box in sb")
    return bad
def reference(xs, sb, pe, he, bx, zs, lim):
    X = np.zeros((N, 8, 16, M), np.int64); X[..., :V] = xs.astype(np.float32).astype(np.int64).reshape(N, 8, 16, V)
    rows = np.stack([gentries(a) for a in sb]).astype(np.int64).reshape(N, 8, B, 16)
    P = np.zeros((N, 8, M), np.int64); Q = np.zeros((N, 8, M), np.int64); P[..., :V] = pe; Q[..., :V] = he
    J = np.zeros((N, 8, V), np.int64) + np.arange(V); till = np.full((N, 8, M), -1, np.int64)
    b = bx.astype(np.int64); z = zs.astype(np.float32).astype(np.int64).reshape(N, 8, 16, T); back = np.zeros((N, 8, T), np.int64)
    L = lim.astype(np.int64); A = np.zeros((N, 8), np.int64); BIG = 2 ** 20
    for t in range(S):
        for q in range(N):
            o = (q - t) % N
            for g in range(8):
                act = np.flatnonzero(back[o, g] <= t)
                if act.size == 0: continue
                x = X[q, g]; a = b[o, g, act]; zz = z[o, g][:, act]
                s = rows[q, g][a]; c = J[q, g][s]
                void = (c >= V) & (Q[q, g][s] == a[:, None]); held = till[q, g][c] >= t; free = ~void & ~held
                D = np.add.reduce(np.abs(x[:, c] - zz[:, :, None]), axis=0)
                key = np.where(free, D * 16 + np.arange(16), BIG); two = np.argsort(key, axis=1, kind="stable")[:, :2]
                kk = np.take_along_axis(key, two, 1); ef = np.take_along_axis(c, two, 1); e = ef[:, 0]; f = ef[:, 1]
                some = kk[:, 0] < BIG; pair = kk[:, 1] < BIG; xe = x[:, e]; xf = x[:, f]
                claim = np.flatnonzero(some); tk = claim[np.unique(e[claim], return_index=True)[1]]
                wait = some.copy(); wait[tk] = False
                ms = np.unique(a, return_index=True)[1]
                split = ~some | ((kk[:, 0] >> 4) > L[q, g, 1])
                apart = np.add.reduce(np.abs(xe - xf), axis=0)
                join = pair & ~split & (e < V) & (f < V) & (Q[q, g][e] == a) & (Q[q, g][f] == a) & (apart < L[q, g, 0] + 8 * (A[q, g] & 31))
                sp = ms[split[ms]]; jo = ms[join[ms]]; et = e[tk]; i = act[tk]
                b[o, g, i] = np.where(a[tk] == P[q, g][et], Q[q, g][et], P[q, g][et])
                stay = np.where(et >= V, LH, 1); till[q, g, et] = t + stay; back[o, g, i] = t + stay + 1
                back_s = s[sp][void[sp] & ~held[sp]]; J[q, g, back_s] = back_s
                n = V + T * t + act[jo]; J[q, g, e[jo]] = n; J[q, g, f[jo]] = n
                P[q, g, n] = P[q, g][e[jo]]; Q[q, g, n] = P[q, g][f[jo]]; A[q, g] += jo.size
                x[:, n] = np.maximum(xe, xf)[:, jo]; x[:, et] = zz[:, tk]
                z[o, g][:, i] = (zz[:, tk] + xe[:, tk]) >> 1
                z[o, g][:, act[wait]] = np.abs(zz - xe)[:, wait]
    return {"yj": J.astype(np.float32), "yx": X.reshape(N, 128, M).astype(np.float32).astype(BF), "yb": b.astype(np.float32), "yz": z.reshape(N, 128, T).astype(np.float32).astype(BF)}

@@ -1,0 +1,685 @@
+import numpy as np
+from concourse.mybir import AluOpType as Op, ActivationFunctionType as Fn
+
+NV, NB, NT, NS = 2048, 256, 192, 7
+MW = 216
+F32, BF, I32, U16 = "float32", "bfloat16", "int32", "uint16"
+_S = {
+    "X": (192 + 3392, BF), "JF": (6144, BF), "EN": (3392, BF), "CH": (448, F32), "CHH": (256, BF), "CHL": (256, BF),
+    "SBI": (256, I32), "SBF": (256, F32), "SBU": (256, U16), "SB2": (512, F32), "HS2": (512, F32), "TH2": (512, BF),
+    "HSK": (256, F32), "HT": (2048, BF), "SIO": (2048, F32), "GH": (4096, BF), "HEL": (128, U16), "HL": (128, U16),
+    "OH": (2048, BF), "SBH": (256, BF), "SBL": (256, BF),
+    "IN": (8 * MW, BF), "OUT": (7 * MW, BF), "LX": (7 * 36, U16),
+    "G": (3264, BF), "D": (3264, BF), "AB": (3072, BF), "EQ": (2304, BF), "ES": (2304, BF),
+    "PI": (2, I32), "PJ": (2, I32), "COL": (24, F32), "IM": (144, F32), "IMP": (128, F32), "IG": (128, F32),
+    "BD": (128, BF), "BDF": (128, F32), "ID": (128, BF), "IDF": (128, F32), "IDS": (10 * 128, BF),
+    "ZR": (512, BF), "ONE": (512, BF), "BB": (144, BF), "BND": (10 * 144, BF), "LO": (128, BF), "LC": (128, BF), "LJ": (128, BF),
+    "U": (2048, BF), "DG": (2048, BF), "BD3": (128, BF), "ON0": (384, BF),
+    "R16": (16, F32), "WD": (16, F32), "I16": (16, F32), "SW": (512, BF), "DUP": (256, F32), "CB": (12, BF),
+    "RO": (12, U16), "RO2": (12, U16), "KC": (192, F32), "KC2": (192, F32), "RS": (193, F32), "NI": (192, BF), "II": (60, F32),
+    "OWN": (512, F32), "T1": (48, F32), "T2": (12, I32), "T3": (12, F32), "PEI": (128, I32), "HEI": (128, I32),
+    "PEB": (128, BF), "HEB": (128, BF), "HIC": (128, BF), "LOC": (128, BF), "BXI": (192, I32), "BXB": (192, BF),
+    "LMI": (2, I32), "LMF": (2, F32), "LIM": (8, F32), "AI": (2, I32),
+    "LM": (12, U16), "HK": (192, F32), "TK": (192, BF), "HR": (192, F32), "TR": (192, BF), "TT": (192, BF),
+    "L1": (192, U16), "CL": (192, U16), "PEN": (192, BF), "KS": (192, F32), "KR": (192, F32),
+    "TM": (192, F32), "A32": (48, I32), "MK": (384, BF), "U1": (192, F32), "Q1": (192, F32),
+    "YJ": (128, F32), "YB": (192, F32), "GE": (384, BF), "DU": (192, BF), "AH": (24, I32), "NS": (192, F32),
+    "AF": (192, BF), "EF": (192, U16), "QI": (24, I32),
+    "NF": (192, BF), "CO": (24, U16), "DE": (384, BF), "EL": (24, U16), "BL": (24, U16), "NE": (384, BF), "SM": (320, F32),
+    "SB": (64, BF), "WH": (576, BF), "FL": (576, BF), "UU": (192, BF), "OD": (192, F32), "SN": (192, F32), "ZM": (192, BF),
+    "SK": (192, F32),
+}
+TWICE = ("NF", "CO", "DE", "EL", "BL", "NE", "SM", "SB", "WH", "FL", "UU", "OD", "SN", "ZM", "SK")
+SCRATCH = {k: ("sbuf", [128, w * (2 if k in TWICE else 1)], d) for k, (w, d) in _S.items()}
+for _b in range(8):
+    SCRATCH["b%d" % _b] = ("psum", [128, 512], F32)
+SEMAPHORES = ["cv", "cs", "ct", "cg", "snt"] + ["arr%d" % i for i in range(NS)] + ["d%d" % i for i in range(40)]
+CHAINED = ("b1", "b2", "b3", "b5")
+
+P22, P23, P24 = float(2 ** 22), float(2 ** 23), float(2 ** 24)
+SOME = 1009.0 * 8192
+IDS = {"NID": -1.0, "ID2": 2.0, "IDH": 0.5, "IDP": P24, "IDT": -1.0 / 2048, "E01": -144.0, "I13": 8192.0, "I14": 16384.0,
+       "NI14": -16384.0, "NIK": -1024.0}
+BANDS = ("B0", "B1", "B2", "B03", "BAL", "BK", "BN", "BPQ", "BC", "BE")
+CY, GA, SCA, PE, LAT, DMA, REM = 1.04, 1.56, 3.8, 0.53, 90.0, 2300.0, 2500.0
+LOOKS = ((0, 2, 2), (2, 6, 2), (6, 11, 6), (11, 16, 11))
+LOOK0 = ((0, 4, 0), (4, 8, 4), (8, 12, 8), (12, 16, 12))
+ABS = (0, 3, 5, 8, 11, 13, 15, 16)
+KEYS = ((0, 5), (5, 11), (11, 16))
+HTS, GHV, DEV, LOV = 4, 3, 2, 1
+TURNS, SIG, SEED = 2200, 1500.0, 1
+PLAN = []
+
+
+def rank_program(g, core, T, topo):
+    rank = T.rank_of(core)
+    if rank is None:
+        return
+    N = len(T.cores)
+    Q = {"v": g.vector, "s": g.scalar, "t": g.tensor, "g": g, "y": g.sync}
+    own = {"v": "cv", "s": "cs", "t": "ct", "g": "cg"}
+    ops = []
+    nd = [0]
+    par = [0]
+    kind = [0]
+
+    def a(name, lo=0, hi=None, st=1, p=None):
+        if name in IDS:
+            j = list(IDS).index(name)
+            return a("IDS", 128 * j, 128 * j + 128)
+        if name in BANDS:
+            j = BANDS.index(name)
+            return a("BND", 144 * j + lo, 144 * j + (144 if hi is None else hi))
+        w = _S[name][0] if name in _S else 512
+        if hi is None:
+            hi = w
+        if name in TWICE:
+            lo, hi = lo + w * par[0], hi + w * par[0]
+        ps = slice(None) if p is None else p
+        ap = T[name][ps, lo:hi] if st == 1 else T[name][ps, lo:hi:st]
+        reg = (name, 0, 512, None) if name in CHAINED else (name, lo, hi, None if p is None else p.start)
+        return (ap, [reg], [], (hi - lo + st - 1) // st)
+
+    def ind(win, off):
+        return (win[0].indirect(off[0]), win[1], off[1], 16 * off[3])
+
+    def val(x):
+        return x[0] if isinstance(x, tuple) else x
+
+    def psum(x):
+        return x[1][0][0][0] == "b"
+
+    def two(x):
+        return not psum(x) and _S[x[1][0][0]][1] in (BF, U16)
+
+    def put(e, reads, writes, call, cost, sem=None, n=1, cont=False, lat=0.0):
+        rs, ws = [], []
+        for x in reads:
+            if isinstance(x, tuple):
+                rs += x[1] + x[2]
+        for x in writes:
+            ws += x[1]
+            rs += x[2]
+        ops.append({"e": e, "r": rs, "w": ws, "call": call, "c": cost, "sem": sem or own[e], "n": n, "cont": cont, "lat": lat, "k": kind[0]})
+        kind[0] += 1
+
+    def vcost(out, x, per):
+        if out[2]:
+            return 50 + out[3] * SCA * CY
+        if x[2]:
+            return 60 + out[3] * GA * CY
+        return max(64, out[3] * per) * CY
+
+    def cp(out, x):
+        put("v", [x], [out], lambda: g.vector.tensor_copy(out[0], x[0]), vcost(out, x, 0.5 if two(out) and two(x) else 1))
+
+    def tt(out, x, y, o):
+        put("v", [x, y], [out], lambda: g.vector.tensor_tensor(out[0], x[0], y[0], o), vcost(out, x, 1 if psum(x) or psum(y) else 2))
+
+    def ts(out, x, s1, o1, s2=None, o2=None):
+        c = vcost(out, x, 0.5 if two(out) and two(x) else 1)
+        if o2 is None:
+            put("v", [x, s1], [out], lambda: g.vector.tensor_scalar(out[0], x[0], val(s1), None, o1), c)
+        else:
+            put("v", [x, s1, s2], [out], lambda: g.vector.tensor_scalar(out[0], x[0], val(s1), val(s2), o1, o2), c)
+
+    def ms(out, c):
+        put("v", [], [out], lambda: g.vector.memset(out[0], c), vcost(out, out, 0.5 if two(out) else 1))
+
+    def tr(out, x):
+        put("v", [x], [out], lambda: g.vector.transpose(out[0], x[0]), vcost(out, x, 0.5 if two(out) else 1))
+
+    def scan(out, d0, d1):
+        put("v", [d0, d1], [out], lambda: g.vector.tensor_tensor_scan(out[0], d0[0], d1[0], 0.0, Op.add, Op.min), vcost(out, d1, 1))
+
+    def act(out, x, f=Fn.Identity, bias=0.0, scale=1.0, acc=None):
+        if acc is None:
+            put("s", [x, bias, scale], [out], lambda: g.scalar.activation(out[0], x[0], f, bias=val(bias), scale=val(scale)), vcost(out, x, 1))
+        else:
+            put("s", [x], [out, acc], lambda: g.scalar.activation(out[0], x[0], f, accum_out=acc[0]), vcost(out, x, 1))
+
+    def iota(out, pat, base=0, ch=0):
+        if _S[out[1][0][0]][1] == I32:
+            put("g", [], [out], lambda: g.iota(out[0], pat, base, ch), 130 + 2 * CY * out[3])
+        else:
+            put("g", [], [out], lambda: g.iota(out[0], pat, base, ch, allow_small_or_imprecise_dtypes=True), 130 + 2 * CY * out[3])
+
+    def mm(items, start=True, stop=True):
+        def call():
+            for i, it in enumerate(items):
+                ins = g.tensor.matmul(it[0][0], it[1][0], it[2][0], start and i == 0, stop and i == len(items) - 1)
+            return ins
+        c = sum(max(64, it[2][3]) * PE * (1 if two(it[1]) else 4) for it in items)
+        put("t", [x for it in items for x in it[1:]], [it[0] for it in items], call, c, cont=not start, lat=70.0)
+
+    def dma(e, out, x, sem=None, extra=0.0):
+        if sem is None:
+            sem = "d%d" % nd[0]
+            nd[0] += 1
+        put(e, [x], [out], lambda: Q[e].dma_start(out[0], x[0]), 60.0, sem, 16, lat=DMA + extra)
+
+    def hbm(ap):
+        return (ap, [], [], 0)
+
+    def row(j):
+        return slice(j, 128, 16)
+
+    def band(name, r):
+        return a(name, 15 - r, 143 - r)
+
+    def zero(bank, lo, n):
+        return (a(bank, lo, lo + n), a("ZR", 0, 128), a("ZR", 0, n))
+
+    def pick(bank, lo, bnd, src, slo, n):
+        return [(a(bank, lo, lo + n), band(bnd, r), a(src, slo + r, slo + 16 * n, 16)) for r in range(16)]
+
+    def spread(bank, lo, src, slo, n):
+        return [(a(bank, lo + r, lo + 16 * n, 16), a("U", 128 * r, 128 * r + 128), a(src, slo, slo + n)) for r in range(16)]
+
+    def lowest(eq, src, sc, cl):
+        for c in range(12):
+            ts(a(eq, 208 * c, 192 * c + 192), a(src, 16 * c, 192), a(sc, cl + c, cl + c + 1), Op.is_equal)
+            kind[0] -= 1
+        kind[0] += 1
+
+        def off(cs):
+            return [(a("b5", 16 * c + 16, 192), a("BD"), a(eq, 208 * c + 16, 192 * c + 192)) for c in cs]
+        mm([zero("b5", 0, 192)] + off(range(6)), True, False)
+        mm(off(range(6, 11)), False, False)
+        mm([(a("b5", r, 192, 16), a("DG", 128 * r, 128 * r + 128), a(eq, r, 208 * 11 + r + 1, 208)) for r in range(16)], False, True)
+
+    def fill(out, c):
+        act(out, a("ZR", 0, out[3]), bias=c)
+
+    def msum(out, terms):
+        mm([(a("b7", 0, 128), a(w), x) for (w, x) in terms])
+        act(out, a("b7", 0, 128))
+
+    def col(j):
+        return a("COL", j, j + 1)
+
+    ms(a("BXI"), 0)
+    ms(a("LMI"), 0)
+    dma("y", a("SBI"), hbm(T.sb[:]))
+    dma("s", a("HEI"), hbm(T.he[:]))
+    dma("y", a("BXI", p=row(0)), hbm(T.bx[:]))
+    dma("s", a("PEI"), hbm(T.pe[:]))
+    dma("y", a("LMI", p=row(0)), hbm(T.lim[:]))
+    dma("y", a("IN", 0, 192), hbm(T.zs[:]))
+    dma("y", a("X", 192, 192 + NV), hbm(T.xs[:]), None, 2500.0)
+    for h in range(2):
+        dma("y", a("JF", 2048 * h, 2048 * h + 2048), a("X", 192, 192 + NV), None, 2500.0)
+
+    iota(a("PI", 0, 1), [[0, 1]], 0, 1)
+    iota(a("IM"), [[1, 144]])
+    iota(a("IG"), [[1, 8], [0, 16]])
+    iota(a("IMP"), [[1, 128]], 0, -1)
+    iota(a("KC"), [[16, 12], [192, 16]])
+    iota(a("II"), [[0, 5], [16, 12]])
+    iota(a("NI"), [[1, 192]])
+    iota(a("SIO"), [[1, 2048]])
+    iota(a("OWN"), [[0, 2], [1, 256]])
+    ms(a("ZR"), 0.0)
+    ms(a("JF", 4096, 6144), 0.0)
+    act(a("EN", 0, NV), a("JF", 4096, 6144))
+    ts(a("PJ", 0, 1), a("PI", 0, 1), 15, Op.bitwise_and)
+    ts(a("PJ", 1, 2), a("PI", 0, 1), 4, Op.logical_shift_right)
+    cp(a("COL", 0, 2), a("PJ"))
+    ts(a("PI", 1, 2), a("PJ", 1, 2), 1, Op.bitwise_and)
+    cp(col(3), a("PI", 1, 2))
+    ts(col(2), col(3), -1.0, Op.mult, 1.0, Op.add)
+    ts(col(4), col(1), 16.0, Op.mult, 15.0, Op.add)
+    ts(col(10), col(0), 128.0, Op.mult)
+    ts(a("HIC"), a("IG"), 0.0, Op.mult, col(10), Op.add)
+    cp(a("LOC"), a("IM", 0, 128))
+    dma("y", a("JF", 4096, 6144, p=row(0)), a("HIC"))
+    dma("y", a("JF", 4096, 6144, p=row(2)), a("LOC"))
+    ts(a("R16"), a("IM", 0, 16), col(0), Op.is_equal)
+    ts(col(11), a("R16", 1, 2), 1024.0, Op.mult, a("R16", 0, 1), Op.add)
+    ts(col(5), col(0), 3.5, Op.is_lt)
+    ts(col(6), col(0), 256.0, Op.mult)
+    fill(a("ON0", 0, 192), 1.0)
+    fill(a("ON0", 192, 384), 0.0)
+    ts(a("BD"), a("IG"), col(1), Op.is_equal)
+    act(a("BDF"), a("BD"))
+    ts(a("ID"), a("IMP"), 0.0, Op.is_equal)
+    act(a("IDF"), a("ID"))
+    ts(a("BB"), a("IM"), col(4), Op.is_equal)
+    for nm, w in (("B2", a("R16", 2, 3)), ("B0", a("R16", 0, 1)), ("B03", col(5)), ("B1", a("R16", 1, 2)), ("BAL", 8192.0),
+                  ("BK", col(6)), ("BN", -8192.0), ("BPQ", col(11))):
+        act(a(nm), a("BB"), scale=w)
+    for be in range(2):
+        for ga in range(2):
+            ts(a("SW", 256 * be + 128 * ga, 256 * be + 128 * ga + 128), a("IMP"), 16.0 * (ga - be), Op.is_equal, col(2 + be), Op.mult)
+        msum(a("DUP", 128 * be, 128 * be + 128), [("ID", a("SW", 256 * be + 128 * ga, 256 * be + 128 * ga + 128)) for ga in range(2)])
+    for r in range(16):
+        ts(a("U", 128 * r, 128 * r + 128), a("BD"), a("R16", r, r + 1), Op.mult)
+        kind[0] -= 1
+    kind[0] += 1
+    ms(a("CB", 0, 12, 2), 0.0)
+    ms(a("CB", 1, 12, 2), 256.0)
+    cp(a("SBF"), a("SBI"))
+    cp(a("HEB"), a("HEI"))
+    cp(a("PEB"), a("PEI"))
+    dma("y", a("EN", 0, NV, p=row(1)), a("HEB"))
+    dma("y", a("EN", 0, NV, p=row(0)), a("PEB"))
+    mm([(a("b1", 0, 256), a("DUP", 0, 128), a("SBF"))])
+    mm([(a("b1", 256, 512), a("DUP", 128, 256), a("SBF"))])
+    act(a("SB2"), a("b1"))
+    cp(a("BXB"), a("BXI"))
+    mm(pick("b6", 0, "B0", "BXB", 0, 12))
+    ts(a("II"), a("II"), col(0), Op.add)
+    ts(a("II", 36, 48), a("II", 36, 48), 256.0, Op.add)
+    ts(a("II", 48, 60), a("II", 48, 60), 3072.0, Op.add)
+    ts(a("T1", 0, 12), a("II", 0, 12), -5.5, Op.add, 1.0 / 12, Op.mult)
+    cp(a("T2"), a("T1", 0, 12))
+    ts(a("T3"), a("T2"), -191.0, Op.mult)
+    ts(a("T1", 16, 28), a("II", 0, 12), 16.0, Op.mult)
+    tt(a("T1", 32, 44), a("T1", 16, 28), a("T3"), Op.add)
+    cp(a("RO"), a("T1", 32, 44))
+    ts(col(9), col(0), 12.0, Op.mult)
+    ts(a("RO2"), a("IM", 0, 12), col(9), Op.add)
+    cp(a("IN", 192, 204), a("b6", 0, 12))
+    ms(a("IN", 204, 216), 0.0)
+    ts(a("WD"), a("IM", 0, 16), col(0), Op.is_gt)
+    ts(a("I16"), a("R16"), -256.0, Op.mult)
+    tt(a("WD"), a("WD"), a("I16"), Op.add)
+    for r in range(16):
+        ts(a("DG", 128 * r, 128 * r + 128), a("BD"), a("WD", r, r + 1), Op.mult)
+        kind[0] -= 1
+    kind[0] += 1
+    for nm, w in IDS.items():
+        act(a(nm), a("ID"), scale=w)
+    act(a("BD3"), a("BD"), scale=col(5))
+    ts(col(7), col(0), 2.0, Op.mult)
+    act(a("KC"), a("KC"), bias=col(7), scale=2.0)
+    act(a("KC2"), a("KC"), bias=2.0)
+    fill(a("RS"), 0.0)
+    ms(a("RS", 1, 193, 16), float(2 ** 27))
+    ms(a("TM", 0, 1), 0.0)
+    fill(a("G", 3072, 3264), 0.0)
+    fill(a("CH"), 0.0)
+    fill(a("ONE"), 1.0)
+    cp(a("LMF"), a("LMI"))
+    mm([(a("b6", 16, 18), a("BDF"), a("LMF"))])
+    ts(a("LIM", 0, 1), a("b6", 16, 17), -P22, Op.add)
+    cp(a("LIM", 1, 2), a("LIM", 0, 1))
+    ts(a("LIM", 2, 3), a("b6", 17, 18), 1.0, Op.add, 1009.0, Op.min)
+    ts(a("LIM", 2, 3), a("LIM", 2, 3), 8192.0, Op.mult)
+    ms(a("LIM", 3, 4), 0.0)
+    act(a("SBH"), a("SBF"))
+    dma("y", a("JF", 0, 4096, p=row(2)), a("SBH"))
+    mm([(a("b7", 0, 256), a("IDF"), a("SBF")), (a("b7", 0, 256), a("NID"), a("SBH"))])
+    act(a("SBL"), a("b7", 0, 256))
+    dma("y", a("JF", 0, 4096, p=row(3)), a("SBL"))
+    mm(pick("b6", 128, "B1", "EN", 0, 128))
+    act(a("BC"), a("B0"), scale=4096.0)
+    act(a("BE"), a("B0"), scale=-8192.0)
+    msum(a("LO"), [("ID", band("BN", 0)), ("ID", band("BN", 1)), ("ID", band("BK", 2)), ("NID", band("BN", 3))])
+    msum(a("LC"), [("ID", band("BC", 0)), ("ID", band("BE", 3))])
+    msum(a("LJ"), [("ID", band("B0", 0)), ("ID", band("B2", 1))])
+    cp(a("SBU"), a("SBI"))
+    cp(a("HEL"), a("b6", 128, 256))
+    for h in range(4):
+        bk = ("b1", "b7")[h % 2]
+        tt(a("OH", 512 * h, 512 * h + 512), ind(a("SBF"), a("HEL", 32 * h, 32 * h + 32)), a("SIO", 512 * h, 512 * h + 512), Op.is_equal)
+        mm([(a(bk), a("LC"), a("ONE")), (a(bk), band("B1", 3), a("EN", 512 * h, 512 * h + 512)),
+            (a(bk), a("LJ"), a("JF", 4096 + 512 * h, 4608 + 512 * h)), (a(bk), a("LO"), a("OH", 512 * h, 512 * h + 512))])
+        if h < HTS:
+            act(a("HT", 512 * h, 512 * h + 512), a(bk), Fn.Relu)
+        else:
+            ts(a("HT", 512 * h, 512 * h + 512), a(bk), 0.0, Op.max)
+    for h in range(8):
+        (cp if h < GHV else act)(a("GH", 512 * h, 512 * h + 512), ind(a("HT"), a("SBU", 32 * h, 32 * h + 32)))
+
+    def unmark(t, part):
+        cp(ind(a("X", 0, 192 + NV + NT * (t + 1)), a("LX", 36 * t + 12 * part, 36 * t + 12 * part + 12)), a("IN", MW * t, MW * t + 192))
+
+    first = 0
+    for t in range(NS):
+        par[0] = t % 2
+        if t == 1:
+            first = kind[0]
+        if t > 1:
+            kind[0] = first
+        last = t == NS - 1
+        z = a("IN", MW * t, MW * t + 192)
+        ao = MW * t + 192
+        box = a("IN", ao, ao + 12)
+        back = a("IN", ao + 12, ao + 24)
+        wide = NV + NT * t
+        it = [(a("b0", 0, 12), a("ID"), a("CB"))]
+        for be in range(2):
+            for ga in range(2):
+                it.append((a("b0", be, 12, 2), a("SW", 256 * be + 128 * ga, 256 * be + 128 * ga + 128), a("IN", ao + ga, ao + 12, 2)))
+        mm(it)
+        cp(a("LM"), a("b0", 0, 12))
+        cp(a("HK"), ind(a("HS2" if t else "SB2"), a("LM")))
+        tr(a("HR"), a("HK"))
+        cp(a("L1"), ind(a("HR"), a("RO")))
+        if t:
+            act(a("TK"), ind(a("TH2"), a("LM")))
+            tr(a("TR"), a("TK"))
+            act(a("TT"), ind(a("TR"), a("RO")))
+        jw = a("JF") if t else a("JF", 4096, 6144)
+        banks = ["b0", "b1", "b6", "b7"]
+        for q, (k0, k1, kv) in enumerate(LOOKS if t else LOOK0):
+            if kv > k0:
+                cp(a("G", 192 * k0, 192 * kv), ind(jw, a("L1", 12 * k0, 12 * kv)))
+            if kv < k1:
+                act(a("G", 192 * kv, 192 * k1), ind(jw, a("L1", 12 * kv, 12 * k1)))
+            if t:
+                w = 12 * (k1 - k0)
+                mm(pick(banks[q], 0, "B03", "G", 192 * k0, w))
+                cp(a("CL", 12 * k0, 12 * k1), a(banks[q], 0, w))
+                tt(a("PEN", 12 * k0, 12 * k1), a(banks[q], 0, w), a("TT", 12 * k0, 12 * k1), Op.is_ge)
+        mm([zero("b4", 0, 192)] + spread("b4", 0, "IN", ao, 12))
+        ts(a("SM", 0, 12), back, t + 0.5, Op.is_gt, 8192.0, Op.mult)
+        tt(a("SB", 0, 12), box, a("SM", 0, 12), Op.add)
+        cp(a("BL", 0, 12), box)
+        act(a("AF"), a("b4", 0, 192))
+        lowest("ES", "AF", "SB", 0)
+        act(a("NF"), a("b5", 0, 192), bias=256.0 * P24 - P22, scale=P24)
+        mm(pick("b6", 84, "B0", "NF", 0, 12))
+        tt(a("SM", 24, 36), a("b6", 84, 96), box, Op.max)
+        tt(a("SM", 36, 48), a("SM", 24, 36), a("II", 36, 48), Op.min)
+        cp(a("BL", 12, 24), a("SM", 36, 48))
+        act(a("OD"), ind(a("CH", 0, 256), a("BL", 0, 12)))
+        act(a("SK"), ind(a("SBF"), a("BL", 0, 12)))
+        act(a("SN"), a("SK"), bias=float(wide), scale=-1.0)
+        mm([(a("b1", 256, 448), a("IDF"), a("SN")), (a("b1", 256, 448), a("ID"), a("NI"))])
+        act(a("NS"), a("b1", 256, 448))
+        act(a("D", 3072, 3264), z)
+        cl = "CL" if t else "L1"
+        mm([zero("b2", 0, 192)], True, False)
+        for k in range(16):
+            tt(a("D", 192 * k, 192 * k + 192), ind(a("X", 192, 192 + wide), a(cl, 12 * k, 12 * k + 12)), z, Op.subtract)
+            kind[0] -= 1
+        kind[0] += 1
+        if t:
+            mm([(a("b2", 0, 192), a("IDP"), a("PEN")), (a("b2", 0, 192), a("IDT"), a("TT"))], False, False)
+        for k0, k1 in zip(ABS, ABS[1:]):
+            act(a("AB", 192 * k0, 192 * k1), a("D", 192 * k0, 192 * k1), Fn.Abs)
+        for (k0, k1) in KEYS:
+            mm(pick("b2", 12 * k0, "BAL", "AB", 192 * k0, 12 * (k1 - k0)), False, k1 == 16)
+        for h in range(4):
+            mm([(a("b3", 0, 384), a("IDP"), a("ON0"))] * (h == 0)
+               + [(a("b3", 0, 192), band("BAL", k), a("AB", 192 * k, 192 * k + 192)) for k in range(4 * h, 4 * h + 4)], h == 0, False)
+        act(a("KS"), a("b2", 0, 192))
+        tt(a("KR"), ind(a("KS"), a("RO2")), a("KC2" if t else "KC"), Op.add)
+        m1, m2 = a("b2", 15, 192, 16), a("b2", 207, 384, 16)
+        scan(a("b2", 0, 192), a("RS", 1, 193), a("KR"))
+        cp(a("A32", 0, 12), m1)
+        ts(a("A32", 24, 36), a("A32", 0, 12), 1, Op.logical_shift_right, 4095, Op.bitwise_and)
+        ts(a("SM", 60, 72), m1, SOME, Op.is_ge, 8192.0, Op.mult)
+        tt(a("SM", 72, 84), a("SM", 60, 72), a("SM", 0, 12), Op.add)
+        tt(a("SM", 48, 60), a("SM", 72, 84), a("II", 48, 60), Op.min)
+        tt(a("SM", 12, 24), a("SM", 48, 60), a("A32", 24, 36), Op.max)
+        cp(a("CO", 0, 12), a("SM", 12, 24))
+        act(a("GE", 0, 192), ind(a("G"), a("CO", 0, 12)))
+        ts(a("SB", 24, 36), m1, a("LIM", 2, 3), Op.is_ge, -3 * P23, Op.mult)
+        ts(a("SM", 180, 192), m1, a("LIM", 2, 3), Op.is_ge, 4096.0, Op.mult)
+        tt(a("TM", 1, 192), a("b2", 0, 191), a("KR", 1, 192), Op.max)
+        scan(a("b2", 192, 384), a("RS", 0, 192), a("TM"))
+        cp(a("A32", 12, 24), m2)
+        ts(a("SM", 192, 204), m2, SOME, Op.is_ge, 4096.0, Op.mult)
+        ts(a("A32", 36, 48), a("A32", 12, 24), 1, Op.logical_shift_right, 4095, Op.bitwise_and)
+        cp(a("CO", 12, 24), a("A32", 36, 48))
+        mm(pick("b6", 480, "B03", "GE", 0, 12))
+        mm([(a("b4", 192, 384), a("BD3"), a("GE", 0, 192))])
+        act(a("GE", 192, 384), ind(a("G"), a("CO", 12, 24)))
+        mm(pick("b6", 492, "B03", "GE", 192, 12))
+        de, df = a("DE", 0, 192), a("DE", 192, 384)
+        (cp if DEV & 1 else act)(de, ind(a("D"), a("CO", 0, 12)))
+        (cp if DEV & 2 else act)(df, ind(a("D"), a("CO", 12, 24)))
+        mm([(a("b0", 0, 192), a("ID"), de), (a("b0", 0, 192), a("ID2"), z)])
+        mm([(a("b6", 96, 288), a("ID"), de), (a("b6", 96, 288), a("NID"), df)])
+        tt(a("SM", 84, 96), a("b6", 480, 492), a("SM", 72, 84), Op.add)
+        cp(a("EL", 0, 12), a("b6", 480, 492))
+        cp(a("EL", 12, 24), a("b6", 492, 504))
+        ts(a("SM", 96, 108), a("b6", 480, 492), 2047.5, Op.is_gt, 4096.0, Op.mult)
+        ts(a("SM", 120, 132), a("b6", 480, 492), 192.0, Op.add)
+        act(a("NE", 0, 192), ind(a("EN", 0, wide), a("EL", 0, 12)))
+        act(a("NE", 192, 384), ind(a("EN", 0, wide), a("EL", 12, 24)))
+        act(a("WH", 0, 192), de, Fn.Abs)
+        act(a("WH", 192, 384), a("b0", 0, 192), bias=143.75, scale=0.5)
+        act(a("WH", 384, 576), a("b6", 96, 288), Fn.Abs)
+        nq = 12 if t else 24
+        mm(pick("b7", 448, "BPQ", "NE", 0, nq)
+           + [(a("b7", 448 + 12 * j, 460 + 12 * j), a(w), box) for j in range(nq // 12) for w in ("NID", "NIK")])
+        ts(a("QI", 0, nq), a("b7", 448, 448 + nq), 1.0 / 1024, Op.mult)
+        ts(a("SM", 288, 300), a("QI", 0, 12), -1024.0, Op.mult)
+        tt(a("SM", 300, 312), a("b7", 448, 460), a("SM", 288, 300), Op.add)
+        mm([(a("b2", 192, 384), a("ID"), a("WH", 192, 384)), (a("b2", 192, 384), a("NID"), a("WH", 0, 192)),
+            (a("b2", 192, 384), a("E01"), a("ONE", 0, 192))])
+        mm([(a("b7", 64, 256), a("BD3"), a("GE", 192, 384))])
+        ts(a("SM", 132, 144), a("SM", 300, 312), 0.0, Op.is_equal)
+        tt(a("SM", 144, 156), a("QI", 0, 12), a("SM", 132, 144), Op.mult)
+        tt(a("SM", 156, 168), a("SM", 300, 312), a("SM", 144, 156), Op.add)
+        ts(a("SM", 108, 120), a("SM", 96, 108), 1.0 / 4096, Op.mult, t + 2.0, Op.add)
+        tt(a("SM", 168, 180), a("SM", 108, 120), back, Op.subtract)
+        cp(a("EF"), a("b4", 192, 384))
+        lowest("EQ", "EF", "SM", 84)
+        act(a("FL", 192, 384), a("b5", 0, 192), Fn.Relu, bias=-255.0, scale=-1.0)
+        mm(pick("b6", 72, "B0", "FL", 192, 12))
+        tt(a("UU"), a("b2", 192, 384), a("FL", 192, 384), Op.mult)
+        mm([(a("b0", 0, 192), a("ID"), a("WH", 0, 192)), (a("b0", 0, 192), a("ID"), a("UU"))])
+        act(a("OUT", MW * t, MW * t + 192), a("b0", 0, 192))
+        tk = a("b6", 72, 84)
+        tt(a("SM", 240, 252), tk, a("SM", 156, 168), Op.mult)
+        tt(a("SM", 252, 264), tk, a("SM", 168, 180), Op.mult)
+        tt(a("OUT", MW * t + 192, MW * t + 216), a("SM", 240, 264), a("IN", ao, ao + 24), Op.add)
+        dst = T.cores[(rank + 1) % N if not last else (rank - t) % N]
+        rid, pid = topo.addr(dst, core)
+        eng = topo.engines(core, dst)[:8]
+        src, land, arr = a("OUT", MW * t, MW * t + MW), a("IN", MW * (t + 1), MW * (t + 2)), "arr%d" % t
+        put("g", [src], [land], lambda src=src, land=land, arr=arr, pid=pid, rid=rid, eng=eng: g.remote_dma(
+            land[0], src[0], T.sem[arr], T.sem.snt, pid, rid, sum(1 << e for e in eng)), 500.0, arr, len(eng), lat=REM - 500)
+        tt(a("MK", 0, 192), a("b4", 192, 384), a("SK"), Op.is_equal)
+        tt(a("MK", 192, 384), a("b7", 64, 256), a("SK"), Op.is_equal)
+        if t:
+            ts(a("AH"), a("A32", 0, 24), 1, Op.bitwise_and)
+            ts(a("SM", 264, 288), a("AH"), 0.0, Op.is_equal, 4096.0, Op.mult)
+        else:
+            ts(a("SM", 264, 288), a("QI"), 0.0, Op.not_equal, 4096.0, Op.mult)
+        tt(a("SM", 180, 204), a("SM", 180, 204), a("SM", 264, 288), Op.add)
+        tt(a("SB", 36, 48), a("SM", 180, 192), a("SM", 192, 204), Op.add)
+        mm([(a("b3", 192, 384), a("ID"), a("NF"))], False, False)
+        mm([(a("b3", 192, 384), a("BD"), a("WH", 384, 576))], False, False)
+        mm(spread("b3", 0, "SB", 24, 24), False, True)
+        ts(a("FL", 384, 576), a("b3", 192, 384), a("LIM", 1, 2), Op.is_lt)
+        tt(a("U1"), a("b3", 0, 192), a("OD"), Op.min)
+        act(a("U1"), a("U1"), Fn.Relu)
+        mm([(a("b1", 0, 192), a("NI14"), a("ONE", 0, 192)), (a("b1", 0, 192), a("I13"), a("MK", 0, 192)),
+            (a("b1", 0, 192), a("I13"), a("MK", 192, 384))], True, False)
+        mm([(a("b1", 0, 192), a("I14"), a("FL", 384, 576))], False, True)
+        tt(a("Q1"), a("b1", 0, 192), a("NS"), Op.min)
+        tt(ind(a("CH"), a("BL", 12, 24)), a("U1"), a("Q1"), Op.max)
+        act(a("CHH"), a("CH", 0, 256))
+        dma("y", a("JF", 0, 4096, p=row(0)), a("CHH"), "d38")
+        if LOV:
+            tt(a("CHL"), a("CH", 0, 256), a("CHH"), Op.subtract)
+        else:
+            mm([(a("b3", 0, 256), a("IDF"), a("CH", 0, 256))], True, False)
+            mm([(a("b3", 0, 256), a("NID"), a("CHH"))], False, True)
+            act(a("CHL"), a("b3", 0, 256))
+        dma("y", a("JF", 0, 4096, p=row(1)), a("CHL"), "d39")
+        mm([(a("b4", 0, 192), a("ID"), z), (a("b4", 0, 192), a("IDH"), de), (a("b4", 0, 192), a("IDH"), df),
+            (a("b4", 0, 192), a("IDH"), a("WH", 384, 576))])
+        if not last:
+            mm([(a("b4", 192, 384), band("B0", 0), a("NE", 0, 192)), (a("b4", 192, 384), band("B0", 1), a("NE", 192, 384))])
+            act(a("EN", wide, wide + 192), a("b4", 192, 384))
+            act(a("ZM"), z, bias=128.0)
+            act(a("DU"), a("FL", 384, 576), acc=a("LIM", 4, 5))
+            act(a("LIM", 3, 4), a("LIM", 3, 4), bias=a("LIM", 4, 5))
+            cp(a("AI", 0, 1), a("LIM", 3, 4))
+            ts(a("AI", 1, 2), a("AI", 0, 1), 31, Op.bitwise_and)
+            ts(a("LIM", 1, 2), a("AI", 1, 2), 8.0, Op.mult, a("LIM", 0, 1), Op.add)
+        else:
+            kind[0] += 8
+        tt(a("X", 192 + wide, 192 + wide + 192), a("b4", 0, 192), a("FL", 384, 576), Op.mult)
+        tt(a("SM", 204, 216), tk, a("SM", 120, 132), Op.mult)
+        tt(a("SM", 228, 240), a("SM", 204, 216), a("SM", 96, 108), Op.min)
+        tt(a("SM", 216, 228), a("SM", 204, 216), a("SM", 228, 240), Op.subtract)
+        tt(a("SM", 204, 240), a("SM", 204, 240), a("II", 0, 36), Op.max)
+        cp(a("LX", 36 * t, 36 * t + 36), a("SM", 204, 240))
+        if t >= 1:
+            unmark(t - 1, 0 if last else 1)
+        if t >= 3:
+            unmark(t - 2, 2)
+        elif t:
+            kind[0] += 1
+        cp(ind(a("X", 0, 192 + wide), a("LX", 36 * t, 36 * t + 12)), z if last else a("ZM"))
+        if t == 0:
+            mm(pick("b7", 0, "B03", "GH", 0, 256))
+            act(a("HSK"), a("b7", 0, 256))
+            mm([(a("b1", 0, 256), a("DUP", 0, 128), a("HSK"))])
+            mm([(a("b1", 256, 512), a("DUP", 128, 256), a("HSK"))])
+            act(a("HS2"), a("b1"))
+            act(a("OWN"), a("OWN"), bias=col(6))
+            tt(a("TH2"), a("b1"), a("OWN"), Op.is_equal)
+            ts(a("TH2"), a("TH2"), -2048.0, Op.mult, 4096.0, Op.add)
+        if t == 1:
+            mm([(a("b7", 256, 384), band("B03", r), a("HT", 128 * r, 128 * r + 128)) for r in range(16)])
+            cp(a("HL"), a("b7", 256, 384))
+
+    kind[0] += 2
+    for h in range(4):
+        dma("y", hbm(T.yx[:, 848 * h:848 * h + 848]), a("X", 192 + 848 * h, 192 + 848 * h + 848), None, 3000.0)
+    act(a("G", 0, 1024), ind(a("JF"), a("HL", 0, 64)))
+    cp(a("G", 1024, 2048), ind(a("JF"), a("HL", 64, 128)))
+    fin = MW * NS
+    dma("y", hbm(T.yz[:]), a("IN", fin, fin + 192))
+    mm([zero("b4", 0, 192)] + spread("b4", 0, "IN", fin + 192, 12))
+    mm(pick("b1", 0, "B03", "G", 0, 128))
+    act(a("YB"), a("b4", 0, 192))
+    dma("s", hbm(T.yb[:]), a("YB", p=row(0)))
+    cp(a("YJ"), a("b1", 0, 128))
+    dma("y", hbm(T.yj[:]), a("YJ"))
+
+    def clash(r, s):
+        return r[1] < s[2] and s[1] < r[2] and (r[3] is None or s[3] is None or r[3] == s[3])
+
+    def covers(r, s):
+        return r[1] <= s[1] and s[2] <= r[2] and r[3] in (None, s[3])
+
+    seen = {}
+    for i, o in enumerate(ops):
+        dep = set()
+        for r in o["r"]:
+            dep.update(j for (s, w, j) in seen.get(r[0], []) if w and clash(r, s))
+        for r in o["w"]:
+            dep.update(j for (s, w, j) in seen.get(r[0], []) if clash(r, s))
+        o["dep"] = dep
+        for r in o["w"]:
+            seen[r[0]] = [x for x in seen.get(r[0], []) if not covers(r, x[0])] + [(r, True, i)]
+        for r in set(o["r"]):
+            seen.setdefault(r[0], []).append((r, False, i))
+        o["bk"] = sorted(set(r[0] for r in o["r"] + o["w"] if r[0][0] == "b"))
+    n = len(ops)
+    kids = [[] for o in ops]
+    for i, o in enumerate(ops):
+        for j in sorted(o["dep"]):
+            kids[j].append(i)
+    full = [o["c"] + o["lat"] for o in ops]
+    keys = [[(o["e"], 0.0)] + [(b, LAT + 70.0) for b in o["bk"]] for o in ops]
+    deps = [sorted(o["dep"]) for o in ops]
+
+    def ways(lean, kinds):
+        way = [0.0] * n
+        for i in range(n - 1, -1, -1):
+            way[i] = full[i] + lean[ops[i]["k"]] + max([way[k] + LAT for k in kids[i]], default=0.0)
+        return {i: way[i] + lean[kinds + ops[i]["k"]] for i in range(n)}
+
+    def lay(rev, prio):
+        pre, post = (kids, deps) if rev else (deps, kids)
+        left = [len(p) for p in pre]
+        at = [0.0] * n
+        st = [0.0] * n
+        busy = {}
+        cand = set(i for i in range(n) if left[i] == 0)
+        while cand:
+            i = max(cand, key=prio.get)
+            cand.remove(i)
+            o = ops[i]
+            s0, c, e = at[i] + (o["lat"] if rev else 0.0), o["c"], o["e"]
+            moved = True
+            while moved:
+                moved = False
+                for (key, pad) in keys[i]:
+                    lst = busy.setdefault(key, [])
+                    j = len(lst)
+                    while j and lst[j - 1][1] + pad > s0:
+                        j -= 1
+                    while j < len(lst) and lst[j][0] - pad < s0 + c:
+                        if (pad == 0.0 or lst[j][2] != e) and s0 < lst[j][1] + pad:
+                            s0 = lst[j][1] + pad
+                            moved = True
+                        j += 1
+            st[i] = s0
+            for (key, pad) in keys[i]:
+                lst = busy[key]
+                j = len(lst)
+                while j and lst[j - 1][0] > s0:
+                    j -= 1
+                lst.insert(j, (s0, s0 + c, e))
+            end = s0 + c + (0.0 if rev else o["lat"]) + LAT
+            for k in post[i]:
+                if at[k] < end:
+                    at[k] = end
+                left[k] -= 1
+                if left[k] == 0:
+                    cand.add(k)
+        return st, max(st[i] + ops[i]["c"] + (0.0 if rev else ops[i]["lat"]) for i in range(n))
+
+    if not PLAN:
+        rng = np.random.RandomState(SEED)
+        kinds = max(o["k"] for o in ops) + 1
+        lean = [0.0] * (2 * kinds)
+        best = None
+        for turn in range(TURNS):
+            tryl = list(lean)
+            if turn:
+                for k in rng.randint(0, 2 * kinds, 1 + turn % 6):
+                    tryl[int(k)] += float(rng.normal()) * SIG
+            st, span = lay(False, ways(tryl, kinds))
+            if best is None or span <= best[0]:
+                best, lean = (span, st), tryl
+        for turn in range(2):
+            sb, _ = lay(True, {i: best[1][i] + full[i] for i in range(n)})
+            st, span = lay(False, {i: sb[i] + ops[i]["c"] for i in range(n)})
+            if span < best[0]:
+                best = (span, st)
+        PLAN.append(sorted(range(n), key=lambda i: (best[1][i], i)))
+        PLAN.append(best[0])
+    clock = {k: {} for k in Q}
+    total = {}
+    tok = {}
+    user = {}
+    for i in PLAN[0]:
+        o = ops[i]
+        e = o["e"]
+        need = [j for j in deps[i] if not (o["cont"] and ops[j]["e"] == "t")]
+        need += [user[b] for b in o["bk"] if b in user and ops[user[b]]["e"] != e]
+        for j in sorted(need, key=lambda j: -tok[j][1]):
+            sem, m, c = tok[j]
+            if clock[e].get(sem, 0) < m:
+                Q[e].wait_ge(T.sem[sem], m)
+                for k, v in c.items():
+                    if clock[e].get(k, 0) < v:
+                        clock[e][k] = v
+        ins = o["call"]()
+        sem = o["sem"]
+        total[sem] = total.get(sem, 0) + o["n"]
+        if sem[:3] == "arr":
+            total["snt"] = total.get("snt", 0) + o["n"]
+            tok[i] = (sem, total[sem], {sem: total[sem]})
+        else:
+            ins.then_inc(T.sem[sem], o["n"])
+            c = dict(clock[e])
+            c[sem] = total[sem]
+            tok[i] = (sem, total[sem], c)
+        for b in o["bk"]:
+            user[b] = i
+    for s, m in total.items():
+        g.wait_ge(T.sem[s], m)

@@ -3,51 +3,52 @@ from concourse.mybir import AluOpType as Op, ActivationFunctionType as Fn
 
 NV, NB, NT, NS = 2048, 256, 192, 7
 MW = 216
+NR = 16 * NT
 F32, BF, I32, U16 = "float32", "bfloat16", "int32", "uint16"
 _S = {
-    "X": (192 + 3392, BF), "JF": (6144, BF), "EN": (3392, BF), "CH": (448, F32), "CHH": (256, BF), "CHL": (256, BF),
-    "SBI": (256, I32), "SBF": (256, F32), "SBU": (256, U16), "SB2": (512, F32), "HS2": (512, F32), "TH2": (512, BF),
+    "X": (192 + 3392, BF), "JF": (6144, BF), "EN": (3392, BF), "CH": (456, F32), "CHH": (256, BF), "CHL": (256, BF),
+    "SBI": (256, I32), "SBF": (256, F32), "SBU": (256, U16), "SB2": (512, F32), "HS2": (512, F32), "SKT": (456, F32),
     "HSK": (256, F32), "HT": (2048, BF), "SIO": (2048, F32), "GH": (4096, BF), "HEL": (128, U16), "HL": (128, U16),
-    "OH": (2048, BF), "SBH": (256, BF), "SBL": (256, BF),
-    "IN": (8 * MW, BF), "OUT": (7 * MW, BF), "LX": (7 * 36, U16),
-    "G": (3264, BF), "D": (3264, BF), "AB": (3072, BF), "EQ": (2304, BF), "ES": (2304, BF),
+    "OH": (2048, BF), "SBH": (256, BF), "SBL": (256, BF), "PK": (256, BF), "OWN": (256, F32),
+    "OUT": (7 * MW, BF), "LX": (7 * 12, U16), "MT": (272, BF), "MA": (512, BF),
+    "G": (NR + 7 * MW, BF), "D": (NR + 8 * MW, BF), "AB": (NR, BF), "EQ": (2304, BF), "ES": (2304, BF),
     "PI": (2, I32), "PJ": (2, I32), "COL": (24, F32), "IM": (144, F32), "IMP": (128, F32), "IG": (128, F32),
-    "BD": (128, BF), "BDF": (128, F32), "ID": (128, BF), "IDF": (128, F32), "IDS": (10 * 128, BF),
-    "ZR": (512, BF), "ONE": (512, BF), "BB": (144, BF), "BND": (10 * 144, BF), "LO": (128, BF), "LC": (128, BF), "LJ": (128, BF),
-    "U": (2048, BF), "DG": (2048, BF), "BD3": (128, BF), "ON0": (384, BF),
-    "R16": (16, F32), "WD": (16, F32), "I16": (16, F32), "SW": (512, BF), "DUP": (256, F32), "CB": (12, BF),
-    "RO": (12, U16), "RO2": (12, U16), "KC": (192, F32), "KC2": (192, F32), "RS": (193, F32), "NI": (192, BF), "II": (60, F32),
-    "OWN": (512, F32), "T1": (48, F32), "T2": (12, I32), "T3": (12, F32), "PEI": (128, I32), "HEI": (128, I32),
+    "BD": (128, BF), "BDF": (128, F32), "ID": (128, BF), "IDS": (9 * 128, BF), "IFS": (4 * 128, F32),
+    "ZR": (512, BF), "ONE": (512, BF), "BB": (144, BF), "BND": (13 * 144, BF), "MX": (9 * 128, BF), "W1": (128, BF),
+    "U": (2048, BF), "DG": (2048, BF), "RC": (192, BF),
+    "R16": (16, F32), "WD": (16, F32), "I16": (16, F32), "SW": (4 * 512, BF), "DUP": (256, F32), "IB": (12, BF),
+    "RO": (12, U16), "RS": (193, F32), "NI": (192, BF), "II": (36, F32), "CM": (192, BF),
+    "T1": (60, F32), "T2": (12, I32), "PEI": (128, I32), "HEI": (128, I32), "DQ": (128, BF),
     "PEB": (128, BF), "HEB": (128, BF), "HIC": (128, BF), "LOC": (128, BF), "BXI": (192, I32), "BXB": (192, BF),
-    "LMI": (2, I32), "LMF": (2, F32), "LIM": (8, F32), "AI": (2, I32),
-    "LM": (12, U16), "HK": (192, F32), "TK": (192, BF), "HR": (192, F32), "TR": (192, BF), "TT": (192, BF),
-    "L1": (192, U16), "CL": (192, U16), "PEN": (192, BF), "KS": (192, F32), "KR": (192, F32),
-    "TM": (192, F32), "A32": (48, I32), "MK": (384, BF), "U1": (192, F32), "Q1": (192, F32),
-    "YJ": (128, F32), "YB": (192, F32), "GE": (384, BF), "DU": (192, BF), "AH": (24, I32), "NS": (192, F32),
-    "AF": (192, BF), "EF": (192, U16), "QI": (24, I32),
-    "NF": (192, BF), "CO": (24, U16), "DE": (384, BF), "EL": (24, U16), "BL": (24, U16), "NE": (384, BF), "SM": (320, F32),
-    "SB": (64, BF), "WH": (576, BF), "FL": (576, BF), "UU": (192, BF), "OD": (192, F32), "SN": (192, F32), "ZM": (192, BF),
-    "SK": (192, F32),
+    "LMI": (2, I32), "LMF": (2, F32), "LIM": (8, F32), "AI": (6, I32),
+    "LM": (12, U16), "HK": (192, F32), "HR": (192, F32), "L1": (192, U16), "CL": (192, U16), "KR": (192, F32),
+    "TM": (192, F32), "A32": (72, I32), "U1": (192, F32), "Q1": (192, F32), "VF": (192, BF),
+    "YJ": (128, F32), "YB": (384, F32), "GE": (384, BF), "AF": (192, BF), "EF": (192, U16),
+    "NZ": (384, BF), "TZ": (192, BF), "FZ": (192, BF),
+    "NF": (192, BF), "CO": (60, U16), "DE": (384, BF), "EL": (24, U16), "BL": (24, U16), "NE": (384, BF), "SM": (192, F32),
+    "KK": (108, BF), "WH": (576, BF), "FL": (384, BF), "UU": (192, BF), "OD": (192, F32), "SK": (192, F32), "LW": (192, BF),
+    "M": (192, BF), "BX": (12, BF),
 }
-TWICE = ("NF", "CO", "DE", "EL", "BL", "NE", "SM", "SB", "WH", "FL", "UU", "OD", "SN", "ZM", "SK")
+TWICE = ("NF", "CO", "DE", "EL", "BL", "NE", "SM", "KK", "WH", "FL", "UU", "OD", "SK", "LW", "M", "BX")
 SCRATCH = {k: ("sbuf", [128, w * (2 if k in TWICE else 1)], d) for k, (w, d) in _S.items()}
 for _b in range(8):
     SCRATCH["b%d" % _b] = ("psum", [128, 512], F32)
-SEMAPHORES = ["cv", "cs", "ct", "cg", "snt"] + ["arr%d" % i for i in range(NS)] + ["d%d" % i for i in range(40)]
+SEMAPHORES = ["cv", "cs", "ct", "cg", "snt"] + ["arr%d" % i for i in range(NS)] + ["d%d" % i for i in range(48)]
 CHAINED = ("b1", "b2", "b3", "b5")
 
-P22, P23, P24 = float(2 ** 22), float(2 ** 23), float(2 ** 24)
-SOME = 1009.0 * 8192
-IDS = {"NID": -1.0, "ID2": 2.0, "IDH": 0.5, "IDP": P24, "IDT": -1.0 / 2048, "E01": -144.0, "I13": 8192.0, "I14": 16384.0,
-       "NI14": -16384.0, "NIK": -1024.0}
-BANDS = ("B0", "B1", "B2", "B03", "BAL", "BK", "BN", "BPQ", "BC", "BE")
+MARK = 192.0
+SPLIT, SOME, VOID = float(2 ** 19), float(2 ** 20), float(2 ** 22)
+IDS = {"NID": -1.0, "IDH": 0.5, "E01": -192.0, "I13": 8192.0, "I12": 4096.0, "IV": VOID,
+       "I8": 256.0}
+IFS = {"IDF": 1.0, "NIF": -1.0, "IDQ": 1.0 / 8192, "I13F": 8192.0}
+MXS = ("LO", "LC", "LJ", "LE", "LN0", "LN1", "BD3", "BDN", "WC")
+BANDS = ("B0", "B1", "B2", "B03", "BAL", "BK", "BN", "BP", "BC", "BE", "BEP", "B5", "BM")
+SCALES = (1.0, 16.0, 192.0, 1024.0)
 CY, GA, SCA, PE, LAT, DMA, REM = 1.04, 1.56, 3.8, 0.53, 90.0, 2300.0, 2500.0
 LOOKS = ((0, 2, 2), (2, 6, 2), (6, 11, 6), (11, 16, 11))
-LOOK0 = ((0, 4, 0), (4, 8, 4), (8, 12, 8), (12, 16, 12))
 ABS = (0, 3, 5, 8, 11, 13, 15, 16)
-KEYS = ((0, 5), (5, 11), (11, 16))
-HTS, GHV, DEV, LOV = 4, 3, 2, 1
-TURNS, SIG, SEED = 2200, 1500.0, 1
+HTS, GHV, DEV, LOV, HKV = 4, 3, 0, 0, 1
+TURNS, SIG, SEED = 1500, 1500.0, 1
 PLAN = []
 
 
@@ -63,10 +64,11 @@ def rank_program(g, core, T, topo):
     par = [0]
     kind = [0]
 
-    def a(name, lo=0, hi=None, st=1, p=None):
-        if name in IDS:
-            j = list(IDS).index(name)
-            return a("IDS", 128 * j, 128 * j + 128)
+    def a(name, lo=0, hi=None, st=1, p=None, old=0):
+        for (buf, names) in (("IDS", list(IDS)), ("IFS", list(IFS)), ("MX", MXS)):
+            if name in names:
+                j = names.index(name)
+                return a(buf, 128 * j, 128 * j + 128)
         if name in BANDS:
             j = BANDS.index(name)
             return a("BND", 144 * j + lo, 144 * j + (144 if hi is None else hi))
@@ -74,7 +76,7 @@ def rank_program(g, core, T, topo):
         if hi is None:
             hi = w
         if name in TWICE:
-            lo, hi = lo + w * par[0], hi + w * par[0]
+            lo, hi = lo + w * (par[0] ^ old), hi + w * (par[0] ^ old)
         ps = slice(None) if p is None else p
         ap = T[name][ps, lo:hi] if st == 1 else T[name][ps, lo:hi:st]
         reg = (name, 0, 512, None) if name in CHAINED else (name, lo, hi, None if p is None else p.start)
@@ -136,7 +138,8 @@ def rank_program(g, core, T, topo):
         if acc is None:
             put("s", [x, bias, scale], [out], lambda: g.scalar.activation(out[0], x[0], f, bias=val(bias), scale=val(scale)), vcost(out, x, 1))
         else:
-            put("s", [x], [out, acc], lambda: g.scalar.activation(out[0], x[0], f, accum_out=acc[0]), vcost(out, x, 1))
+            put("s", [x, bias, scale], [out, acc], lambda: g.scalar.activation(
+                out[0], x[0], f, bias=val(bias), scale=val(scale), accum_out=acc[0]), vcost(out, x, 1) + 20)
 
     def iota(out, pat, base=0, ch=0):
         if _S[out[1][0][0]][1] == I32:
@@ -176,6 +179,10 @@ def rank_program(g, core, T, topo):
     def spread(bank, lo, src, slo, n):
         return [(a(bank, lo + r, lo + 16 * n, 16), a("U", 128 * r, 128 * r + 128), a(src, slo, slo + n)) for r in range(16)]
 
+    def swap(bank, lo, w, src, slo, st=1):
+        return [(a(bank, lo + be, lo + 12, 2), a("SW", 512 * w + 256 * be + 128 * ga, 512 * w + 256 * be + 128 * ga + 128),
+                 a(src, slo + st * ga, slo + st * 11 + 1, 2 * st)) for be in range(2) for ga in range(2)]
+
     def lowest(eq, src, sc, cl):
         for c in range(12):
             ts(a(eq, 208 * c, 192 * c + 192), a(src, 16 * c, 192), a(sc, cl + c, cl + c + 1), Op.is_equal)
@@ -198,6 +205,24 @@ def rank_program(g, core, T, topo):
     def col(j):
         return a("COL", j, j + 1)
 
+    def unit(j):
+        return a("R16", j, j + 1)
+
+    def sm(j, n=1):
+        return a("SM", 12 * j, 12 * (j + n))
+
+    def kk(j, n=1):
+        return a("KK", 12 * j, 12 * (j + n))
+
+    def a32(j, n=1):
+        return a("A32", 12 * j, 12 * (j + n))
+
+    def co(j):
+        return a("CO", 12 * j, 12 * j + 12)
+
+    def rowz(name, k, lo=0):
+        return a(name, lo + k, lo + 192, 16)
+
     ms(a("BXI"), 0)
     ms(a("LMI"), 0)
     dma("y", a("SBI"), hbm(T.sb[:]))
@@ -205,7 +230,7 @@ def rank_program(g, core, T, topo):
     dma("y", a("BXI", p=row(0)), hbm(T.bx[:]))
     dma("s", a("PEI"), hbm(T.pe[:]))
     dma("y", a("LMI", p=row(0)), hbm(T.lim[:]))
-    dma("y", a("IN", 0, 192), hbm(T.zs[:]))
+    dma("y", a("D", NR, NR + 192), hbm(T.zs[:]))
     dma("y", a("X", 192, 192 + NV), hbm(T.xs[:]), None, 2500.0)
     for h in range(2):
         dma("y", a("JF", 2048 * h, 2048 * h + 2048), a("X", 192, 192 + NV), None, 2500.0)
@@ -214,13 +239,17 @@ def rank_program(g, core, T, topo):
     iota(a("IM"), [[1, 144]])
     iota(a("IG"), [[1, 8], [0, 16]])
     iota(a("IMP"), [[1, 128]], 0, -1)
-    iota(a("KC"), [[16, 12], [192, 16]])
-    iota(a("II"), [[0, 5], [16, 12]])
+    iota(a("II"), [[0, 3], [16, 12]])
+    iota(a("W1"), [[0, 8], [16, 16]])
     iota(a("NI"), [[1, 192]])
     iota(a("SIO"), [[1, 2048]])
-    iota(a("OWN"), [[0, 2], [1, 256]])
+    iota(a("OWN"), [[1, 256]])
+    iota(a("MA", 0, 256), [[0, 16], [1, 16]])
+    iota(a("MA", 256, 512), [[1, 16], [0, 16]])
+    iota(a("G", NR, NR + 7 * MW), [[0, 7 * MW]], 1)
     ms(a("ZR"), 0.0)
     ms(a("JF", 4096, 6144), 0.0)
+    fill(a("ONE"), 1.0)
     act(a("EN", 0, NV), a("JF", 4096, 6144))
     ts(a("PJ", 0, 1), a("PI", 0, 1), 15, Op.bitwise_and)
     ts(a("PJ", 1, 2), a("PI", 0, 1), 4, Op.logical_shift_right)
@@ -235,52 +264,52 @@ def rank_program(g, core, T, topo):
     dma("y", a("JF", 4096, 6144, p=row(0)), a("HIC"))
     dma("y", a("JF", 4096, 6144, p=row(2)), a("LOC"))
     ts(a("R16"), a("IM", 0, 16), col(0), Op.is_equal)
-    ts(col(11), a("R16", 1, 2), 1024.0, Op.mult, a("R16", 0, 1), Op.add)
+    ts(col(11), unit(2), 2.0, Op.mult)
     ts(col(5), col(0), 3.5, Op.is_lt)
     ts(col(6), col(0), 256.0, Op.mult)
-    fill(a("ON0", 0, 192), 1.0)
-    fill(a("ON0", 192, 384), 0.0)
+    ts(col(7), unit(4), 8192.0, Op.mult, col(5), Op.add)
     ts(a("BD"), a("IG"), col(1), Op.is_equal)
     act(a("BDF"), a("BD"))
     ts(a("ID"), a("IMP"), 0.0, Op.is_equal)
-    act(a("IDF"), a("ID"))
+    for nm, w in IFS.items():
+        act(a(nm), a("ID"), scale=w)
     ts(a("BB"), a("IM"), col(4), Op.is_equal)
-    for nm, w in (("B2", a("R16", 2, 3)), ("B0", a("R16", 0, 1)), ("B03", col(5)), ("B1", a("R16", 1, 2)), ("BAL", 8192.0),
-                  ("BK", col(6)), ("BN", -8192.0), ("BPQ", col(11))):
+    for nm, w in (("B2", unit(2)), ("B0", unit(0)), ("B03", col(5)), ("B1", unit(1)), ("BAL", 512.0), ("BK", col(6)), ("BN", -8192.0),
+                  ("BP", 8192.0), ("BEP", col(7)), ("B5", unit(5))):
         act(a(nm), a("BB"), scale=w)
     for be in range(2):
         for ga in range(2):
             ts(a("SW", 256 * be + 128 * ga, 256 * be + 128 * ga + 128), a("IMP"), 16.0 * (ga - be), Op.is_equal, col(2 + be), Op.mult)
         msum(a("DUP", 128 * be, 128 * be + 128), [("ID", a("SW", 256 * be + 128 * ga, 256 * be + 128 * ga + 128)) for ga in range(2)])
+    for w in range(1, 4):
+        ts(a("SW", 512 * w, 512 * w + 512), a("SW", 0, 512), SCALES[w], Op.mult)
     for r in range(16):
-        ts(a("U", 128 * r, 128 * r + 128), a("BD"), a("R16", r, r + 1), Op.mult)
+        ts(a("U", 128 * r, 128 * r + 128), a("BD"), unit(r), Op.mult)
         kind[0] -= 1
     kind[0] += 1
-    ms(a("CB", 0, 12, 2), 0.0)
-    ms(a("CB", 1, 12, 2), 256.0)
     cp(a("SBF"), a("SBI"))
     cp(a("HEB"), a("HEI"))
     cp(a("PEB"), a("PEI"))
-    dma("y", a("EN", 0, NV, p=row(1)), a("HEB"))
-    dma("y", a("EN", 0, NV, p=row(0)), a("PEB"))
+    tt(a("DQ"), a("HEI"), a("PEI"), Op.subtract)
+    for j, x in ((1, a("HEB")), (0, a("PEB")), (3, a("DQ")), (2, a("ONE", 0, 128))):
+        dma("y", a("EN", 0, NV, p=row(j)), x)
     mm([(a("b1", 0, 256), a("DUP", 0, 128), a("SBF"))])
     mm([(a("b1", 256, 512), a("DUP", 128, 256), a("SBF"))])
     act(a("SB2"), a("b1"))
     cp(a("BXB"), a("BXI"))
-    mm(pick("b6", 0, "B0", "BXB", 0, 12))
+    tr(a("TZ"), a("BXB"))
+    cp(a("D", NR + 192, NR + 204), rowz("TZ", 0))
+    ms(a("D", NR + 204, NR + 216), 0.0)
     ts(a("II"), a("II"), col(0), Op.add)
-    ts(a("II", 36, 48), a("II", 36, 48), 256.0, Op.add)
-    ts(a("II", 48, 60), a("II", 48, 60), 3072.0, Op.add)
+    cp(a("IB"), a("II", 0, 12))
+    ts(a("II", 12, 24), a("II", 12, 24), 256.0, Op.add)
+    ts(a("II", 24, 36), a("II", 24, 36), -192.0, Op.add)
     ts(a("T1", 0, 12), a("II", 0, 12), -5.5, Op.add, 1.0 / 12, Op.mult)
     cp(a("T2"), a("T1", 0, 12))
-    ts(a("T3"), a("T2"), -191.0, Op.mult)
+    ts(a("T1", 48, 60), a("T2"), -191.0, Op.mult)
     ts(a("T1", 16, 28), a("II", 0, 12), 16.0, Op.mult)
-    tt(a("T1", 32, 44), a("T1", 16, 28), a("T3"), Op.add)
+    tt(a("T1", 32, 44), a("T1", 16, 28), a("T1", 48, 60), Op.add)
     cp(a("RO"), a("T1", 32, 44))
-    ts(col(9), col(0), 12.0, Op.mult)
-    ts(a("RO2"), a("IM", 0, 12), col(9), Op.add)
-    cp(a("IN", 192, 204), a("b6", 0, 12))
-    ms(a("IN", 204, 216), 0.0)
     ts(a("WD"), a("IM", 0, 16), col(0), Op.is_gt)
     ts(a("I16"), a("R16"), -256.0, Op.mult)
     tt(a("WD"), a("WD"), a("I16"), Op.add)
@@ -291,39 +320,59 @@ def rank_program(g, core, T, topo):
     for nm, w in IDS.items():
         act(a(nm), a("ID"), scale=w)
     act(a("BD3"), a("BD"), scale=col(5))
-    ts(col(7), col(0), 2.0, Op.mult)
-    act(a("KC"), a("KC"), bias=col(7), scale=2.0)
-    act(a("KC2"), a("KC"), bias=2.0)
+    act(a("BDN"), a("BD"), scale=-4096.0)
     fill(a("RS"), 0.0)
     ms(a("RS", 1, 193, 16), float(2 ** 27))
     ms(a("TM", 0, 1), 0.0)
-    fill(a("G", 3072, 3264), 0.0)
-    fill(a("CH"), 0.0)
-    fill(a("ONE"), 1.0)
+    fill(a("CH", 0, 448), 0.0)
+    ms(a("CH", 448, 456), 1.0)
+    fill(a("SKT", 256, 456), 0.0)
+    fill(a("YB", 192, 384), 0.0)
+    fill(a("CM"), MARK)
+    ts(a("MA"), a("MA"), col(0), Op.is_equal)
+    mm([(a("b7", 256, 512), a("ID"), a("MA", 256 * j, 256 * j + 256)) for j in range(2)])
+    act(a("MT", 1, 257), a("b7", 256, 512), bias=1.0)
+    ms(a("MT", 0, 1), 0.0)
+    ms(a("MT", 257, 272), 1.0)
     cp(a("LMF"), a("LMI"))
     mm([(a("b6", 16, 18), a("BDF"), a("LMF"))])
-    ts(a("LIM", 0, 1), a("b6", 16, 17), -P22, Op.add)
+    ts(a("LIM", 0, 1), a("b6", 16, 17), -73728.5, Op.add)
     cp(a("LIM", 1, 2), a("LIM", 0, 1))
-    ts(a("LIM", 2, 3), a("b6", 17, 18), 1.0, Op.add, 1009.0, Op.min)
-    ts(a("LIM", 2, 3), a("LIM", 2, 3), 8192.0, Op.mult)
     ms(a("LIM", 3, 4), 0.0)
+    ts(a("LIM", 2, 3), a("b6", 17, 18), 1008.0, Op.min, -1.0, Op.mult)
+    ts(a("AI", 2, 3), a("LIM", 2, 3), 1023.0, Op.add)
+    ts(a("AI", 3, 4), a("AI", 2, 3), 5, Op.logical_shift_right)
+    ts(a("AI", 4, 5), a("AI", 2, 3), 31, Op.bitwise_and)
+    ts(col(12), a("AI", 3, 4), unit(0), Op.mult, unit(2), Op.add)
+    ts(col(12), a("AI", 4, 5), unit(1), Op.mult, col(12), Op.add)
+    fill(a("RC"), col(12))
+    ts(col(13), unit(0), 16384.0, Op.mult)
+    ts(col(13), unit(1), 512.0, Op.mult, col(13), Op.add)
+    ts(a("W1"), a("W1"), unit(2), Op.mult, col(13), Op.add)
+    tt(a("WC"), a("W1"), a("BD"), Op.mult)
     act(a("SBH"), a("SBF"))
     dma("y", a("JF", 0, 4096, p=row(2)), a("SBH"))
     mm([(a("b7", 0, 256), a("IDF"), a("SBF")), (a("b7", 0, 256), a("NID"), a("SBH"))])
     act(a("SBL"), a("b7", 0, 256))
     dma("y", a("JF", 0, 4096, p=row(3)), a("SBL"))
+    for j in (0, 1, 4):
+        dma("y", a("JF", 0, 4096, p=row(j)), a("ZR", 0, 256))
     mm(pick("b6", 128, "B1", "EN", 0, 128))
     act(a("BC"), a("B0"), scale=4096.0)
     act(a("BE"), a("B0"), scale=-8192.0)
-    msum(a("LO"), [("ID", band("BN", 0)), ("ID", band("BN", 1)), ("ID", band("BK", 2)), ("NID", band("BN", 3))])
+    act(a("BM"), a("B0"), scale=-1.0)
+    msum(a("LO"), [("ID", band("BN", 0)), ("ID", band("BN", 1)), ("ID", band("BK", 2)), ("ID", band("BP", 3))])
     msum(a("LC"), [("ID", band("BC", 0)), ("ID", band("BE", 3))])
     msum(a("LJ"), [("ID", band("B0", 0)), ("ID", band("B2", 1))])
+    msum(a("LE"), [("ID", band("B1", 3)), ("ID", band("B0", 5))])
+    msum(a("LN0"), [("ID", band("B5", 0)), ("NID", band("B5", 3))])
+    act(a("LN1"), band("B5", 3))
     cp(a("SBU"), a("SBI"))
     cp(a("HEL"), a("b6", 128, 256))
     for h in range(4):
         bk = ("b1", "b7")[h % 2]
         tt(a("OH", 512 * h, 512 * h + 512), ind(a("SBF"), a("HEL", 32 * h, 32 * h + 32)), a("SIO", 512 * h, 512 * h + 512), Op.is_equal)
-        mm([(a(bk), a("LC"), a("ONE")), (a(bk), band("B1", 3), a("EN", 512 * h, 512 * h + 512)),
+        mm([(a(bk), a("LC"), a("ONE")), (a(bk), a("LE"), a("EN", 512 * h, 512 * h + 512)),
             (a(bk), a("LJ"), a("JF", 4096 + 512 * h, 4608 + 512 * h)), (a(bk), a("LO"), a("OH", 512 * h, 512 * h + 512))])
         if h < HTS:
             act(a("HT", 512 * h, 512 * h + 512), a(bk), Fn.Relu)
@@ -332,8 +381,13 @@ def rank_program(g, core, T, topo):
     for h in range(8):
         (cp if h < GHV else act)(a("GH", 512 * h, 512 * h + 512), ind(a("HT"), a("SBU", 32 * h, 32 * h + 32)))
 
-    def unmark(t, part):
-        cp(ind(a("X", 0, 192 + NV + NT * (t + 1)), a("LX", 36 * t + 12 * part, 36 * t + 12 * part + 12)), a("IN", MW * t, MW * t + 192))
+    def numbers(t, upto, plus):
+        out = ind(a("X", 0, 192 + NV + NT * upto), a("LX", 12 * t, 12 * t + 12))
+        z = a("D", NR + MW * t, NR + MW * t + 192)
+        if plus is None:
+            cp(out, z)
+        else:
+            tt(out, z, plus, Op.add)
 
     first = 0
     for t in range(NS):
@@ -343,202 +397,200 @@ def rank_program(g, core, T, topo):
         if t > 1:
             kind[0] = first
         last = t == NS - 1
-        z = a("IN", MW * t, MW * t + 192)
-        ao = MW * t + 192
-        box = a("IN", ao, ao + 12)
-        back = a("IN", ao + 12, ao + 24)
+        zo = NR + MW * t
+        z = a("D", zo, zo + 192)
+        ao = zo + 192
+        box = a("D", ao, ao + 12)
+        rest = a("D", ao + 12, ao + 24)
         wide = NV + NT * t
-        it = [(a("b0", 0, 12), a("ID"), a("CB"))]
-        for be in range(2):
-            for ga in range(2):
-                it.append((a("b0", be, 12, 2), a("SW", 256 * be + 128 * ga, 256 * be + 128 * ga + 128), a("IN", ao + ga, ao + 12, 2)))
-        mm(it)
-        cp(a("LM"), a("b0", 0, 12))
-        cp(a("HK"), ind(a("HS2" if t else "SB2"), a("LM")))
+        cp(a("LM", 0, 12, 2), a("D", ao, ao + 12, 2))
+        ts(a("LM", 1, 12, 2), a("D", ao + 1, ao + 12, 2), 256.0, Op.add)
+        (cp if HKV else act)(a("HK"), ind(a("HS2" if t else "SB2"), a("LM")))
         tr(a("HR"), a("HK"))
         cp(a("L1"), ind(a("HR"), a("RO")))
-        if t:
-            act(a("TK"), ind(a("TH2"), a("LM")))
-            tr(a("TR"), a("TK"))
-            act(a("TT"), ind(a("TR"), a("RO")))
-        jw = a("JF") if t else a("JF", 4096, 6144)
-        banks = ["b0", "b1", "b6", "b7"]
-        for q, (k0, k1, kv) in enumerate(LOOKS if t else LOOK0):
+        banks = [("b0", 0), ("b1", 0), ("b6", 64), ("b7", 0)]
+        for q, (k0, k1, kv) in enumerate(LOOKS if t else ()):
             if kv > k0:
-                cp(a("G", 192 * k0, 192 * kv), ind(jw, a("L1", 12 * k0, 12 * kv)))
+                cp(a("G", 192 * k0, 192 * kv), ind(a("JF"), a("L1", 12 * k0, 12 * kv)))
             if kv < k1:
-                act(a("G", 192 * kv, 192 * k1), ind(jw, a("L1", 12 * kv, 12 * k1)))
-            if t:
-                w = 12 * (k1 - k0)
-                mm(pick(banks[q], 0, "B03", "G", 192 * k0, w))
-                cp(a("CL", 12 * k0, 12 * k1), a(banks[q], 0, w))
-                tt(a("PEN", 12 * k0, 12 * k1), a(banks[q], 0, w), a("TT", 12 * k0, 12 * k1), Op.is_ge)
-        mm([zero("b4", 0, 192)] + spread("b4", 0, "IN", ao, 12))
-        ts(a("SM", 0, 12), back, t + 0.5, Op.is_gt, 8192.0, Op.mult)
-        tt(a("SB", 0, 12), box, a("SM", 0, 12), Op.add)
-        cp(a("BL", 0, 12), box)
+                act(a("G", 192 * kv, 192 * k1), ind(a("JF"), a("L1", 12 * kv, 12 * k1)))
+            w = 12 * (k1 - k0)
+            bk, lo = banks[q]
+            mm(pick(bk, lo, "B03", "G", 192 * k0, w))
+            cp(a("CL", 12 * k0, 12 * k1), a(bk, lo, lo + w))
+        if t:
+            ts(kk(6), rest, 0.5, Op.is_gt)
+            ts(rest, rest, -1.0, Op.add, 0.0, Op.max)
+        mm([zero("b6", 32, 12)] + swap("b6", 32, 0, "D", ao) + (swap("b6", 32, 3, "KK", 72 + 108 * 0) if t else []))
+        ts(a("BX"), a("b6", 32, 44), 448.0, Op.min)
+        cp(a("BL", 0, 12), a("BX"))
+        mm([zero("b4", 0, 192)] + spread("b4", 0, "BX", 0, 12))
         act(a("AF"), a("b4", 0, 192))
-        lowest("ES", "AF", "SB", 0)
-        act(a("NF"), a("b5", 0, 192), bias=256.0 * P24 - P22, scale=P24)
-        mm(pick("b6", 84, "B0", "NF", 0, 12))
-        tt(a("SM", 24, 36), a("b6", 84, 96), box, Op.max)
-        tt(a("SM", 36, 48), a("SM", 24, 36), a("II", 36, 48), Op.min)
-        cp(a("BL", 12, 24), a("SM", 36, 48))
-        act(a("OD"), ind(a("CH", 0, 256), a("BL", 0, 12)))
-        act(a("SK"), ind(a("SBF"), a("BL", 0, 12)))
-        act(a("SN"), a("SK"), bias=float(wide), scale=-1.0)
-        mm([(a("b1", 256, 448), a("IDF"), a("SN")), (a("b1", 256, 448), a("ID"), a("NI"))])
-        act(a("NS"), a("b1", 256, 448))
-        act(a("D", 3072, 3264), z)
+        lowest("ES", "AF", "BX", 0)
+        act(a("NF"), a("b5", 0, 192), Fn.Sign, bias=256.0)
+        tr(a("FZ"), a("NF"))
+        mm([(a("b7", 192, 204), a("ID"), a("BX"))] + swap("b7", 192, 3, "FZ", 0, 16))
+        tt(sm(1), a("b7", 192, 204), a("II", 12, 24), Op.min)
+        cp(a("BL", 12, 24), sm(1))
+        act(a("SK"), ind(a("SKT" if t else "SBF"), a("BL", 0, 12)))
+        mm([(a("b1", 256, 448), a("ID"), a("NI")), (a("b1", 256, 448), a("NIF"), a("SK"))], True, False)
+        key = a("b3", 0, 192)
+        mm([(key, a("WC"), a("RC"))], True, False)
+        if t:
+            act(a("OD"), ind(a("CH"), a("BL", 0, 12)))
+            act(a("VF"), a("OD"), Fn.Sign)
+            mm([(key, a("IDQ"), a("SK"))], False, False)
+            mm([(key, a("IV"), a("VF"))], False, False)
         cl = "CL" if t else "L1"
-        mm([zero("b2", 0, 192)], True, False)
         for k in range(16):
             tt(a("D", 192 * k, 192 * k + 192), ind(a("X", 192, 192 + wide), a(cl, 12 * k, 12 * k + 12)), z, Op.subtract)
             kind[0] -= 1
         kind[0] += 1
-        if t:
-            mm([(a("b2", 0, 192), a("IDP"), a("PEN")), (a("b2", 0, 192), a("IDT"), a("TT"))], False, False)
         for k0, k1 in zip(ABS, ABS[1:]):
             act(a("AB", 192 * k0, 192 * k1), a("D", 192 * k0, 192 * k1), Fn.Abs)
-        for (k0, k1) in KEYS:
-            mm(pick("b2", 12 * k0, "BAL", "AB", 192 * k0, 12 * (k1 - k0)), False, k1 == 16)
-        for h in range(4):
-            mm([(a("b3", 0, 384), a("IDP"), a("ON0"))] * (h == 0)
-               + [(a("b3", 0, 192), band("BAL", k), a("AB", 192 * k, 192 * k + 192)) for k in range(4 * h, 4 * h + 4)], h == 0, False)
-        act(a("KS"), a("b2", 0, 192))
-        tt(a("KR"), ind(a("KS"), a("RO2")), a("KC2" if t else "KC"), Op.add)
+            mm([(key, band("BAL", k), a("AB", 192 * k, 192 * k + 192)) for k in range(k0, k1)], False, k1 == 16)
+        tr(a("KR"), key)
         m1, m2 = a("b2", 15, 192, 16), a("b2", 207, 384, 16)
         scan(a("b2", 0, 192), a("RS", 1, 193), a("KR"))
-        cp(a("A32", 0, 12), m1)
-        ts(a("A32", 24, 36), a("A32", 0, 12), 1, Op.logical_shift_right, 4095, Op.bitwise_and)
-        ts(a("SM", 60, 72), m1, SOME, Op.is_ge, 8192.0, Op.mult)
-        tt(a("SM", 72, 84), a("SM", 60, 72), a("SM", 0, 12), Op.add)
-        tt(a("SM", 48, 60), a("SM", 72, 84), a("II", 48, 60), Op.min)
-        tt(a("SM", 12, 24), a("SM", 48, 60), a("A32", 24, 36), Op.max)
-        cp(a("CO", 0, 12), a("SM", 12, 24))
-        act(a("GE", 0, 192), ind(a("G"), a("CO", 0, 12)))
-        ts(a("SB", 24, 36), m1, a("LIM", 2, 3), Op.is_ge, -3 * P23, Op.mult)
-        ts(a("SM", 180, 192), m1, a("LIM", 2, 3), Op.is_ge, 4096.0, Op.mult)
+        ts(a32(0), m1, SOME + 256 + 18 * t, Op.min)
+        ts(a32(2), a32(0), 1, Op.logical_shift_right, 255, Op.bitwise_and)
+        ts(kk(0), a32(2), 0.125, Op.mult)
+        mm([(a("b7", 64, 76), a("ID"), a("IB"))] + swap("b7", 64, 2, "KK", 0))
+        cp(co(0), a("b7", 64, 76))
+        ts(kk(2), m1, SPLIT, Op.is_ge, -32768.0, Op.mult)
         tt(a("TM", 1, 192), a("b2", 0, 191), a("KR", 1, 192), Op.max)
         scan(a("b2", 192, 384), a("RS", 0, 192), a("TM"))
-        cp(a("A32", 12, 24), m2)
-        ts(a("SM", 192, 204), m2, SOME, Op.is_ge, 4096.0, Op.mult)
-        ts(a("A32", 36, 48), a("A32", 12, 24), 1, Op.logical_shift_right, 4095, Op.bitwise_and)
-        cp(a("CO", 12, 24), a("A32", 36, 48))
-        mm(pick("b6", 480, "B03", "GE", 0, 12))
+        ts(a32(1), m2, SOME + 256, Op.min)
+        ts(a32(3), a32(1), 1, Op.logical_shift_right, 255, Op.bitwise_and)
+        ts(kk(1), a32(3), 0.125, Op.mult)
+        mm([(a("b7", 76, 88), a("ID"), a("IB"))] + swap("b7", 76, 2, "KK", 12))
+        cp(co(1), a("b7", 76, 88))
+        for j in range(2):
+            if t:
+                act(a("GE", 192 * j, 192 * j + 192), ind(a("G", 0, zo + 192), co(j)))
+            else:
+                ts(kk(7 + j), a32(2 + j), 32.0, Op.mult)
+                mm([(a("b0", 32 + 12 * j, 44 + 12 * j), a("ID"), a("BX"))] + swap("b0", 32 + 12 * j, 0, "KK", 84 + 12 * j))
+                cp(co(2 + j), a("b0", 32 + 12 * j, 44 + 12 * j))
+                act(a("GE", 192 * j, 192 * j + 192), ind(a("JF", 0, 4096), co(2 + j)))
+        ne = 1 if t else 2
+        e = a("b6", 0, 12)
         mm([(a("b4", 192, 384), a("BD3"), a("GE", 0, 192))])
-        act(a("GE", 192, 384), ind(a("G"), a("CO", 12, 24)))
-        mm(pick("b6", 492, "B03", "GE", 192, 12))
+        mm(pick("b6", 0, "BEP", "GE", 0, 12))
         de, df = a("DE", 0, 192), a("DE", 192, 384)
-        (cp if DEV & 1 else act)(de, ind(a("D"), a("CO", 0, 12)))
-        (cp if DEV & 2 else act)(df, ind(a("D"), a("CO", 12, 24)))
-        mm([(a("b0", 0, 192), a("ID"), de), (a("b0", 0, 192), a("ID2"), z)])
-        mm([(a("b6", 96, 288), a("ID"), de), (a("b6", 96, 288), a("NID"), df)])
-        tt(a("SM", 84, 96), a("b6", 480, 492), a("SM", 72, 84), Op.add)
-        cp(a("EL", 0, 12), a("b6", 480, 492))
-        cp(a("EL", 12, 24), a("b6", 492, 504))
-        ts(a("SM", 96, 108), a("b6", 480, 492), 2047.5, Op.is_gt, 4096.0, Op.mult)
-        ts(a("SM", 120, 132), a("b6", 480, 492), 192.0, Op.add)
-        act(a("NE", 0, 192), ind(a("EN", 0, wide), a("EL", 0, 12)))
-        act(a("NE", 192, 384), ind(a("EN", 0, wide), a("EL", 12, 24)))
+        (cp if DEV & 1 else act)(de, ind(a("D", 0, zo + 192), co(0)))
+        (cp if DEV & 2 else act)(df, ind(a("D", 0, zo + 192), co(1)))
+        ts(a("EL", 0, 12), e, float(wide - 1), Op.min)
+        tt(sm(2), e, a("II", 24, 36), Op.subtract)
+        if not t:
+            mm(pick("b7", 160, "BEP", "GE", 192, 12))
+            cp(a("EL", 12, 24), a("b7", 160, 172))
+        for j in range(ne):
+            act(a("NE", 192 * j, 192 * j + 192), ind(a("EN", 0, wide), a("EL", 12 * j, 12 * j + 12)))
         act(a("WH", 0, 192), de, Fn.Abs)
-        act(a("WH", 192, 384), a("b0", 0, 192), bias=143.75, scale=0.5)
-        act(a("WH", 384, 576), a("b6", 96, 288), Fn.Abs)
-        nq = 12 if t else 24
-        mm(pick("b7", 448, "BPQ", "NE", 0, nq)
-           + [(a("b7", 448 + 12 * j, 460 + 12 * j), a(w), box) for j in range(nq // 12) for w in ("NID", "NIK")])
-        ts(a("QI", 0, nq), a("b7", 448, 448 + nq), 1.0 / 1024, Op.mult)
-        ts(a("SM", 288, 300), a("QI", 0, 12), -1024.0, Op.mult)
-        tt(a("SM", 300, 312), a("b7", 448, 460), a("SM", 288, 300), Op.add)
-        mm([(a("b2", 192, 384), a("ID"), a("WH", 192, 384)), (a("b2", 192, 384), a("NID"), a("WH", 0, 192)),
-            (a("b2", 192, 384), a("E01"), a("ONE", 0, 192))])
-        mm([(a("b7", 64, 256), a("BD3"), a("GE", 192, 384))])
-        ts(a("SM", 132, 144), a("SM", 300, 312), 0.0, Op.is_equal)
-        tt(a("SM", 144, 156), a("QI", 0, 12), a("SM", 132, 144), Op.mult)
-        tt(a("SM", 156, 168), a("SM", 300, 312), a("SM", 144, 156), Op.add)
-        ts(a("SM", 108, 120), a("SM", 96, 108), 1.0 / 4096, Op.mult, t + 2.0, Op.add)
-        tt(a("SM", 168, 180), a("SM", 108, 120), back, Op.subtract)
+        act(a("WH", 192, 384), de, bias=191.75, scale=0.5)
+        mm([(a("b0", 64, 256), a("ID"), de), (a("b0", 64, 256), a("NID"), df)])
+        act(a("WH", 384, 576), a("b0", 64, 256), Fn.Abs)
+        tr(a("NZ", 0, 192 * ne), a("NE", 0, 192 * ne))
+        tt(sm(4), rowz("NZ", 0), box, Op.is_equal)
+        tt(sm(3), rowz("NZ", 0), box, Op.subtract)
+        tt(sm(5), sm(4), rowz("NZ", 3), Op.mult)
+        tt(sm(6), sm(5), sm(3), Op.add)
+        mm([(a("b2", 192, 384), a(w), x) for (w, x) in (
+            ("ID", z), ("E01", a("ONE", 0, 192)), ("ID", a("WH", 192, 384)), ("NID", a("WH", 0, 192)))])
         cp(a("EF"), a("b4", 192, 384))
-        lowest("EQ", "EF", "SM", 84)
-        act(a("FL", 192, 384), a("b5", 0, 192), Fn.Relu, bias=-255.0, scale=-1.0)
-        mm(pick("b6", 72, "B0", "FL", 192, 12))
-        tt(a("UU"), a("b2", 192, 384), a("FL", 192, 384), Op.mult)
-        mm([(a("b0", 0, 192), a("ID"), a("WH", 0, 192)), (a("b0", 0, 192), a("ID"), a("UU"))])
-        act(a("OUT", MW * t, MW * t + 192), a("b0", 0, 192))
-        tk = a("b6", 72, 84)
-        tt(a("SM", 240, 252), tk, a("SM", 156, 168), Op.mult)
-        tt(a("SM", 252, 264), tk, a("SM", 168, 180), Op.mult)
-        tt(a("OUT", MW * t + 192, MW * t + 216), a("SM", 240, 264), a("IN", ao, ao + 24), Op.add)
+        lowest("EQ", "EF", "b6", 0)
+        act(a("FL", 0, 192), a("b5", 0, 192), Fn.Relu, bias=-255.0, scale=-1.0)
+        tr(a("TZ"), a("FL", 0, 192))
+        tt(a("UU"), a("b2", 192, 384), a("FL", 0, 192), Op.mult)
+        mm([(a("b0", 256, 448), a("ID"), a("WH", 0, 192)), (a("b0", 256, 448), a("ID"), a("UU"))])
+        act(a("OUT", MW * t, MW * t + 192), a("b0", 256, 448))
+        tt(sm(7), rowz("TZ", 0), sm(6), Op.mult)
+        tt(sm(8), rowz("TZ", 0), rowz("NZ", 2), Op.mult)
+        tt(a("OUT", MW * t + 192, MW * t + 216), sm(7, 2), a("D", ao, ao + 24), Op.add)
         dst = T.cores[(rank + 1) % N if not last else (rank - t) % N]
         rid, pid = topo.addr(dst, core)
         eng = topo.engines(core, dst)[:8]
-        src, land, arr = a("OUT", MW * t, MW * t + MW), a("IN", MW * (t + 1), MW * (t + 2)), "arr%d" % t
+        src, land, arr = a("OUT", MW * t, MW * t + MW), a("D", zo + MW, zo + 2 * MW), "arr%d" % t
         put("g", [src], [land], lambda src=src, land=land, arr=arr, pid=pid, rid=rid, eng=eng: g.remote_dma(
             land[0], src[0], T.sem[arr], T.sem.snt, pid, rid, sum(1 << e for e in eng)), 500.0, arr, len(eng), lat=REM - 500)
-        tt(a("MK", 0, 192), a("b4", 192, 384), a("SK"), Op.is_equal)
-        tt(a("MK", 192, 384), a("b7", 64, 256), a("SK"), Op.is_equal)
         if t:
-            ts(a("AH"), a("A32", 0, 24), 1, Op.bitwise_and)
-            ts(a("SM", 264, 288), a("AH"), 0.0, Op.is_equal, 4096.0, Op.mult)
+            ts(a32(4, 2), a32(0, 2), 1, Op.bitwise_and)
+            tt(kk(3), a32(4), a32(5), Op.add)
         else:
-            ts(a("SM", 264, 288), a("QI"), 0.0, Op.not_equal, 4096.0, Op.mult)
-        tt(a("SM", 180, 204), a("SM", 180, 204), a("SM", 264, 288), Op.add)
-        tt(a("SB", 36, 48), a("SM", 180, 192), a("SM", 192, 204), Op.add)
-        mm([(a("b3", 192, 384), a("ID"), a("NF"))], False, False)
-        mm([(a("b3", 192, 384), a("BD"), a("WH", 384, 576))], False, False)
-        mm(spread("b3", 0, "SB", 24, 24), False, True)
-        ts(a("FL", 384, 576), a("b3", 192, 384), a("LIM", 1, 2), Op.is_lt)
-        tt(a("U1"), a("b3", 0, 192), a("OD"), Op.min)
-        act(a("U1"), a("U1"), Fn.Relu)
-        mm([(a("b1", 0, 192), a("NI14"), a("ONE", 0, 192)), (a("b1", 0, 192), a("I13"), a("MK", 0, 192)),
-            (a("b1", 0, 192), a("I13"), a("MK", 192, 384))], True, False)
-        mm([(a("b1", 0, 192), a("I14"), a("FL", 384, 576))], False, True)
-        tt(a("Q1"), a("b1", 0, 192), a("NS"), Op.min)
-        tt(ind(a("CH"), a("BL", 12, 24)), a("U1"), a("Q1"), Op.max)
+            for j in range(2):
+                tt(kk(3 + j), rowz("NZ", 1, 192 * j), box, Op.not_equal)
+        code = a("b7", 88, 100)
+        mm([(code, a("ID"), a("ONE", 0, 12))] + swap("b7", 88, 0, "KK", 0) + swap("b7", 88, 1, "KK", 12) + swap("b7", 88, 0, "KK", 24)
+           + swap("b7", 88, 3, "FZ", 0, 16) + swap("b7", 88, 3, "KK", 36) + ([] if t else swap("b7", 88, 3, "KK", 48)))
+        ts(co(4), code, 257.0, Op.min)
+        act(a("M"), ind(a("MT"), co(4)))
+        sg = a("FL", 192, 384)
+        mm([(a("b6", 256, 448), a("BD"), a("WH", 384, 576)), (a("b6", 256, 448), a("BDN"), a("M"))])
+        act(sg, a("b6", 256, 448), Fn.Sign, bias=a("LIM", 1, 2), scale=-1.0, acc=a("LIM", 4, 5))
+        mm([(a("b1", 256, 448), a("I13"), a("M"))], False, False)
+        mm([(a("b1", 256, 448), a("I12"), sg)], False, True)
+        act(a("Q1"), a("b1", 256, 448), Fn.Relu, bias=float(wide - 20480))
+        if t:
+            act(a("VF"), key, Fn.Relu, bias=-VOID - SOME)
+            mm([(a("b3", 192, 384), a("ID"), a("VF")), (a("b3", 192, 384), a("I13"), a("M"))])
+            tt(a("U1"), a("b3", 192, 384), a("OD"), Op.min)
+            tt(ind(a("CH", 0, 448), a("BL", 12, 24)), a("U1"), a("Q1"), Op.max)
+        else:
+            cp(ind(a("CH", 0, 448), a("BL", 12, 24)), a("Q1"))
         act(a("CHH"), a("CH", 0, 256))
-        dma("y", a("JF", 0, 4096, p=row(0)), a("CHH"), "d38")
+        dma("y", a("JF", 0, 4096, p=row(0)), a("CHH"), "d46")
         if LOV:
             tt(a("CHL"), a("CH", 0, 256), a("CHH"), Op.subtract)
         else:
-            mm([(a("b3", 0, 256), a("IDF"), a("CH", 0, 256))], True, False)
-            mm([(a("b3", 0, 256), a("NID"), a("CHH"))], False, True)
-            act(a("CHL"), a("b3", 0, 256))
-        dma("y", a("JF", 0, 4096, p=row(1)), a("CHL"), "d39")
-        mm([(a("b4", 0, 192), a("ID"), z), (a("b4", 0, 192), a("IDH"), de), (a("b4", 0, 192), a("IDH"), df),
-            (a("b4", 0, 192), a("IDH"), a("WH", 384, 576))])
+            mm([(a("b3", 256, 512), a("IDF"), a("CH", 0, 256))], True, False)
+            mm([(a("b3", 256, 512), a("NID"), a("CHH"))], False, True)
+            act(a("CHL"), a("b3", 256, 512))
+        dma("y", a("JF", 0, 4096, p=row(1)), a("CHL"), "d47")
+        mm([(a("b4", 0, 192), a(w), x) for (w, x) in (
+            ("ID", z), ("IDH", de), ("IDH", df), ("IDH", a("WH", 384, 576)), ("I8", sg))])
+        act(a("X", 192 + wide, 192 + wide + 192), a("b4", 0, 192), Fn.Relu, bias=-256.0)
         if not last:
-            mm([(a("b4", 192, 384), band("B0", 0), a("NE", 0, 192)), (a("b4", 192, 384), band("B0", 1), a("NE", 192, 384))])
-            act(a("EN", wide, wide + 192), a("b4", 192, 384))
-            act(a("ZM"), z, bias=128.0)
-            act(a("DU"), a("FL", 384, 576), acc=a("LIM", 4, 5))
-            act(a("LIM", 3, 4), a("LIM", 3, 4), bias=a("LIM", 4, 5))
-            cp(a("AI", 0, 1), a("LIM", 3, 4))
+            if t:
+                mm([(a("b4", 192, 384), a("LN%d" % j), a("GE", 192 * j, 192 * j + 192)) for j in range(2)])
+            else:
+                mm([(a("b4", 192, 384), w, a("NE", 192 * j, 192 * j + 192))
+                    for (w, j) in ((band("B0", 0), 0), (band("BM", 3), 0), (band("B0", 3), 1))])
+            act(a("EN", wide, wide + 192), a("b4", 192, 384), bias=col(11))
+            act(a("LIM", 3, 4), a("LIM", 4, 5), bias=a("LIM", 3, 4), scale=0.5)
+            ts(a("AI", 0, 1), a("LIM", 3, 4), 96.0 * (t + 1), Op.add)
             ts(a("AI", 1, 2), a("AI", 0, 1), 31, Op.bitwise_and)
             ts(a("LIM", 1, 2), a("AI", 1, 2), 8.0, Op.mult, a("LIM", 0, 1), Op.add)
         else:
-            kind[0] += 8
-        tt(a("X", 192 + wide, 192 + wide + 192), a("b4", 0, 192), a("FL", 384, 576), Op.mult)
-        tt(a("SM", 204, 216), tk, a("SM", 120, 132), Op.mult)
-        tt(a("SM", 228, 240), a("SM", 204, 216), a("SM", 96, 108), Op.min)
-        tt(a("SM", 216, 228), a("SM", 204, 216), a("SM", 228, 240), Op.subtract)
-        tt(a("SM", 204, 240), a("SM", 204, 240), a("II", 0, 36), Op.max)
-        cp(a("LX", 36 * t, 36 * t + 36), a("SM", 204, 240))
-        if t >= 1:
-            unmark(t - 1, 0 if last else 1)
-        if t >= 3:
-            unmark(t - 2, 2)
+            kind[0] += 6
+        mm([zero("b6", 12, 12)] + swap("b6", 12, 0, "TZ", 0, 16))
+        tt(sm(11), a("b6", 12, 24), sm(2), Op.mult)
+        tt(sm(12), sm(11), a("II", 0, 12), Op.add)
+        cp(a("LX", 12 * t, 12 * t + 12), sm(12))
+        if 1 <= t < NS - 2:
+            ts(a("LW"), a("EF"), 2047.5, Op.is_gt, MARK, Op.mult)
         elif t:
             kind[0] += 1
-        cp(ind(a("X", 0, 192 + wide), a("LX", 36 * t, 36 * t + 12)), z if last else a("ZM"))
+        if t >= 1:
+            numbers(t - 1, t, a("LW", old=1) if 2 <= t < NS - 1 else None)
+        if t >= 3:
+            numbers(t - 2, t, None)
+        elif t:
+            kind[0] += 1
+        numbers(t, t, None if last else a("CM"))
         if t == 0:
-            mm(pick("b7", 0, "B03", "GH", 0, 256))
-            act(a("HSK"), a("b7", 0, 256))
+            mm(pick("b7", 256, "B03", "GH", 0, 256))
+            act(a("HSK"), a("b7", 256, 512))
             mm([(a("b1", 0, 256), a("DUP", 0, 128), a("HSK"))])
             mm([(a("b1", 256, 512), a("DUP", 128, 256), a("HSK"))])
             act(a("HS2"), a("b1"))
             act(a("OWN"), a("OWN"), bias=col(6))
-            tt(a("TH2"), a("b1"), a("OWN"), Op.is_equal)
-            ts(a("TH2"), a("TH2"), -2048.0, Op.mult, 4096.0, Op.add)
+            tt(a("OWN"), a("b7", 256, 512), a("OWN"), Op.not_equal)
+            mm([(a("b7", 256, 512), a("IDF"), a("SBF")), (a("b7", 256, 512), a("I13F"), a("OWN"))])
+            act(a("SKT", 0, 256), a("b7", 256, 512))
+            mm(pick("b4", 0, "B5", "GH", 0, 256))
+            act(a("PK"), a("b4", 0, 256))
+            dma("y", a("JF", 0, 4096, p=row(5)), a("PK"))
         if t == 1:
             mm([(a("b7", 256, 384), band("B03", r), a("HT", 128 * r, 128 * r + 128)) for r in range(16)])
             cp(a("HL"), a("b7", 256, 384))
@@ -548,12 +600,12 @@ def rank_program(g, core, T, topo):
         dma("y", hbm(T.yx[:, 848 * h:848 * h + 848]), a("X", 192 + 848 * h, 192 + 848 * h + 848), None, 3000.0)
     act(a("G", 0, 1024), ind(a("JF"), a("HL", 0, 64)))
     cp(a("G", 1024, 2048), ind(a("JF"), a("HL", 64, 128)))
-    fin = MW * NS
-    dma("y", hbm(T.yz[:]), a("IN", fin, fin + 192))
-    mm([zero("b4", 0, 192)] + spread("b4", 0, "IN", fin + 192, 12))
+    fin = NR + MW * NS
+    dma("y", hbm(T.yz[:]), a("D", fin, fin + 192))
+    cp(rowz("YB", 0, 192), a("D", fin + 192, fin + 204))
     mm(pick("b1", 0, "B03", "G", 0, 128))
-    act(a("YB"), a("b4", 0, 192))
-    dma("s", hbm(T.yb[:]), a("YB", p=row(0)))
+    tr(a("YB", 0, 192), a("YB", 192, 384))
+    dma("s", hbm(T.yb[:]), a("YB", 0, 192, p=row(0)))
     cp(a("YJ"), a("b1", 0, 128))
     dma("y", hbm(T.yj[:]), a("YJ"))
 

@@ -15,8 +15,8 @@ _S = {
     "PI": (2, I32), "PJ": (2, I32), "COL": (24, F32), "IM": (144, F32), "IMP": (128, F32), "IG": (128, F32),
     "BD": (128, BF), "BDF": (128, F32), "ID": (128, BF), "IDS": (9 * 128, BF), "IFS": (4 * 128, F32),
     "ZR": (512, BF), "ONE": (512, BF), "BB": (144, BF), "BND": (13 * 144, BF), "MX": (9 * 128, BF), "W1": (128, BF),
-    "U": (2048, BF), "DG": (2048, BF), "RC": (192, BF),
-    "R16": (16, F32), "WD": (16, F32), "I16": (16, F32), "SW": (4 * 512, BF), "DUP": (256, F32), "IB": (12, BF),
+    "IO": (456, BF), "ZZ": (768, BF), "DG": (2048, BF), "RC": (192, BF),
+    "R16": (16, F32), "WD": (16, F32), "I16": (16, F32), "SW": (4 * 512, BF), "DUP": (256, F32), "IB": (16, BF), "CZ": (12, BF),
     "RO": (12, U16), "RS": (193, F32), "NI": (192, BF), "II": (36, F32), "CM": (192, BF),
     "T1": (60, F32), "T2": (12, I32), "PEI": (128, I32), "HEI": (128, I32), "DQ": (128, BF),
     "PEB": (128, BF), "HEB": (128, BF), "HIC": (128, BF), "LOC": (128, BF), "BXI": (192, I32), "BXB": (192, BF),
@@ -26,29 +26,34 @@ _S = {
     "YJ": (128, F32), "YB": (384, F32), "GE": (384, BF), "AF": (192, BF), "EF": (192, U16),
     "NZ": (384, BF), "TZ": (192, BF), "FZ": (192, BF),
     "NF": (192, BF), "CO": (60, U16), "DE": (384, BF), "EL": (24, U16), "BL": (24, U16), "NE": (384, BF), "SM": (192, F32),
-    "KK": (108, BF), "WH": (576, BF), "FL": (384, BF), "UU": (192, BF), "OD": (192, F32), "SK": (192, F32), "LW": (192, BF),
+    "KK": (120, BF), "WH": (576, BF), "FL": (384, BF), "UU": (192, BF), "OD": (192, F32), "SK": (192, F32), "LW": (192, BF),
     "M": (192, BF), "BX": (12, BF),
 }
 TWICE = ("NF", "CO", "DE", "EL", "BL", "NE", "SM", "KK", "WH", "FL", "UU", "OD", "SK", "LW", "M", "BX")
 SCRATCH = {k: ("sbuf", [128, w * (2 if k in TWICE else 1)], d) for k, (w, d) in _S.items()}
 for _b in range(8):
     SCRATCH["b%d" % _b] = ("psum", [128, 512], F32)
-SEMAPHORES = ["cv", "cs", "ct", "cg", "snt"] + ["arr%d" % i for i in range(NS)] + ["d%d" % i for i in range(48)]
-CHAINED = ("b1", "b2", "b3", "b5")
+SEMAPHORES = ["cv", "cs", "ct", "cg", "snt"] + ["ar%s%d" % (k, i) for k in "rz" for i in range(NS)] + ["d%d" % i for i in range(48)]
+CHAINED = ("b0", "b1", "b2", "b3", "b5")
 
 MARK = 192.0
 SPLIT, SOME, VOID = float(2 ** 19), float(2 ** 20), float(2 ** 22)
 IDS = {"NID": -1.0, "IDH": 0.5, "E01": -192.0, "I13": 8192.0, "I12": 4096.0, "IV": VOID,
        "I8": 256.0}
 IFS = {"IDF": 1.0, "NIF": -1.0, "IDQ": 1.0 / 8192, "I13F": 8192.0}
-MXS = ("LO", "LC", "LJ", "LE", "LN0", "LN1", "BD3", "BDN", "WC")
-BANDS = ("B0", "B1", "B2", "B03", "BAL", "BK", "BN", "BP", "BC", "BE", "BEP", "B5", "BM")
+MXS = ("LO", "LC", "LE", "LN0", "LN1", "BD3", "BDN", "WC")
+BANDS = ("B0", "B1", "B4", "B03", "BAL", "BK", "BN", "BP", "BC", "BE", "BEP", "B5", "BM")
 SCALES = (1.0, 16.0, 192.0, 1024.0)
 CY, GA, SCA, PE, LAT, DMA, REM = 1.04, 1.56, 3.8, 0.53, 90.0, 2300.0, 2500.0
-LOOKS = ((0, 2, 2), (2, 6, 2), (6, 11, 6), (11, 16, 11))
-ABS = (0, 3, 5, 8, 11, 13, 15, 16)
-HTS, GHV, DEV, LOV, HKV = 4, 3, 0, 0, 1
-TURNS, SIG, SEED = 1500, 1500.0, 1
+TURN = (0, 4, 12)
+FREE = (0, 6, 12)
+LOOKS = (0, 2, 4, 6, 9, 11, 14, 16)
+PICKS = (0, 2, 6, 11, 16)
+DIFF = (0, 2, 4, 6, 8, 10, 11, 13, 15, 16)
+ABS = (0, 2, 4, 6, 8, 11, 13, 15, 16)
+LOV = 0
+TURNS, SIG, SEED = 35000, 1500.0, 1
+WISH, HEAT = 800.0, 100.0
 PLAN = []
 
 
@@ -134,12 +139,38 @@ def rank_program(g, core, T, topo):
     def scan(out, d0, d1):
         put("v", [d0, d1], [out], lambda: g.vector.tensor_tensor_scan(out[0], d0[0], d1[0], 0.0, Op.add, Op.min), vcost(out, d1, 1))
 
-    def act(out, x, f=Fn.Identity, bias=0.0, scale=1.0, acc=None):
+    def sact(out, x, f=Fn.Identity, bias=0.0, scale=1.0, acc=None):
         if acc is None:
             put("s", [x, bias, scale], [out], lambda: g.scalar.activation(out[0], x[0], f, bias=val(bias), scale=val(scale)), vcost(out, x, 1))
         else:
             put("s", [x, bias, scale], [out, acc], lambda: g.scalar.activation(
                 out[0], x[0], f, bias=val(bias), scale=val(scale), accum_out=acc[0]), vcost(out, x, 1) + 20)
+
+    def either():
+        o = ops.pop()
+        ops[-1]["alt"] = {k: o[k] for k in ("e", "call", "c", "sem")}
+        ops[-1]["r"] = ops[-1]["r"] + o["r"]
+        kind[0] -= 1
+
+    def act(out, x, f=Fn.Identity, bias=0.0, scale=1.0):
+        sact(out, x, f, bias, scale)
+        if f == Fn.Identity and bias == 0.0 and scale == 1.0:
+            cp(out, x)
+        elif f == Fn.Identity:
+            ts(out, x, scale, Op.mult, bias, Op.add)
+        elif f == Fn.Relu and scale == 1.0:
+            ts(out, x, bias, Op.add, 0.0, Op.max)
+        else:
+            return
+        either()
+
+    def over(out, x, c):
+        sact(out, x, Fn.Sign, -c)
+        ts(out, x, c + 0.5, Op.is_gt)
+        either()
+
+    def gcp(out, x):
+        put("g", [x], [out], lambda: g.affine_select(out[0], x[0], [[0, x[3]]], Op.is_ge, 0.0, 0, 0), 170 + 2 * CY * out[3])
 
     def iota(out, pat, base=0, ch=0):
         if _S[out[1][0][0]][1] == I32:
@@ -176,9 +207,6 @@ def rank_program(g, core, T, topo):
     def pick(bank, lo, bnd, src, slo, n):
         return [(a(bank, lo, lo + n), band(bnd, r), a(src, slo + r, slo + 16 * n, 16)) for r in range(16)]
 
-    def spread(bank, lo, src, slo, n):
-        return [(a(bank, lo + r, lo + 16 * n, 16), a("U", 128 * r, 128 * r + 128), a(src, slo, slo + n)) for r in range(16)]
-
     def swap(bank, lo, w, src, slo, st=1):
         return [(a(bank, lo + be, lo + 12, 2), a("SW", 512 * w + 256 * be + 128 * ga, 512 * w + 256 * be + 128 * ga + 128),
                  a(src, slo + st * ga, slo + st * 11 + 1, 2 * st)) for be in range(2) for ga in range(2)]
@@ -186,8 +214,6 @@ def rank_program(g, core, T, topo):
     def lowest(eq, src, sc, cl):
         for c in range(12):
             ts(a(eq, 208 * c, 192 * c + 192), a(src, 16 * c, 192), a(sc, cl + c, cl + c + 1), Op.is_equal)
-            kind[0] -= 1
-        kind[0] += 1
 
         def off(cs):
             return [(a("b5", 16 * c + 16, 192), a("BD"), a(eq, 208 * c + 16, 192 * c + 192)) for c in cs]
@@ -224,7 +250,7 @@ def rank_program(g, core, T, topo):
         return a(name, lo + k, lo + 192, 16)
 
     ms(a("BXI"), 0)
-    ms(a("LMI"), 0)
+    iota(a("LMI"), [[0, 2]])
     dma("y", a("SBI"), hbm(T.sb[:]))
     dma("s", a("HEI"), hbm(T.he[:]))
     dma("y", a("BXI", p=row(0)), hbm(T.bx[:]))
@@ -232,9 +258,12 @@ def rank_program(g, core, T, topo):
     dma("y", a("LMI", p=row(0)), hbm(T.lim[:]))
     dma("y", a("D", NR, NR + 192), hbm(T.zs[:]))
     dma("y", a("X", 192, 192 + NV), hbm(T.xs[:]), None, 2500.0)
-    for h in range(2):
+    ms(a("EN", 0, NV), 0.0)
+    for h in range(3):
         dma("y", a("JF", 2048 * h, 2048 * h + 2048), a("X", 192, 192 + NV), None, 2500.0)
 
+    iota(a("ZR"), [[0, 512]])
+    iota(a("ONE"), [[0, 512]], 1)
     iota(a("PI", 0, 1), [[0, 1]], 0, 1)
     iota(a("IM"), [[1, 144]])
     iota(a("IG"), [[1, 8], [0, 16]])
@@ -242,39 +271,38 @@ def rank_program(g, core, T, topo):
     iota(a("II"), [[0, 3], [16, 12]])
     iota(a("W1"), [[0, 8], [16, 16]])
     iota(a("NI"), [[1, 192]])
+    iota(a("IO"), [[1, 456]])
     iota(a("SIO"), [[1, 2048]])
     iota(a("OWN"), [[1, 256]])
     iota(a("MA", 0, 256), [[0, 16], [1, 16]])
     iota(a("MA", 256, 512), [[1, 16], [0, 16]])
     iota(a("G", NR, NR + 7 * MW), [[0, 7 * MW]], 1)
-    ms(a("ZR"), 0.0)
-    ms(a("JF", 4096, 6144), 0.0)
-    fill(a("ONE"), 1.0)
-    act(a("EN", 0, NV), a("JF", 4096, 6144))
     ts(a("PJ", 0, 1), a("PI", 0, 1), 15, Op.bitwise_and)
     ts(a("PJ", 1, 2), a("PI", 0, 1), 4, Op.logical_shift_right)
     cp(a("COL", 0, 2), a("PJ"))
     ts(a("PI", 1, 2), a("PJ", 1, 2), 1, Op.bitwise_and)
     cp(col(3), a("PI", 1, 2))
-    ts(col(2), col(3), -1.0, Op.mult, 1.0, Op.add)
-    ts(col(4), col(1), 16.0, Op.mult, 15.0, Op.add)
-    ts(col(10), col(0), 128.0, Op.mult)
-    ts(a("HIC"), a("IG"), 0.0, Op.mult, col(10), Op.add)
-    cp(a("LOC"), a("IM", 0, 128))
+    act(col(2), col(3), bias=1.0, scale=-1.0)
+    act(col(4), col(1), bias=15.0, scale=16.0)
+    act(col(10), col(0), scale=128.0)
+    fill(a("HIC"), col(10))
+    iota(a("LOC"), [[1, 128]])
     dma("y", a("JF", 4096, 6144, p=row(0)), a("HIC"))
     dma("y", a("JF", 4096, 6144, p=row(2)), a("LOC"))
+    for j in (1, 3, 4):
+        dma("y", a("JF", 4096, 6144, p=row(j)), a("ZR", 0, 128))
     ts(a("R16"), a("IM", 0, 16), col(0), Op.is_equal)
-    ts(col(11), unit(2), 2.0, Op.mult)
+    act(col(11), unit(2), scale=2.0)
     ts(col(5), col(0), 3.5, Op.is_lt)
-    ts(col(6), col(0), 256.0, Op.mult)
-    ts(col(7), unit(4), 8192.0, Op.mult, col(5), Op.add)
+    act(col(6), col(0), scale=256.0)
+    act(col(7), unit(4), bias=col(5), scale=8192.0)
     ts(a("BD"), a("IG"), col(1), Op.is_equal)
     act(a("BDF"), a("BD"))
     ts(a("ID"), a("IMP"), 0.0, Op.is_equal)
     for nm, w in IFS.items():
         act(a(nm), a("ID"), scale=w)
     ts(a("BB"), a("IM"), col(4), Op.is_equal)
-    for nm, w in (("B2", unit(2)), ("B0", unit(0)), ("B03", col(5)), ("B1", unit(1)), ("BAL", 512.0), ("BK", col(6)), ("BN", -8192.0),
+    for nm, w in (("B4", unit(4)), ("B0", unit(0)), ("B03", col(5)), ("B1", unit(1)), ("BAL", 512.0), ("BK", col(6)), ("BN", -8192.0),
                   ("BP", 8192.0), ("BEP", col(7)), ("B5", unit(5))):
         act(a(nm), a("BB"), scale=w)
     for be in range(2):
@@ -282,63 +310,58 @@ def rank_program(g, core, T, topo):
             ts(a("SW", 256 * be + 128 * ga, 256 * be + 128 * ga + 128), a("IMP"), 16.0 * (ga - be), Op.is_equal, col(2 + be), Op.mult)
         msum(a("DUP", 128 * be, 128 * be + 128), [("ID", a("SW", 256 * be + 128 * ga, 256 * be + 128 * ga + 128)) for ga in range(2)])
     for w in range(1, 4):
-        ts(a("SW", 512 * w, 512 * w + 512), a("SW", 0, 512), SCALES[w], Op.mult)
-    for r in range(16):
-        ts(a("U", 128 * r, 128 * r + 128), a("BD"), unit(r), Op.mult)
-        kind[0] -= 1
-    kind[0] += 1
+        act(a("SW", 512 * w, 512 * w + 512), a("SW", 0, 512), scale=SCALES[w])
     cp(a("SBF"), a("SBI"))
     cp(a("HEB"), a("HEI"))
     cp(a("PEB"), a("PEI"))
     tt(a("DQ"), a("HEI"), a("PEI"), Op.subtract)
-    for j, x in ((1, a("HEB")), (0, a("PEB")), (3, a("DQ")), (2, a("ONE", 0, 128))):
+    for j, x in ((1, a("HEB")), (0, a("PEB")), (3, a("DQ")), (2, a("ONE", 0, 128)), (4, a("HIC")), (5, a("LOC"))):
         dma("y", a("EN", 0, NV, p=row(j)), x)
     mm([(a("b1", 0, 256), a("DUP", 0, 128), a("SBF"))])
     mm([(a("b1", 256, 512), a("DUP", 128, 256), a("SBF"))])
     act(a("SB2"), a("b1"))
     cp(a("BXB"), a("BXI"))
     tr(a("TZ"), a("BXB"))
-    cp(a("D", NR + 192, NR + 204), rowz("TZ", 0))
-    ms(a("D", NR + 204, NR + 216), 0.0)
-    ts(a("II"), a("II"), col(0), Op.add)
-    cp(a("IB"), a("II", 0, 12))
-    ts(a("II", 12, 24), a("II", 12, 24), 256.0, Op.add)
-    ts(a("II", 24, 36), a("II", 24, 36), -192.0, Op.add)
-    ts(a("T1", 0, 12), a("II", 0, 12), -5.5, Op.add, 1.0 / 12, Op.mult)
-    cp(a("T2"), a("T1", 0, 12))
+    iota(a("CZ"), [[0, 6], [-256, 2]], 256)
+    act(col(14), col(2), scale=256.0)
+    tt(a("D", NR + 192, NR + 204), rowz("TZ", 0), a("CZ"), Op.subtract)
+    iota(a("D", NR + 204, NR + 216), [[0, 12]])
+    act(a("II"), a("II"), bias=col(0))
+    act(a("IB", 0, 12), a("II", 0, 12))
+    act(a("II", 12, 24), a("II", 12, 24), bias=256.0)
+    act(a("II", 24, 36), a("II", 24, 36), bias=-192.0)
+    ts(a("T2"), a("II", 0, 12), -5.5, Op.add, 1.0 / 12, Op.mult)
     ts(a("T1", 48, 60), a("T2"), -191.0, Op.mult)
-    ts(a("T1", 16, 28), a("II", 0, 12), 16.0, Op.mult)
+    act(a("T1", 16, 28), a("II", 0, 12), scale=16.0)
     tt(a("T1", 32, 44), a("T1", 16, 28), a("T1", 48, 60), Op.add)
     cp(a("RO"), a("T1", 32, 44))
     ts(a("WD"), a("IM", 0, 16), col(0), Op.is_gt)
-    ts(a("I16"), a("R16"), -256.0, Op.mult)
+    act(a("I16"), a("R16"), scale=-256.0)
     tt(a("WD"), a("WD"), a("I16"), Op.add)
     for r in range(16):
-        ts(a("DG", 128 * r, 128 * r + 128), a("BD"), a("WD", r, r + 1), Op.mult)
-        kind[0] -= 1
-    kind[0] += 1
+        act(a("DG", 128 * r, 128 * r + 128), a("BD"), scale=a("WD", r, r + 1))
     for nm, w in IDS.items():
         act(a(nm), a("ID"), scale=w)
     act(a("BD3"), a("BD"), scale=col(5))
     act(a("BDN"), a("BD"), scale=-4096.0)
-    fill(a("RS"), 0.0)
+    iota(a("RS"), [[0, 193]])
     ms(a("RS", 1, 193, 16), float(2 ** 27))
-    ms(a("TM", 0, 1), 0.0)
-    fill(a("CH", 0, 448), 0.0)
-    ms(a("CH", 448, 456), 1.0)
-    fill(a("SKT", 256, 456), 0.0)
-    fill(a("YB", 192, 384), 0.0)
-    fill(a("CM"), MARK)
+    iota(a("TM", 0, 1), [[0, 1]])
+    iota(a("CH", 0, 448), [[0, 448]])
+    iota(a("CH", 448, 456), [[0, 8]], 1)
+    iota(a("SKT", 256, 456), [[0, 200]])
+    iota(a("YB", 192, 384), [[0, 192]])
+    iota(a("CM"), [[0, 192]], int(MARK))
     ts(a("MA"), a("MA"), col(0), Op.is_equal)
     mm([(a("b7", 256, 512), a("ID"), a("MA", 256 * j, 256 * j + 256)) for j in range(2)])
     act(a("MT", 1, 257), a("b7", 256, 512), bias=1.0)
-    ms(a("MT", 0, 1), 0.0)
-    ms(a("MT", 257, 272), 1.0)
+    iota(a("MT", 0, 1), [[0, 1]])
+    iota(a("MT", 257, 272), [[0, 15]], 1)
     cp(a("LMF"), a("LMI"))
     mm([(a("b6", 16, 18), a("BDF"), a("LMF"))])
-    ts(a("LIM", 0, 1), a("b6", 16, 17), -73728.5, Op.add)
-    cp(a("LIM", 1, 2), a("LIM", 0, 1))
-    ms(a("LIM", 3, 4), 0.0)
+    act(a("LIM", 1, 2), a("b6", 16, 17), bias=-73728.5)
+    act(a("LIM", 3, 4), a("b6", 16, 17), bias=160 * 256 - 73728.5)
+    act(a("LIM", 5, 6), a("LIM", 3, 4), bias=159.5 + 1.0 / 64, scale=-1.0 / 256)
     ts(a("LIM", 2, 3), a("b6", 17, 18), 1008.0, Op.min, -1.0, Op.mult)
     ts(a("AI", 2, 3), a("LIM", 2, 3), 1023.0, Op.add)
     ts(a("AI", 3, 4), a("AI", 2, 3), 5, Op.logical_shift_right)
@@ -346,9 +369,9 @@ def rank_program(g, core, T, topo):
     ts(col(12), a("AI", 3, 4), unit(0), Op.mult, unit(2), Op.add)
     ts(col(12), a("AI", 4, 5), unit(1), Op.mult, col(12), Op.add)
     fill(a("RC"), col(12))
-    ts(col(13), unit(0), 16384.0, Op.mult)
-    ts(col(13), unit(1), 512.0, Op.mult, col(13), Op.add)
-    ts(a("W1"), a("W1"), unit(2), Op.mult, col(13), Op.add)
+    act(col(13), unit(0), scale=16384.0)
+    act(col(13), unit(1), bias=col(13), scale=512.0)
+    act(a("W1"), a("W1"), bias=col(13), scale=unit(2))
     tt(a("WC"), a("W1"), a("BD"), Op.mult)
     act(a("SBH"), a("SBF"))
     dma("y", a("JF", 0, 4096, p=row(2)), a("SBH"))
@@ -363,8 +386,7 @@ def rank_program(g, core, T, topo):
     act(a("BM"), a("B0"), scale=-1.0)
     msum(a("LO"), [("ID", band("BN", 0)), ("ID", band("BN", 1)), ("ID", band("BK", 2)), ("ID", band("BP", 3))])
     msum(a("LC"), [("ID", band("BC", 0)), ("ID", band("BE", 3))])
-    msum(a("LJ"), [("ID", band("B0", 0)), ("ID", band("B2", 1))])
-    msum(a("LE"), [("ID", band("B1", 3)), ("ID", band("B0", 5))])
+    msum(a("LE"), [("ID", band("B1", 3)), ("ID", band("B0", 5)), ("ID", band("B4", 0)), ("ID", band("B5", 1))])
     msum(a("LN0"), [("ID", band("B5", 0)), ("NID", band("B5", 3))])
     act(a("LN1"), band("B5", 3))
     cp(a("SBU"), a("SBI"))
@@ -373,61 +395,58 @@ def rank_program(g, core, T, topo):
         bk = ("b1", "b7")[h % 2]
         tt(a("OH", 512 * h, 512 * h + 512), ind(a("SBF"), a("HEL", 32 * h, 32 * h + 32)), a("SIO", 512 * h, 512 * h + 512), Op.is_equal)
         mm([(a(bk), a("LC"), a("ONE")), (a(bk), a("LE"), a("EN", 512 * h, 512 * h + 512)),
-            (a(bk), a("LJ"), a("JF", 4096 + 512 * h, 4608 + 512 * h)), (a(bk), a("LO"), a("OH", 512 * h, 512 * h + 512))])
-        if h < HTS:
-            act(a("HT", 512 * h, 512 * h + 512), a(bk), Fn.Relu)
-        else:
-            ts(a("HT", 512 * h, 512 * h + 512), a(bk), 0.0, Op.max)
+            (a(bk), a("LO"), a("OH", 512 * h, 512 * h + 512))])
+        act(a("HT", 512 * h, 512 * h + 512), a(bk), Fn.Relu)
     for h in range(8):
-        (cp if h < GHV else act)(a("GH", 512 * h, 512 * h + 512), ind(a("HT"), a("SBU", 32 * h, 32 * h + 32)))
+        act(a("GH", 512 * h, 512 * h + 512), ind(a("HT"), a("SBU", 32 * h, 32 * h + 32)))
 
-    def numbers(t, upto, plus):
-        out = ind(a("X", 0, 192 + NV + NT * upto), a("LX", 12 * t, 12 * t + 12))
-        z = a("D", NR + MW * t, NR + MW * t + 192)
-        if plus is None:
-            cp(out, z)
-        else:
-            tt(out, z, plus, Op.add)
+    def numbers(t, upto, plus, cut):
+        for j0, j1 in zip(cut, cut[1:]):
+            out = ind(a("X", 0, 192 + NV + NT * upto), a("LX", 12 * t + j0, 12 * t + j1))
+            z = a("D", NR + MW * t + 16 * j0, NR + MW * t + 16 * j1)
+            if plus is None:
+                cp(out, z)
+            else:
+                tt(out, z, a(plus, 16 * j0, 16 * j1, old=1), Op.add)
 
     first = 0
+    begin = []
     for t in range(NS):
         par[0] = t % 2
+        last = t == NS - 1
+        begin.append(len(ops))
         if t == 1:
             first = kind[0]
-        if t > 1:
+        if 1 < t and not last:
             kind[0] = first
-        last = t == NS - 1
         zo = NR + MW * t
         z = a("D", zo, zo + 192)
         ao = zo + 192
-        box = a("D", ao, ao + 12)
+        box = kk(9)
         rest = a("D", ao + 12, ao + 24)
         wide = NV + NT * t
-        cp(a("LM", 0, 12, 2), a("D", ao, ao + 12, 2))
-        ts(a("LM", 1, 12, 2), a("D", ao + 1, ao + 12, 2), 256.0, Op.add)
-        (cp if HKV else act)(a("HK"), ind(a("HS2" if t else "SB2"), a("LM")))
+        ts(a("LM"), a("D", ao, ao + 12), 256.0, Op.add)
+        tt(box, a("D", ao, ao + 12), a("CZ"), Op.add)
+        act(a("HK"), ind(a("HS2" if t else "SB2"), a("LM")))
         tr(a("HR"), a("HK"))
-        cp(a("L1"), ind(a("HR"), a("RO")))
+        for j0, j1 in zip(TURN, TURN[1:]):
+            cp(a("L1", 16 * j0, 16 * j1), ind(a("HR"), a("RO", j0, j1)))
         banks = [("b0", 0), ("b1", 0), ("b6", 64), ("b7", 0)]
-        for q, (k0, k1, kv) in enumerate(LOOKS if t else ()):
-            if kv > k0:
-                cp(a("G", 192 * k0, 192 * kv), ind(a("JF"), a("L1", 12 * k0, 12 * kv)))
-            if kv < k1:
-                act(a("G", 192 * kv, 192 * k1), ind(a("JF"), a("L1", 12 * kv, 12 * k1)))
+        for k0, k1 in zip(LOOKS, LOOKS[1:] if t else ()):
+            act(a("G", 192 * k0, 192 * k1), ind(a("JF"), a("L1", 12 * k0, 12 * k1)))
+        for (bk, lo), k0, k1 in zip(banks, PICKS, PICKS[1:] if t else ()):
             w = 12 * (k1 - k0)
-            bk, lo = banks[q]
             mm(pick(bk, lo, "B03", "G", 192 * k0, w))
             cp(a("CL", 12 * k0, 12 * k1), a(bk, lo, lo + w))
         if t:
-            ts(kk(6), rest, 0.5, Op.is_gt)
-            ts(rest, rest, -1.0, Op.add, 0.0, Op.max)
-        mm([zero("b6", 32, 12)] + swap("b6", 32, 0, "D", ao) + (swap("b6", 32, 3, "KK", 72 + 108 * 0) if t else []))
-        ts(a("BX"), a("b6", 32, 44), 448.0, Op.min)
+            over(kk(6), rest, 0.0)
+            act(rest, rest, Fn.Relu, bias=-1.0)
+        mm([zero("b6", 32, 12)] + swap("b6", 32, 0, "D", ao) + (swap("b6", 32, 3, "KK", 72) if t else []))
+        ts(a("BX"), a("b6", 32, 44), col(14), Op.add, 448.0, Op.min)
         cp(a("BL", 0, 12), a("BX"))
-        mm([zero("b4", 0, 192)] + spread("b4", 0, "BX", 0, 12))
-        act(a("AF"), a("b4", 0, 192))
+        act(a("AF"), ind(a("IO"), a("BL", 0, 12)))
         lowest("ES", "AF", "BX", 0)
-        act(a("NF"), a("b5", 0, 192), Fn.Sign, bias=256.0)
+        over(a("NF"), a("b5", 0, 192), -256.0)
         tr(a("FZ"), a("NF"))
         mm([(a("b7", 192, 204), a("ID"), a("BX"))] + swap("b7", 192, 3, "FZ", 0, 16))
         tt(sm(1), a("b7", 192, 204), a("II", 12, 24), Op.min)
@@ -438,14 +457,15 @@ def rank_program(g, core, T, topo):
         mm([(key, a("WC"), a("RC"))], True, False)
         if t:
             act(a("OD"), ind(a("CH"), a("BL", 0, 12)))
-            act(a("VF"), a("OD"), Fn.Sign)
+            over(a("VF"), a("OD"), 0.0)
             mm([(key, a("IDQ"), a("SK"))], False, False)
             mm([(key, a("IV"), a("VF"))], False, False)
         cl = "CL" if t else "L1"
-        for k in range(16):
-            tt(a("D", 192 * k, 192 * k + 192), ind(a("X", 192, 192 + wide), a(cl, 12 * k, 12 * k + 12)), z, Op.subtract)
-            kind[0] -= 1
-        kind[0] += 1
+        for j in range(max(k1 - k0 for k0, k1 in zip(DIFF, DIFF[1:]))):
+            gcp(a("ZZ", 192 * j, 192 * j + 192), z)
+        for k0, k1 in zip(DIFF, DIFF[1:]):
+            tt(a("D", 192 * k0, 192 * k1), ind(a("X", 192, 192 + wide), a(cl, 12 * k0, 12 * k1)),
+               a("ZZ", 0, 192 * (k1 - k0)) if k1 - k0 > 1 else z, Op.subtract)
         for k0, k1 in zip(ABS, ABS[1:]):
             act(a("AB", 192 * k0, 192 * k1), a("D", 192 * k0, 192 * k1), Fn.Abs)
             mm([(key, band("BAL", k), a("AB", 192 * k, 192 * k + 192)) for k in range(k0, k1)], False, k1 == 16)
@@ -455,7 +475,7 @@ def rank_program(g, core, T, topo):
         ts(a32(0), m1, SOME + 256 + 18 * t, Op.min)
         ts(a32(2), a32(0), 1, Op.logical_shift_right, 255, Op.bitwise_and)
         ts(kk(0), a32(2), 0.125, Op.mult)
-        mm([(a("b7", 64, 76), a("ID"), a("IB"))] + swap("b7", 64, 2, "KK", 0))
+        mm([(a("b7", 64, 76), a("ID"), a("IB", 0, 12))] + swap("b7", 64, 2, "KK", 0))
         cp(co(0), a("b7", 64, 76))
         ts(kk(2), m1, SPLIT, Op.is_ge, -32768.0, Op.mult)
         tt(a("TM", 1, 192), a("b2", 0, 191), a("KR", 1, 192), Op.max)
@@ -463,7 +483,7 @@ def rank_program(g, core, T, topo):
         ts(a32(1), m2, SOME + 256, Op.min)
         ts(a32(3), a32(1), 1, Op.logical_shift_right, 255, Op.bitwise_and)
         ts(kk(1), a32(3), 0.125, Op.mult)
-        mm([(a("b7", 76, 88), a("ID"), a("IB"))] + swap("b7", 76, 2, "KK", 12))
+        mm([(a("b7", 76, 88), a("ID"), a("IB", 0, 12))] + swap("b7", 76, 2, "KK", 12))
         cp(co(1), a("b7", 76, 88))
         for j in range(2):
             if t:
@@ -478,8 +498,8 @@ def rank_program(g, core, T, topo):
         mm([(a("b4", 192, 384), a("BD3"), a("GE", 0, 192))])
         mm(pick("b6", 0, "BEP", "GE", 0, 12))
         de, df = a("DE", 0, 192), a("DE", 192, 384)
-        (cp if DEV & 1 else act)(de, ind(a("D", 0, zo + 192), co(0)))
-        (cp if DEV & 2 else act)(df, ind(a("D", 0, zo + 192), co(1)))
+        act(de, ind(a("D", 0, zo + 192), co(0)))
+        tt(df, ind(a("D", 0, zo + 192), co(1)), de, Op.subtract)
         ts(a("EL", 0, 12), e, float(wide - 1), Op.min)
         tt(sm(2), e, a("II", 24, 36), Op.subtract)
         if not t:
@@ -489,8 +509,7 @@ def rank_program(g, core, T, topo):
             act(a("NE", 192 * j, 192 * j + 192), ind(a("EN", 0, wide), a("EL", 12 * j, 12 * j + 12)))
         act(a("WH", 0, 192), de, Fn.Abs)
         act(a("WH", 192, 384), de, bias=191.75, scale=0.5)
-        mm([(a("b0", 64, 256), a("ID"), de), (a("b0", 64, 256), a("NID"), df)])
-        act(a("WH", 384, 576), a("b0", 64, 256), Fn.Abs)
+        act(a("WH", 384, 576), df, Fn.Abs)
         tr(a("NZ", 0, 192 * ne), a("NE", 0, 192 * ne))
         tt(sm(4), rowz("NZ", 0), box, Op.is_equal)
         tt(sm(3), rowz("NZ", 0), box, Op.subtract)
@@ -498,9 +517,23 @@ def rank_program(g, core, T, topo):
         tt(sm(6), sm(5), sm(3), Op.add)
         mm([(a("b2", 192, 384), a(w), x) for (w, x) in (
             ("ID", z), ("E01", a("ONE", 0, 192)), ("ID", a("WH", 192, 384)), ("NID", a("WH", 0, 192)))])
+        if t:
+            ts(a32(4, 2), a32(0, 2), 1, Op.bitwise_and)
+            tt(kk(3), a32(4), a32(5), Op.add)
+        else:
+            for j in range(2):
+                tt(kk(3 + j), rowz("NZ", 1, 192 * j), box, Op.not_equal)
+        code = a("b0", 88, 100)
+        mm([(code, a("ID"), a("ONE", 0, 12))] + swap("b0", 88, 3, "FZ", 0, 16), True, False)
+        mm(swap("b0", 88, 0, "KK", 0) + swap("b0", 88, 0, "KK", 24), False, False)
+        mm(swap("b0", 88, 1, "KK", 12) + swap("b0", 88, 3, "KK", 36) + ([] if t else swap("b0", 88, 3, "KK", 48)), False, True)
+        ts(co(4), code, 257.0, Op.min)
+        act(a("M"), ind(a("MT"), co(4)))
         cp(a("EF"), a("b4", 192, 384))
         lowest("EQ", "EF", "b6", 0)
-        act(a("FL", 0, 192), a("b5", 0, 192), Fn.Relu, bias=-255.0, scale=-1.0)
+        sact(a("FL", 0, 192), a("b5", 0, 192), Fn.Relu, bias=-255.0, scale=-1.0)
+        ts(a("FL", 0, 192), a("b5", 0, 192), -255.5, Op.is_lt)
+        either()
         tr(a("TZ"), a("FL", 0, 192))
         tt(a("UU"), a("b2", 192, 384), a("FL", 0, 192), Op.mult)
         mm([(a("b0", 256, 448), a("ID"), a("WH", 0, 192)), (a("b0", 256, 448), a("ID"), a("UU"))])
@@ -511,23 +544,13 @@ def rank_program(g, core, T, topo):
         dst = T.cores[(rank + 1) % N if not last else (rank - t) % N]
         rid, pid = topo.addr(dst, core)
         eng = topo.engines(core, dst)[:8]
-        src, land, arr = a("OUT", MW * t, MW * t + MW), a("D", zo + MW, zo + 2 * MW), "arr%d" % t
-        put("g", [src], [land], lambda src=src, land=land, arr=arr, pid=pid, rid=rid, eng=eng: g.remote_dma(
-            land[0], src[0], T.sem[arr], T.sem.snt, pid, rid, sum(1 << e for e in eng)), 500.0, arr, len(eng), lat=REM - 500)
-        if t:
-            ts(a32(4, 2), a32(0, 2), 1, Op.bitwise_and)
-            tt(kk(3), a32(4), a32(5), Op.add)
-        else:
-            for j in range(2):
-                tt(kk(3 + j), rowz("NZ", 1, 192 * j), box, Op.not_equal)
-        code = a("b7", 88, 100)
-        mm([(code, a("ID"), a("ONE", 0, 12))] + swap("b7", 88, 0, "KK", 0) + swap("b7", 88, 1, "KK", 12) + swap("b7", 88, 0, "KK", 24)
-           + swap("b7", 88, 3, "FZ", 0, 16) + swap("b7", 88, 3, "KK", 36) + ([] if t else swap("b7", 88, 3, "KK", 48)))
-        ts(co(4), code, 257.0, Op.min)
-        act(a("M"), ind(a("MT"), co(4)))
+        for lo, hi, arr in ((192, MW, "arr%d" % t), (0, 192, "arz%d" % t)):
+            src, land = a("OUT", MW * t + lo, MW * t + hi), a("D", zo + MW + lo, zo + MW + hi)
+            put("g", [src], [land], lambda src=src, land=land, arr=arr, pid=pid, rid=rid, eng=eng: g.remote_dma(
+                land[0], src[0], T.sem[arr], T.sem.snt, pid, rid, sum(1 << e for e in eng)), 500.0, arr, len(eng), lat=REM - 500)
         sg = a("FL", 192, 384)
         mm([(a("b6", 256, 448), a("BD"), a("WH", 384, 576)), (a("b6", 256, 448), a("BDN"), a("M"))])
-        act(sg, a("b6", 256, 448), Fn.Sign, bias=a("LIM", 1, 2), scale=-1.0, acc=a("LIM", 4, 5))
+        sact(sg, a("b6", 256, 448), Fn.Sign, bias=a("LIM", 1, 2), scale=-1.0, acc=a("LIM", 4, 5))
         mm([(a("b1", 256, 448), a("I13"), a("M"))], False, False)
         mm([(a("b1", 256, 448), a("I12"), sg)], False, True)
         act(a("Q1"), a("b1", 256, 448), Fn.Relu, bias=float(wide - 20480))
@@ -548,7 +571,7 @@ def rank_program(g, core, T, topo):
             act(a("CHL"), a("b3", 256, 512))
         dma("y", a("JF", 0, 4096, p=row(1)), a("CHL"), "d47")
         mm([(a("b4", 0, 192), a(w), x) for (w, x) in (
-            ("ID", z), ("IDH", de), ("IDH", df), ("IDH", a("WH", 384, 576)), ("I8", sg))])
+            ("ID", z), ("ID", de), ("IDH", df), ("IDH", a("WH", 384, 576)), ("I8", sg))])
         act(a("X", 192 + wide, 192 + wide + 192), a("b4", 0, 192), Fn.Relu, bias=-256.0)
         if not last:
             if t:
@@ -557,12 +580,11 @@ def rank_program(g, core, T, topo):
                 mm([(a("b4", 192, 384), w, a("NE", 192 * j, 192 * j + 192))
                     for (w, j) in ((band("B0", 0), 0), (band("BM", 3), 0), (band("B0", 3), 1))])
             act(a("EN", wide, wide + 192), a("b4", 192, 384), bias=col(11))
-            act(a("LIM", 3, 4), a("LIM", 4, 5), bias=a("LIM", 3, 4), scale=0.5)
-            ts(a("AI", 0, 1), a("LIM", 3, 4), 96.0 * (t + 1), Op.add)
-            ts(a("AI", 1, 2), a("AI", 0, 1), 31, Op.bitwise_and)
-            ts(a("LIM", 1, 2), a("AI", 1, 2), 8.0, Op.mult, a("LIM", 0, 1), Op.add)
+            act(a("LIM", 3, 4), a("LIM", 4, 5), bias=a("LIM", 3, 4), scale=4.0)
+            act(a("IB", 12, 13), a("LIM", 3, 4), bias=a("LIM", 5, 6), scale=1.0 / 256)
+            act(a("LIM", 1, 2), a("IB", 12, 13), bias=a("LIM", 3, 4), scale=-256.0)
         else:
-            kind[0] += 6
+            kind[0] += 5
         mm([zero("b6", 12, 12)] + swap("b6", 12, 0, "TZ", 0, 16))
         tt(sm(11), a("b6", 12, 24), sm(2), Op.mult)
         tt(sm(12), sm(11), a("II", 0, 12), Op.add)
@@ -572,12 +594,12 @@ def rank_program(g, core, T, topo):
         elif t:
             kind[0] += 1
         if t >= 1:
-            numbers(t - 1, t, a("LW", old=1) if 2 <= t < NS - 1 else None)
+            numbers(t - 1, t, "LW" if 2 <= t < NS - 1 else None, FREE)
         if t >= 3:
-            numbers(t - 2, t, None)
+            numbers(t - 2, t, None, FREE)
         elif t:
-            kind[0] += 1
-        numbers(t, t, None if last else a("CM"))
+            kind[0] += len(FREE) - 1
+        numbers(t, t, None if last else "CM", (0, 12))
         if t == 0:
             mm(pick("b7", 256, "B03", "GH", 0, 256))
             act(a("HSK"), a("b7", 256, 512))
@@ -591,18 +613,16 @@ def rank_program(g, core, T, topo):
             mm(pick("b4", 0, "B5", "GH", 0, 256))
             act(a("PK"), a("b4", 0, 256))
             dma("y", a("JF", 0, 4096, p=row(5)), a("PK"))
-        if t == 1:
-            mm([(a("b7", 256, 384), band("B03", r), a("HT", 128 * r, 128 * r + 128)) for r in range(16)])
-            cp(a("HL"), a("b7", 256, 384))
 
-    kind[0] += 2
+    mm([(a("b7", 256, 384), band("B03", r), a("HT", 128 * r, 128 * r + 128)) for r in range(16)])
+    cp(a("HL"), a("b7", 256, 384))
     for h in range(4):
         dma("y", hbm(T.yx[:, 848 * h:848 * h + 848]), a("X", 192 + 848 * h, 192 + 848 * h + 848), None, 3000.0)
     act(a("G", 0, 1024), ind(a("JF"), a("HL", 0, 64)))
     cp(a("G", 1024, 2048), ind(a("JF"), a("HL", 64, 128)))
     fin = NR + MW * NS
     dma("y", hbm(T.yz[:]), a("D", fin, fin + 192))
-    cp(rowz("YB", 0, 192), a("D", fin + 192, fin + 204))
+    tt(rowz("YB", 0, 192), a("D", fin + 192, fin + 204), a("CZ"), Op.add)
     mm(pick("b1", 0, "B03", "G", 0, 128))
     tr(a("YB", 0, 192), a("YB", 192, 384))
     dma("s", hbm(T.yb[:]), a("YB", 0, 192, p=row(0)))
@@ -629,81 +649,205 @@ def rank_program(g, core, T, topo):
             seen.setdefault(r[0], []).append((r, False, i))
         o["bk"] = sorted(set(r[0] for r in o["r"] + o["w"] if r[0][0] == "b"))
     n = len(ops)
-    kids = [[] for o in ops]
-    for i, o in enumerate(ops):
-        for j in sorted(o["dep"]):
-            kids[j].append(i)
-    full = [o["c"] + o["lat"] for o in ops]
-    keys = [[(o["e"], 0.0)] + [(b, LAT + 70.0) for b in o["bk"]] for o in ops]
     deps = [sorted(o["dep"]) for o in ops]
+    above = []
+    for i in range(n):
+        m = 0
+        for j in deps[i]:
+            m |= above[j]
+        keep = [j for j in deps[i] if not m >> j & 1]
+        for j in deps[i]:
+            m |= 1 << j
+        above.append(0 if ops[i]["sem"][:2] == "ar" else m)
+        deps[i] = keep
+    kids = [[] for o in ops]
+    for i in range(n):
+        for j in deps[i]:
+            kids[j].append(i)
+    kd = [o["k"] for o in ops]
+    full = [o["c"] + o["lat"] + LAT for o in ops]
+    tail = [o["lat"] + LAT for o in ops]
+    forms = [[(o["e"], o["c"])] + ([(o["alt"]["e"], o["alt"]["c"])] if "alt" in o else []) for o in ops]
+    banks = [o["bk"] for o in ops]
+    cont = [o["cont"] for o in ops]
+    pad = LAT + 70.0
 
-    def ways(lean, kinds):
-        way = [0.0] * n
-        for i in range(n - 1, -1, -1):
-            way[i] = full[i] + lean[ops[i]["k"]] + max([way[k] + LAT for k in kids[i]], default=0.0)
-        return {i: way[i] + lean[kinds + ops[i]["k"]] for i in range(n)}
+    kinds = max(kd) + 1
+    way = [0.0] * n
 
-    def lay(rev, prio):
-        pre, post = (kids, deps) if rev else (deps, kids)
-        left = [len(p) for p in pre]
+    def lay(lean, lo, hi, goal, bound):
+        for i in range(hi - 1, lo - 1, -1):
+            w = 0.0
+            for k in kids[i]:
+                if way[k] > w:
+                    w = way[k]
+            way[i] = w + full[i] + lean[kd[i]]
+        order = sorted(range(lo, hi), key=lambda i: -way[i] - lean[kinds + kd[i]])
+        left = [0] * n
+        for i in range(lo, hi):
+            for k in kids[i]:
+                left[k] += 1
         at = [0.0] * n
         st = [0.0] * n
-        busy = {}
-        cand = set(i for i in range(n) if left[i] == 0)
-        while cand:
-            i = max(cand, key=prio.get)
-            cand.remove(i)
-            o = ops[i]
-            s0, c, e = at[i] + (o["lat"] if rev else 0.0), o["c"], o["e"]
-            moved = True
-            while moved:
-                moved = False
-                for (key, pad) in keys[i]:
-                    lst = busy.setdefault(key, [])
+        form = [0] * n
+        busy = {k: [] for k in list(Q) + ["b%d" % b for b in range(8)]}
+        done = [False] * n
+        low, span = 0, 0.0
+        for turn in range(lo, hi):
+            while done[order[low]]:
+                low += 1
+            j = low
+            while done[order[j]] or left[order[j]]:
+                j += 1
+            i = order[j]
+            done[i] = True
+            found = None
+            for f, (e, c) in enumerate(forms[i]):
+                s0 = at[i]
+                moved = True
+                while moved:
+                    lst = busy[e]
                     j = len(lst)
-                    while j and lst[j - 1][1] + pad > s0:
+                    while j and lst[j - 1][1] > s0:
                         j -= 1
-                    while j < len(lst) and lst[j][0] - pad < s0 + c:
-                        if (pad == 0.0 or lst[j][2] != e) and s0 < lst[j][1] + pad:
-                            s0 = lst[j][1] + pad
-                            moved = True
+                    while j < len(lst) and lst[j][0] < s0 + c:
+                        s0 = lst[j][1]
                         j += 1
-            st[i] = s0
-            for (key, pad) in keys[i]:
+                    moved = False
+                    for b in banks[i]:
+                        lst = busy[b]
+                        j = len(lst)
+                        while j and lst[j - 1][1] + pad > s0:
+                            j -= 1
+                        while j < len(lst) and lst[j][0] - pad < s0 + c:
+                            if lst[j][2] != e and s0 < lst[j][1] + pad:
+                                s0 = lst[j][1] + pad
+                                moved = True
+                            j += 1
+                w = s0 + c + (lean[2 * kinds + kd[i]] if f else 0.0)
+                if found is None or w < found[0]:
+                    found = (w, s0, f, e, c)
+            w, s0, f, e, c = found
+            st[i], form[i] = s0, f
+            for key in [e] + banks[i]:
                 lst = busy[key]
                 j = len(lst)
                 while j and lst[j - 1][0] > s0:
                     j -= 1
                 lst.insert(j, (s0, s0 + c, e))
-            end = s0 + c + (0.0 if rev else o["lat"]) + LAT
-            for k in post[i]:
-                if at[k] < end:
-                    at[k] = end
+            end = s0 + c + tail[i]
+            if i == goal:
+                return (end, st, form) if end <= bound else None
+            if end > span:
+                span = end
+                if span > bound and goal < 0:
+                    return None
+            for k in kids[i]:
+                w = s0 + c if e == "t" and cont[k] else end
+                if at[k] < w:
+                    at[k] = w
                 left[k] -= 1
-                if left[k] == 0:
-                    cand.add(k)
-        return st, max(st[i] + ops[i]["c"] + (0.0 if rev else ops[i]["lat"]) for i in range(n))
+        return span, st, form
+
+    def seek(lean, lo, hi, goal, some, turns, rng):
+        lay(lean, 0, n, 0, 1e9)
+        now = best = (lay(lean, lo, hi, goal, 1e9)[0], lean)
+        for turn in range(turns):
+            new = list(now[1])
+            for j in range(1 + turn % 4):
+                new[some[rng.randint(len(some))] + kinds * rng.randint(3)] += float(rng.normal()) * SIG * (0.1 + rng.rand() ** 2)
+            got = lay(new, lo, hi, goal, now[0] - HEAT * (1 - turn / turns) ** 2 * float(np.log(rng.rand())))
+            if got:
+                now = (got[0], new)
+                if now[0] < best[0]:
+                    best = now
+        return best[1]
+
+    def run(rank, alt, base):
+        order = sorted(range(n), key=lambda i: base[i] + rank[kd[i]])
+        left = [len(p) for p in deps]
+        at = [0.0] * n
+        why = [-1] * n
+        held = [False] * n
+        free = {k: (0.0, -1, k) for k in list(Q) + ["b%d" % b for b in range(8)]}
+        wait = []
+        span = tip = 0
+        for i0 in order:
+            wait.append(i0)
+            j = len(wait) - 1
+            while j >= 0:
+                i = wait[j]
+                if left[i]:
+                    j -= 1
+                    continue
+                del wait[j]
+                e, c = forms[i][alt[kd[i]]]
+                s0 = at[i]
+                f = free[e]
+                if f[0] > s0:
+                    s0, why[i], held[i] = f[0], f[1], True
+                for b in banks[i]:
+                    f = free[b]
+                    if f[2] != e and f[0] + pad > s0:
+                        s0, why[i], held[i] = f[0] + pad, f[1], True
+                at[i] = s0
+                f = free[e] = (s0 + c, i, e)
+                for b in banks[i]:
+                    free[b] = f
+                end = s0 + c + tail[i]
+                if end > span:
+                    span, tip = end, i
+                for k in kids[i]:
+                    w = s0 + c if e == "t" and cont[k] else end
+                    if at[k] < w:
+                        at[k], why[k] = w, i
+                    left[k] -= 1
+                j = len(wait) - 1
+        pairs = []
+        while tip >= 0:
+            if held[tip]:
+                pairs.append((tip, why[tip]))
+            tip = why[tip]
+        return span, at, [alt[k] for k in kd], pairs
+
+    def tune(got, turns, rng):
+        sends = [0.0] + [got[1][i] for i in range(n) if ops[i]["sem"][:3] == "arr"]
+        base = [0.0] * n
+        for t in range(1, NS):
+            for i in range(begin[t], begin[t + 1] if t + 1 < NS else n):
+                base[i] = sends[t]
+        rank, alt = [0.0] * kinds, [0] * kinds
+        for i in list(range(n)) + list(range(begin[4], begin[5])):
+            rank[kd[i]], alt[kd[i]] = got[1][i] - base[i], got[2][i]
+        now = best = run(rank, alt, base)
+        for turn in range(turns):
+            i, j = now[3][rng.randint(len(now[3]))]
+            r, f, how = list(rank), list(alt), rng.randint(6)
+            if how == 0 and len(forms[i]) > 1:
+                f[kd[i]] ^= 1
+            elif how == 1 and len(forms[j]) > 1:
+                f[kd[j]] ^= 1
+            elif how % 2:
+                r[kd[i]] = base[j] + rank[kd[j]] - base[i] - 1.0 - SIG * rng.rand() ** 4
+            else:
+                r[kd[j]] = base[i] + rank[kd[i]] - base[j] + 1.0 + SIG * rng.rand() ** 4
+            new = run(r, f, base)
+            if new[0] <= now[0] - HEAT * (1 - turn / turns) ** 2 * float(np.log(rng.rand())):
+                now, rank, alt = new, r, f
+                if now[0] < best[0]:
+                    best = now
+        return best
 
     if not PLAN:
         rng = np.random.RandomState(SEED)
-        kinds = max(o["k"] for o in ops) + 1
-        lean = [0.0] * (2 * kinds)
-        best = None
-        for turn in range(TURNS):
-            tryl = list(lean)
-            if turn:
-                for k in rng.randint(0, 2 * kinds, 1 + turn % 6):
-                    tryl[int(k)] += float(rng.normal()) * SIG
-            st, span = lay(False, ways(tryl, kinds))
-            if best is None or span <= best[0]:
-                best, lean = (span, st), tryl
-        for turn in range(2):
-            sb, _ = lay(True, {i: best[1][i] + full[i] for i in range(n)})
-            st, span = lay(False, {i: sb[i] + ops[i]["c"] for i in range(n)})
-            if span < best[0]:
-                best = (span, st)
+        lean = seek([0.0] * (2 * kinds) + [WISH] * kinds, 0, n, -1, list(range(kinds)), TURNS // 20, rng)
+        best = tune(lay(lean, 0, n, -1, 1e9), TURNS, rng)
         PLAN.append(sorted(range(n), key=lambda i: (best[1][i], i)))
+        PLAN.append(best[2])
         PLAN.append(best[0])
+    for i in range(n):
+        if PLAN[1][i]:
+            ops[i].update(ops[i]["alt"])
     clock = {k: {} for k in Q}
     total = {}
     tok = {}
@@ -723,7 +867,7 @@ def rank_program(g, core, T, topo):
         ins = o["call"]()
         sem = o["sem"]
         total[sem] = total.get(sem, 0) + o["n"]
-        if sem[:3] == "arr":
+        if sem[:2] == "ar":
             total["snt"] = total.get("snt", 0) + o["n"]
             tok[i] = (sem, total[sem], {sem: total[sem]})
         else:

@@ -2,57 +2,58 @@ import numpy as np
 from concourse.mybir import AluOpType as Op, ActivationFunctionType as Fn
 
 NV, NB, NT, NS = 2048, 256, 192, 7
-MW = 216
 NR = 16 * NT
+NX = 192 + NV + NT * NS
 F32, BF, I32, U16 = "float32", "bfloat16", "int32", "uint16"
 _S = {
-    "X": (192 + 3392, BF), "JF": (6144, BF), "EN": (3392, BF), "CH": (456, F32), "CHH": (256, BF), "CHL": (256, BF),
+    "X": (NX, F32), "XO": (NX, BF), "XT": (NX, BF), "JF": (6144, BF), "EN": (3392, BF), "CH": (456, F32), "CHH": (256, BF), "CHL": (256, BF),
     "SBI": (256, I32), "SBF": (256, F32), "SBU": (256, U16), "SB2": (512, F32), "HS2": (512, F32), "SKT": (456, F32),
     "HSK": (256, F32), "HT": (2048, BF), "SIO": (2048, F32), "GH": (4096, BF), "HEL": (128, U16), "HL": (128, U16),
     "OH": (2048, BF), "SBH": (256, BF), "SBL": (256, BF), "PK": (256, BF), "OWN": (256, F32),
-    "OUT": (7 * MW, BF), "LX": (7 * 12, U16), "MT": (272, BF), "MA": (512, BF),
-    "G": (NR + 7 * MW, BF), "D": (NR + 8 * MW, BF), "AB": (NR, BF), "EQ": (2304, BF), "ES": (2304, BF),
+    "OUT": (7 * NT, BF), "BI": (8 * 24, BF), "BO": (7 * 24, BF), "LX": (7 * 12, U16), "MT": (272, BF), "MA": (512, BF),
+    "G": (NR + 7 * NT, BF), "D": (NR + 8 * NT, BF), "AB": (NR, BF), "EQ": (2304, BF), "ES": (2304, BF),
     "PI": (2, I32), "PJ": (2, I32), "COL": (24, F32), "IM": (144, F32), "IMP": (128, F32), "IG": (128, F32),
-    "BD": (128, BF), "BDF": (128, F32), "ID": (128, BF), "IDS": (9 * 128, BF), "IFS": (4 * 128, F32),
-    "ZR": (512, BF), "ONE": (512, BF), "BB": (144, BF), "BND": (13 * 144, BF), "MX": (9 * 128, BF), "W1": (128, BF),
-    "IO": (456, BF), "ZZ": (768, BF), "DG": (2048, BF), "RC": (192, BF),
-    "R16": (16, F32), "WD": (16, F32), "I16": (16, F32), "SW": (4 * 512, BF), "DUP": (256, F32), "IB": (16, BF), "CZ": (12, BF),
-    "RO": (12, U16), "RS": (193, F32), "NI": (192, BF), "II": (36, F32), "CM": (192, BF),
+    "BD": (128, BF), "BDF": (128, F32), "ID": (128, BF), "IDS": (6 * 128, BF), "IFS": (4 * 128, F32),
+    "ZR": (256, BF), "ONE": (192, BF), "BB": (144, BF), "BND": (13 * 144, BF), "MX": (11 * 128, BF), "W1": (128, BF),
+    "IO": (456, BF), "DG": (2048, BF), "RC": (192, BF), "LT": (192, BF),
+    "R16": (16, F32), "WD": (32, F32), "SW": (4 * 512, BF), "DUP": (256, F32), "IB": (16, BF), "CZ": (12, BF),
+    "RO": (12, U16), "RS": (384, F32), "NI": (192, BF), "II": (36, F32), "CM": (192, BF),
     "T1": (60, F32), "T2": (12, I32), "PEI": (128, I32), "HEI": (128, I32), "DQ": (128, BF),
     "PEB": (128, BF), "HEB": (128, BF), "HIC": (128, BF), "LOC": (128, BF), "BXI": (192, I32), "BXB": (192, BF),
-    "LMI": (2, I32), "LMF": (2, F32), "LIM": (8, F32), "AI": (6, I32),
+    "LMI": (2, I32), "LMF": (2, F32), "LIM": (8, F32), "AI": (8, I32),
     "LM": (12, U16), "HK": (192, F32), "HR": (192, F32), "L1": (192, U16), "CL": (192, U16), "KR": (192, F32),
-    "TM": (192, F32), "A32": (72, I32), "U1": (192, F32), "Q1": (192, F32), "VF": (192, BF),
+    "TM": (192, F32), "A32": (72, I32), "U1": (192, F32), "Q1": (384, F32), "VF": (192, BF), "ZZ": (768, BF),
     "YJ": (128, F32), "YB": (384, F32), "GE": (384, BF), "AF": (192, BF), "EF": (192, U16),
-    "NZ": (384, BF), "TZ": (192, BF), "FZ": (192, BF),
+    "NZ": (384, BF), "TZ": (192, BF), "FZ": (192, BF), "ZM": (384, F32),
     "NF": (192, BF), "CO": (60, U16), "DE": (384, BF), "EL": (24, U16), "BL": (24, U16), "NE": (384, BF), "SM": (192, F32),
-    "KK": (120, BF), "WH": (576, BF), "FL": (384, BF), "UU": (192, BF), "OD": (192, F32), "SK": (192, F32), "LW": (192, BF),
+    "KK": (120, BF), "WH": (576, BF), "FL": (384, BF), "UU": (192, BF), "OD": (192, F32), "SK": (192, F32), "ZL": (192, F32),
     "M": (192, BF), "BX": (12, BF),
 }
-TWICE = ("NF", "CO", "DE", "EL", "BL", "NE", "SM", "KK", "WH", "FL", "UU", "OD", "SK", "LW", "M", "BX")
+TWICE = ("NF", "CO", "DE", "EL", "BL", "NE", "SM", "KK", "WH", "FL", "UU", "OD", "SK", "ZL", "M", "BX")
 SCRATCH = {k: ("sbuf", [128, w * (2 if k in TWICE else 1)], d) for k, (w, d) in _S.items()}
 for _b in range(8):
     SCRATCH["b%d" % _b] = ("psum", [128, 512], F32)
-SEMAPHORES = ["cv", "cs", "ct", "cg", "snt"] + ["ar%s%d" % (k, i) for k in "rz" for i in range(NS)] + ["d%d" % i for i in range(48)]
+SEMAPHORES = (["cv", "cs", "ct", "cg", "snt", "dh", "dl"] + ["ar%s%d" % (k, i) for k in "rz" for i in range(NS)]
+              + ["d%d" % i for i in range(56)])
 CHAINED = ("b0", "b1", "b2", "b3", "b5")
 
-MARK = 192.0
-SPLIT, SOME, VOID = float(2 ** 19), float(2 ** 20), float(2 ** 22)
-IDS = {"NID": -1.0, "IDH": 0.5, "E01": -192.0, "I13": 8192.0, "I12": 4096.0, "IV": VOID,
-       "I8": 256.0}
-IFS = {"IDF": 1.0, "NIF": -1.0, "IDQ": 1.0 / 8192, "I13F": 8192.0}
-MXS = ("LO", "LC", "LE", "LN0", "LN1", "BD3", "BDN", "WC")
-BANDS = ("B0", "B1", "B4", "B03", "BAL", "BK", "BN", "BP", "BC", "BE", "BEP", "B5", "BM")
-SCALES = (1.0, 16.0, 192.0, 1024.0)
-CY, GA, SCA, PE, LAT, DMA, REM = 1.04, 1.56, 3.8, 0.53, 90.0, 2300.0, 2500.0
+LIFT = 192.0
+SPLIT, SOME, VOID = 1023.5, 2048.0, 8192.0
+IDS = {"NID": -1.0, "IDH": 0.5, "E01": -2 * LIFT, "I13": 8192.0, "I9": 512.0, "INF": -2.0 ** 23}
+IFS = {"IDF": 1.0, "NIF": -1.0, "IDQ": 2.0 ** -21}
+MXS = ("LO", "LE", "LN0", "LN1", "BD3", "BDN", "BDP", "BDM", "BDS", "WC")
+BANDS = ("B0", "B1", "B03", "BAL", "BK", "BN", "BP", "BC", "BE", "BEP", "B5", "BM")
+SCALES = (1.0, 32.0, 512.0, 6144.0)
+CY, GA, SCA, PE, LAT, DMA, REM = 0.95, 1.56, 3.8, 0.5, 130.0, 2300.0, 2500.0
 TURN = (0, 4, 12)
 FREE = (0, 6, 12)
-LOOKS = (0, 2, 4, 6, 9, 11, 14, 16)
-PICKS = (0, 2, 6, 11, 16)
-DIFF = (0, 2, 4, 6, 8, 10, 11, 13, 15, 16)
-ABS = (0, 2, 4, 6, 8, 11, 13, 15, 16)
-LOV = 0
-TURNS, SIG, SEED = 35000, 1500.0, 1
+LOOKS = (0, 2, 4, 6, 8, 12, 16)
+PICKS = (0, 2, 8, 12, 16)
+DIFF = (0, 2, 4, 8, 12, 15, 16)
+ABS = (0, 2, 4, 8, 12, 14, 15, 16)
+LOW = 160
+WIDE = max(k1 - k0 for k0, k1 in zip(DIFF, DIFF[1:]))
+TURNS, SIG, SEED = 65000, 1500.0, 1
 WISH, HEAT = 800.0, 100.0
 PLAN = []
 
@@ -67,7 +68,6 @@ def rank_program(g, core, T, topo):
     ops = []
     nd = [0]
     par = [0]
-    kind = [0]
 
     def a(name, lo=0, hi=None, st=1, p=None, old=0):
         for (buf, names) in (("IDS", list(IDS)), ("IFS", list(IFS)), ("MX", MXS)):
@@ -107,8 +107,7 @@ def rank_program(g, core, T, topo):
         for x in writes:
             ws += x[1]
             rs += x[2]
-        ops.append({"e": e, "r": rs, "w": ws, "call": call, "c": cost, "sem": sem or own[e], "n": n, "cont": cont, "lat": lat, "k": kind[0]})
-        kind[0] += 1
+        ops.append({"e": e, "r": rs, "w": ws, "call": call, "c": cost, "sem": sem or own[e], "n": n, "cont": cont, "lat": lat})
 
     def vcost(out, x, per):
         if out[2]:
@@ -137,10 +136,12 @@ def rank_program(g, core, T, topo):
         put("v", [x], [out], lambda: g.vector.transpose(out[0], x[0]), vcost(out, x, 0.5 if two(out) else 1))
 
     def scan(out, d0, d1):
-        put("v", [d0, d1], [out], lambda: g.vector.tensor_tensor_scan(out[0], d0[0], d1[0], 0.0, Op.add, Op.min), vcost(out, d1, 1))
+        put("v", [d0, d1], [out], lambda: g.vector.tensor_tensor_scan(out[0], d0[0], d1[0], 0.0, Op.max, Op.min), vcost(out, d1, 1))
 
     def sact(out, x, f=Fn.Identity, bias=0.0, scale=1.0, acc=None):
-        if acc is None:
+        if out[2]:
+            put("s", [x], [out], lambda: g.scalar.activation(out[0], x[0], f), vcost(out, x, 1) + 15)
+        elif acc is None:
             put("s", [x, bias, scale], [out], lambda: g.scalar.activation(out[0], x[0], f, bias=val(bias), scale=val(scale)), vcost(out, x, 1))
         else:
             put("s", [x, bias, scale], [out, acc], lambda: g.scalar.activation(
@@ -150,7 +151,6 @@ def rank_program(g, core, T, topo):
         o = ops.pop()
         ops[-1]["alt"] = {k: o[k] for k in ("e", "call", "c", "sem")}
         ops[-1]["r"] = ops[-1]["r"] + o["r"]
-        kind[0] -= 1
 
     def act(out, x, f=Fn.Identity, bias=0.0, scale=1.0):
         sact(out, x, f, bias, scale)
@@ -171,6 +171,14 @@ def rank_program(g, core, T, topo):
 
     def gcp(out, x):
         put("g", [x], [out], lambda: g.affine_select(out[0], x[0], [[0, x[3]]], Op.is_ge, 0.0, 0, 0), 170 + 2 * CY * out[3])
+
+    def diag(out, c):
+        act(out, a("ID"), scale=c)
+        o = ops.pop()
+        x = a("ZR", 0, 128)
+        put("g", [x], [out], lambda: g.affine_select(out[0], x[0], [[-1, 128]], Op.not_equal, c, 0, 1), 170 + 2 * CY * 128)
+        ops.append({**o, **o["alt"]})
+        either()
 
     def iota(out, pat, base=0, ch=0):
         if _S[out[1][0][0]][1] == I32:
@@ -217,8 +225,9 @@ def rank_program(g, core, T, topo):
 
         def off(cs):
             return [(a("b5", 16 * c + 16, 192), a("BD"), a(eq, 208 * c + 16, 192 * c + 192)) for c in cs]
-        mm([zero("b5", 0, 192)] + off(range(6)), True, False)
-        mm(off(range(6, 11)), False, False)
+        mm([zero("b5", 0, 192)], True, False)
+        for c0, c1 in ((0, 3), (3, 7), (7, 11)):
+            mm(off(range(c0, c1)), False, False)
         mm([(a("b5", r, 192, 16), a("DG", 128 * r, 128 * r + 128), a(eq, r, 208 * 11 + r + 1, 208)) for r in range(16)], False, True)
 
     def fill(out, c):
@@ -233,6 +242,12 @@ def rank_program(g, core, T, topo):
 
     def unit(j):
         return a("R16", j, j + 1)
+
+    def lim(j):
+        return a("LIM", j, j + 1)
+
+    def ai(j):
+        return a("AI", j, j + 1)
 
     def sm(j, n=1):
         return a("SM", 12 * j, 12 * (j + n))
@@ -249,6 +264,9 @@ def rank_program(g, core, T, topo):
     def rowz(name, k, lo=0):
         return a(name, lo + k, lo + 192, 16)
 
+    def zof(t):
+        return a("D", NR + NT * t, NR + NT * t + 192)
+
     ms(a("BXI"), 0)
     iota(a("LMI"), [[0, 2]])
     dma("y", a("SBI"), hbm(T.sb[:]))
@@ -256,27 +274,32 @@ def rank_program(g, core, T, topo):
     dma("y", a("BXI", p=row(0)), hbm(T.bx[:]))
     dma("s", a("PEI"), hbm(T.pe[:]))
     dma("y", a("LMI", p=row(0)), hbm(T.lim[:]))
-    dma("y", a("D", NR, NR + 192), hbm(T.zs[:]))
-    dma("y", a("X", 192, 192 + NV), hbm(T.xs[:]), None, 2500.0)
-    ms(a("EN", 0, NV), 0.0)
+    dma("y", zof(0), hbm(T.zs[:]))
+    for h in range(2):
+        dma("y", a("XO", 192 + 1024 * h, 1216 + 1024 * h), hbm(T.xs[:, 1024 * h:1024 * h + 1024]), None, 1200.0 + 1200.0 * h)
+    for h in range(4):
+        act(a("X", 192 + 512 * h, 704 + 512 * h), a("XO", 192 + 512 * h, 704 + 512 * h), bias=2 * LIFT)
+    act(zof(0), zof(0), bias=LIFT)
+    ms(a("EN", 0, NV), 1.0)
     for h in range(3):
-        dma("y", a("JF", 2048 * h, 2048 * h + 2048), a("X", 192, 192 + NV), None, 2500.0)
+        dma("y", a("JF", 2048 * h, 2048 * h + 2048), a("XO", 192, 192 + NV), None, 2500.0)
 
-    iota(a("ZR"), [[0, 512]])
-    iota(a("ONE"), [[0, 512]], 1)
+    iota(a("ZR"), [[0, 256]])
+    iota(a("ONE"), [[0, 192]], 1)
     iota(a("PI", 0, 1), [[0, 1]], 0, 1)
     iota(a("IM"), [[1, 144]])
     iota(a("IG"), [[1, 8], [0, 16]])
     iota(a("IMP"), [[1, 128]], 0, -1)
     iota(a("II"), [[0, 3], [16, 12]])
-    iota(a("W1"), [[0, 8], [16, 16]])
+    iota(a("W1"), [[0, 8], [1, 16]], -12)
     iota(a("NI"), [[1, 192]])
     iota(a("IO"), [[1, 456]])
-    iota(a("SIO"), [[1, 2048]])
+    for lo in range(0, NV, 512):
+        iota(a("SIO", lo, lo + 512), [[1, 512]], lo)
     iota(a("OWN"), [[1, 256]])
     iota(a("MA", 0, 256), [[0, 16], [1, 16]])
     iota(a("MA", 256, 512), [[1, 16], [0, 16]])
-    iota(a("G", NR, NR + 7 * MW), [[0, 7 * MW]], 1)
+    iota(a("G", NR, NR + 7 * NT), [[0, 7 * NT]], 1)
     ts(a("PJ", 0, 1), a("PI", 0, 1), 15, Op.bitwise_and)
     ts(a("PJ", 1, 2), a("PI", 0, 1), 4, Op.logical_shift_right)
     cp(a("COL", 0, 2), a("PJ"))
@@ -292,19 +315,28 @@ def rank_program(g, core, T, topo):
     for j in (1, 3, 4):
         dma("y", a("JF", 4096, 6144, p=row(j)), a("ZR", 0, 128))
     ts(a("R16"), a("IM", 0, 16), col(0), Op.is_equal)
-    act(col(11), unit(2), scale=2.0)
     ts(col(5), col(0), 3.5, Op.is_lt)
     act(col(6), col(0), scale=256.0)
     act(col(7), unit(4), bias=col(5), scale=8192.0)
+    act(col(14), col(2), scale=256.0)
+    for j, w in ((11, 2.0), (15, 4.0), (16, -256.0), (17, 1.0 / 32), (18, LIFT)):
+        act(col(j), unit(2), scale=w)
     ts(a("BD"), a("IG"), col(1), Op.is_equal)
     act(a("BDF"), a("BD"))
     ts(a("ID"), a("IMP"), 0.0, Op.is_equal)
-    for nm, w in IFS.items():
-        act(a(nm), a("ID"), scale=w)
+    for nm, w in list(IFS.items()) + list(IDS.items()):
+        diag(a(nm), w)
+    for nm, w in (("BD3", col(5)), ("BDN", -4096.0), ("BDP", 4096.0), ("BDM", 2.0 ** 22), ("BDS", col(18))):
+        act(a(nm), a("BD"), scale=w)
     ts(a("BB"), a("IM"), col(4), Op.is_equal)
-    for nm, w in (("B4", unit(4)), ("B0", unit(0)), ("B03", col(5)), ("B1", unit(1)), ("BAL", 512.0), ("BK", col(6)), ("BN", -8192.0),
+    for nm, w in (("B0", unit(0)), ("B03", col(5)), ("B1", unit(1)), ("BAL", 1.0), ("BK", col(6)), ("BN", -8192.0),
                   ("BP", 8192.0), ("BEP", col(7)), ("B5", unit(5))):
         act(a(nm), a("BB"), scale=w)
+    act(col(19), unit(2), bias=unit(4), scale=4096.0)
+    act(col(20), unit(2), bias=unit(1), scale=-8192.0)
+    act(a("BC"), a("BB"), scale=col(19))
+    act(a("BE"), a("BB"), scale=col(20))
+    act(a("BM"), a("B0"), scale=-1.0)
     for be in range(2):
         for ga in range(2):
             ts(a("SW", 256 * be + 128 * ga, 256 * be + 128 * ga + 128), a("IMP"), 16.0 * (ga - be), Op.is_equal, col(2 + be), Op.mult)
@@ -315,7 +347,7 @@ def rank_program(g, core, T, topo):
     cp(a("HEB"), a("HEI"))
     cp(a("PEB"), a("PEI"))
     tt(a("DQ"), a("HEI"), a("PEI"), Op.subtract)
-    for j, x in ((1, a("HEB")), (0, a("PEB")), (3, a("DQ")), (2, a("ONE", 0, 128)), (4, a("HIC")), (5, a("LOC"))):
+    for j, x in ((1, a("HEB")), (0, a("PEB")), (3, a("DQ")), (4, a("HIC")), (5, a("LOC"))):
         dma("y", a("EN", 0, NV, p=row(j)), x)
     mm([(a("b1", 0, 256), a("DUP", 0, 128), a("SBF"))])
     mm([(a("b1", 256, 512), a("DUP", 128, 256), a("SBF"))])
@@ -323,9 +355,8 @@ def rank_program(g, core, T, topo):
     cp(a("BXB"), a("BXI"))
     tr(a("TZ"), a("BXB"))
     iota(a("CZ"), [[0, 6], [-256, 2]], 256)
-    act(col(14), col(2), scale=256.0)
-    tt(a("D", NR + 192, NR + 204), rowz("TZ", 0), a("CZ"), Op.subtract)
-    iota(a("D", NR + 204, NR + 216), [[0, 12]])
+    tt(a("BI", 1, 24, 2), rowz("TZ", 0), a("CZ"), Op.subtract)
+    ms(a("BI", 0, 24, 2), 0.0)
     act(a("II"), a("II"), bias=col(0))
     act(a("IB", 0, 12), a("II", 0, 12))
     act(a("II", 12, 24), a("II", 12, 24), bias=256.0)
@@ -335,23 +366,19 @@ def rank_program(g, core, T, topo):
     act(a("T1", 16, 28), a("II", 0, 12), scale=16.0)
     tt(a("T1", 32, 44), a("T1", 16, 28), a("T1", 48, 60), Op.add)
     cp(a("RO"), a("T1", 32, 44))
-    ts(a("WD"), a("IM", 0, 16), col(0), Op.is_gt)
-    act(a("I16"), a("R16"), scale=-256.0)
-    tt(a("WD"), a("WD"), a("I16"), Op.add)
+    ts(a("WD", 0, 16), a("IM", 0, 16), col(0), Op.is_gt)
+    act(a("WD", 16, 32), a("R16"), scale=-256.0)
+    tt(a("WD", 0, 16), a("WD", 0, 16), a("WD", 16, 32), Op.add)
     for r in range(16):
         act(a("DG", 128 * r, 128 * r + 128), a("BD"), scale=a("WD", r, r + 1))
-    for nm, w in IDS.items():
-        act(a(nm), a("ID"), scale=w)
-    act(a("BD3"), a("BD"), scale=col(5))
-    act(a("BDN"), a("BD"), scale=-4096.0)
-    iota(a("RS"), [[0, 193]])
-    ms(a("RS", 1, 193, 16), float(2 ** 27))
+    iota(a("RS"), [[0, 384]])
+    fill(a("RS", 193, 384, 16), SOME + 4.0 / 32)
     iota(a("TM", 0, 1), [[0, 1]])
     iota(a("CH", 0, 448), [[0, 448]])
     iota(a("CH", 448, 456), [[0, 8]], 1)
     iota(a("SKT", 256, 456), [[0, 200]])
     iota(a("YB", 192, 384), [[0, 192]])
-    iota(a("CM"), [[0, 192]], int(MARK))
+    iota(a("CM"), [[0, 192]], -int(LIFT))
     ts(a("MA"), a("MA"), col(0), Op.is_equal)
     mm([(a("b7", 256, 512), a("ID"), a("MA", 256 * j, 256 * j + 256)) for j in range(2)])
     act(a("MT", 1, 257), a("b7", 256, 512), bias=1.0)
@@ -359,19 +386,21 @@ def rank_program(g, core, T, topo):
     iota(a("MT", 257, 272), [[0, 15]], 1)
     cp(a("LMF"), a("LMI"))
     mm([(a("b6", 16, 18), a("BDF"), a("LMF"))])
-    act(a("LIM", 1, 2), a("b6", 16, 17), bias=-73728.5)
-    act(a("LIM", 3, 4), a("b6", 16, 17), bias=160 * 256 - 73728.5)
-    act(a("LIM", 5, 6), a("LIM", 3, 4), bias=159.5 + 1.0 / 64, scale=-1.0 / 256)
-    ts(a("LIM", 2, 3), a("b6", 17, 18), 1008.0, Op.min, -1.0, Op.mult)
-    ts(a("AI", 2, 3), a("LIM", 2, 3), 1023.0, Op.add)
-    ts(a("AI", 3, 4), a("AI", 2, 3), 5, Op.logical_shift_right)
-    ts(a("AI", 4, 5), a("AI", 2, 3), 31, Op.bitwise_and)
-    ts(col(12), a("AI", 3, 4), unit(0), Op.mult, unit(2), Op.add)
-    ts(col(12), a("AI", 4, 5), unit(1), Op.mult, col(12), Op.add)
+    cp(ai(5), a("b6", 16, 17))
+    ts(ai(6), ai(5), 992, Op.bitwise_and)
+    ts(ai(7), ai(5), 31, Op.bitwise_and)
+    ts(lim(1), ai(6), unit(0), Op.mult)
+    ts(lim(1), ai(7), unit(1), Op.mult, lim(1), Op.add)
+    act(lim(3), unit(2), bias=lim(1), scale=160.0 * 256)
+    ts(lim(2), a("b6", 17, 18), 1008.0, Op.min, -1.0, Op.mult)
+    ts(ai(2), lim(2), 1023.0, Op.add)
+    ts(ai(3), ai(2), 992, Op.bitwise_and)
+    ts(ai(4), ai(2), 31, Op.bitwise_and)
+    ts(col(12), ai(3), unit(0), Op.mult, unit(2), Op.add)
+    ts(col(12), ai(4), unit(1), Op.mult, col(12), Op.add)
     fill(a("RC"), col(12))
-    act(col(13), unit(0), scale=16384.0)
-    act(col(13), unit(1), bias=col(13), scale=512.0)
-    act(a("W1"), a("W1"), bias=col(13), scale=unit(2))
+    act(col(13), unit(0), bias=unit(1))
+    act(a("W1"), a("W1"), bias=col(13), scale=col(17))
     tt(a("WC"), a("W1"), a("BD"), Op.mult)
     act(a("SBH"), a("SBF"))
     dma("y", a("JF", 0, 4096, p=row(2)), a("SBH"))
@@ -381,12 +410,8 @@ def rank_program(g, core, T, topo):
     for j in (0, 1, 4):
         dma("y", a("JF", 0, 4096, p=row(j)), a("ZR", 0, 256))
     mm(pick("b6", 128, "B1", "EN", 0, 128))
-    act(a("BC"), a("B0"), scale=4096.0)
-    act(a("BE"), a("B0"), scale=-8192.0)
-    act(a("BM"), a("B0"), scale=-1.0)
     msum(a("LO"), [("ID", band("BN", 0)), ("ID", band("BN", 1)), ("ID", band("BK", 2)), ("ID", band("BP", 3))])
-    msum(a("LC"), [("ID", band("BC", 0)), ("ID", band("BE", 3))])
-    msum(a("LE"), [("ID", band("B1", 3)), ("ID", band("B0", 5)), ("ID", band("B4", 0)), ("ID", band("B5", 1))])
+    msum(a("LE"), [("ID", band("BE", 3)), ("ID", band("B0", 5)), ("ID", band("BC", 0)), ("ID", band("B5", 1))])
     msum(a("LN0"), [("ID", band("B5", 0)), ("NID", band("B5", 3))])
     act(a("LN1"), band("B5", 3))
     cp(a("SBU"), a("SBI"))
@@ -394,39 +419,32 @@ def rank_program(g, core, T, topo):
     for h in range(4):
         bk = ("b1", "b7")[h % 2]
         tt(a("OH", 512 * h, 512 * h + 512), ind(a("SBF"), a("HEL", 32 * h, 32 * h + 32)), a("SIO", 512 * h, 512 * h + 512), Op.is_equal)
-        mm([(a(bk), a("LC"), a("ONE")), (a(bk), a("LE"), a("EN", 512 * h, 512 * h + 512)),
-            (a(bk), a("LO"), a("OH", 512 * h, 512 * h + 512))])
+        mm([(a(bk), a("LE"), a("EN", 512 * h, 512 * h + 512)), (a(bk), a("LO"), a("OH", 512 * h, 512 * h + 512))])
         act(a("HT", 512 * h, 512 * h + 512), a(bk), Fn.Relu)
     for h in range(8):
         act(a("GH", 512 * h, 512 * h + 512), ind(a("HT"), a("SBU", 32 * h, 32 * h + 32)))
 
-    def numbers(t, upto, plus, cut):
+    def numbers(t, wide, name, lo, old, cut):
         for j0, j1 in zip(cut, cut[1:]):
-            out = ind(a("X", 0, 192 + NV + NT * upto), a("LX", 12 * t + j0, 12 * t + j1))
-            z = a("D", NR + MW * t + 16 * j0, NR + MW * t + 16 * j1)
-            if plus is None:
-                cp(out, z)
-            else:
-                tt(out, z, a(plus, 16 * j0, 16 * j1, old=1), Op.add)
+            out = ind(a("X", 0, 192 + wide), a("LX", 12 * t + j0, 12 * t + j1))
+            x = a(name, lo + 16 * j0, lo + 16 * j1, old=old)
+            sact(out, x, Fn.Silu)
+            cp(out, x)
+            either()
 
-    first = 0
     begin = []
     for t in range(NS):
         par[0] = t % 2
         last = t == NS - 1
         begin.append(len(ops))
-        if t == 1:
-            first = kind[0]
-        if 1 < t and not last:
-            kind[0] = first
-        zo = NR + MW * t
-        z = a("D", zo, zo + 192)
-        ao = zo + 192
+        z = zof(t)
+        zo = NR + NT * t
+        ao = 24 * t
         box = kk(9)
-        rest = a("D", ao + 12, ao + 24)
+        rest = a("BI", ao, ao + 24, 2)
         wide = NV + NT * t
-        ts(a("LM"), a("D", ao, ao + 12), 256.0, Op.add)
-        tt(box, a("D", ao, ao + 12), a("CZ"), Op.add)
+        ts(a("LM"), a("BI", ao + 1, ao + 24, 2), 256.0, Op.add)
+        tt(box, a("BI", ao + 1, ao + 24, 2), a("CZ"), Op.add)
         act(a("HK"), ind(a("HS2" if t else "SB2"), a("LM")))
         tr(a("HR"), a("HK"))
         for j0, j1 in zip(TURN, TURN[1:]):
@@ -441,14 +459,14 @@ def rank_program(g, core, T, topo):
         if t:
             over(kk(6), rest, 0.0)
             act(rest, rest, Fn.Relu, bias=-1.0)
-        mm([zero("b6", 32, 12)] + swap("b6", 32, 0, "D", ao) + (swap("b6", 32, 3, "KK", 72) if t else []))
+        mm([zero("b6", 32, 12)] + swap("b6", 32, 0, "BI", ao + 1, 2) + (swap("b6", 32, 2, "KK", 72) if t else []))
         ts(a("BX"), a("b6", 32, 44), col(14), Op.add, 448.0, Op.min)
         cp(a("BL", 0, 12), a("BX"))
         act(a("AF"), ind(a("IO"), a("BL", 0, 12)))
         lowest("ES", "AF", "BX", 0)
         over(a("NF"), a("b5", 0, 192), -256.0)
         tr(a("FZ"), a("NF"))
-        mm([(a("b7", 192, 204), a("ID"), a("BX"))] + swap("b7", 192, 3, "FZ", 0, 16))
+        mm([(a("b7", 192, 204), a("ID"), a("BX"))] + swap("b7", 192, 2, "FZ", 0, 16))
         tt(sm(1), a("b7", 192, 204), a("II", 12, 24), Op.min)
         cp(a("BL", 12, 24), sm(1))
         act(a("SK"), ind(a("SKT" if t else "SBF"), a("BL", 0, 12)))
@@ -459,39 +477,46 @@ def rank_program(g, core, T, topo):
             act(a("OD"), ind(a("CH"), a("BL", 0, 12)))
             over(a("VF"), a("OD"), 0.0)
             mm([(key, a("IDQ"), a("SK"))], False, False)
-            mm([(key, a("IV"), a("VF"))], False, False)
+            mm([(key, a("I13"), a("VF"))], False, False)
         cl = "CL" if t else "L1"
-        for j in range(max(k1 - k0 for k0, k1 in zip(DIFF, DIFF[1:]))):
-            gcp(a("ZZ", 192 * j, 192 * j + 192), z)
+        if t:
+            gcp(a("ZZ", 0, 192), z)
+        else:
+            act(a("ZZ", 0, 192), z, bias=-2 * LIFT)
+        gcp(a("ZZ", 192, 384), z if t else a("ZZ", 0, 192))
+        gcp(a("ZZ", 384, 192 * WIDE), a("ZZ", 0, 192 * WIDE - 384))
         for k0, k1 in zip(DIFF, DIFF[1:]):
-            tt(a("D", 192 * k0, 192 * k1), ind(a("X", 192, 192 + wide), a(cl, 12 * k0, 12 * k1)),
-               a("ZZ", 0, 192 * (k1 - k0)) if k1 - k0 > 1 else z, Op.subtract)
+            tt(a("D", 192 * k0, 192 * k1), ind(a("X" if t else "XO", 192, 192 + wide), a(cl, 12 * k0, 12 * k1)),
+               a("ZZ", 0, 192 * (k1 - k0)), Op.subtract)
         for k0, k1 in zip(ABS, ABS[1:]):
-            act(a("AB", 192 * k0, 192 * k1), a("D", 192 * k0, 192 * k1), Fn.Abs)
+            act(a("AB", 192 * k0, 192 * k1), a("D", 192 * k0, 192 * k1), Fn.Abs, bias=-LIFT)
             mm([(key, band("BAL", k), a("AB", 192 * k, 192 * k + 192)) for k in range(k0, k1)], False, k1 == 16)
+        fill(a("RS", 0, 192, 16), SOME + (4.0 + t) / 32)
         tr(a("KR"), key)
         m1, m2 = a("b2", 15, 192, 16), a("b2", 207, 384, 16)
-        scan(a("b2", 0, 192), a("RS", 1, 193), a("KR"))
-        ts(a32(0), m1, SOME + 256 + 18 * t, Op.min)
-        ts(a32(2), a32(0), 1, Op.logical_shift_right, 255, Op.bitwise_and)
-        ts(kk(0), a32(2), 0.125, Op.mult)
-        mm([(a("b7", 64, 76), a("ID"), a("IB", 0, 12))] + swap("b7", 64, 2, "KK", 0))
-        cp(co(0), a("b7", 64, 76))
+        scan(a("b2", 0, 192), a("RS", 0, 192), a("KR"))
+        ts(a32(0), m1, -4.0, Op.add)
+        tt(kk(0), m1, a32(0), Op.subtract)
+        mm([(a("b7", 64, 76), a("ID"), a("IB", 0, 12))] + swap("b7", 64, 3, "KK", 0))
+        ts(co(0), a("b7", 64, 76), -192.0 * 116, Op.add)
         ts(kk(2), m1, SPLIT, Op.is_ge, -32768.0, Op.mult)
         tt(a("TM", 1, 192), a("b2", 0, 191), a("KR", 1, 192), Op.max)
-        scan(a("b2", 192, 384), a("RS", 0, 192), a("TM"))
-        ts(a32(1), m2, SOME + 256, Op.min)
-        ts(a32(3), a32(1), 1, Op.logical_shift_right, 255, Op.bitwise_and)
-        ts(kk(1), a32(3), 0.125, Op.mult)
-        mm([(a("b7", 76, 88), a("ID"), a("IB", 0, 12))] + swap("b7", 76, 2, "KK", 12))
-        cp(co(1), a("b7", 76, 88))
+        scan(a("b2", 192, 384), a("RS", 192, 384), a("TM"))
+        ts(a32(1), m2, -4.0, Op.add)
+        tt(kk(1), m2, a32(1), Op.subtract)
+        if t:
+            ts(a32(2, 2), a("b2", 15, 384, 16), 1024.0, Op.mult)
+            ts(a32(4, 2), a32(2, 2), 4, Op.bitwise_and)
+            tt(kk(3), a32(4), a32(5), Op.add)
+        mm([(a("b7", 76, 88), a("ID"), a("IB", 0, 12))] + swap("b7", 76, 3, "KK", 12))
+        ts(co(1), a("b7", 76, 88), -192.0 * 116, Op.add)
         for j in range(2):
             if t:
                 act(a("GE", 192 * j, 192 * j + 192), ind(a("G", 0, zo + 192), co(j)))
             else:
-                ts(kk(7 + j), a32(2 + j), 32.0, Op.mult)
-                mm([(a("b0", 32 + 12 * j, 44 + 12 * j), a("ID"), a("BX"))] + swap("b0", 32 + 12 * j, 0, "KK", 84 + 12 * j))
-                cp(co(2 + j), a("b0", 32 + 12 * j, 44 + 12 * j))
+                act(kk(7 + j), kk(j), scale=256.0)
+                mm([(a("b0", 32 + 12 * j, 44 + 12 * j), a("ID"), a("BX"))] + swap("b0", 32 + 12 * j, 1, "KK", 84 + 12 * j))
+                ts(co(2 + j), a("b0", 32 + 12 * j, 44 + 12 * j), -256.0 * 116, Op.add)
                 act(a("GE", 192 * j, 192 * j + 192), ind(a("JF", 0, 4096), co(2 + j)))
         ne = 1 if t else 2
         e = a("b6", 0, 12)
@@ -507,27 +532,22 @@ def rank_program(g, core, T, topo):
             cp(a("EL", 12, 24), a("b7", 160, 172))
         for j in range(ne):
             act(a("NE", 192 * j, 192 * j + 192), ind(a("EN", 0, wide), a("EL", 12 * j, 12 * j + 12)))
-        act(a("WH", 0, 192), de, Fn.Abs)
-        act(a("WH", 192, 384), de, bias=191.75, scale=0.5)
+        act(a("WH", 0, 192), de, Fn.Abs, bias=-LIFT)
+        act(a("WH", 192, 384), de, bias=191.75 - LIFT / 2, scale=0.5)
         act(a("WH", 384, 576), df, Fn.Abs)
         tr(a("NZ", 0, 192 * ne), a("NE", 0, 192 * ne))
         tt(sm(4), rowz("NZ", 0), box, Op.is_equal)
         tt(sm(3), rowz("NZ", 0), box, Op.subtract)
         tt(sm(5), sm(4), rowz("NZ", 3), Op.mult)
-        tt(sm(6), sm(5), sm(3), Op.add)
+        tt(rowz("NZ", 10), sm(5), sm(3), Op.add)
         mm([(a("b2", 192, 384), a(w), x) for (w, x) in (
             ("ID", z), ("E01", a("ONE", 0, 192)), ("ID", a("WH", 192, 384)), ("NID", a("WH", 0, 192)))])
-        if t:
-            ts(a32(4, 2), a32(0, 2), 1, Op.bitwise_and)
-            tt(kk(3), a32(4), a32(5), Op.add)
-        else:
+        if not t:
             for j in range(2):
                 tt(kk(3 + j), rowz("NZ", 1, 192 * j), box, Op.not_equal)
-        code = a("b0", 88, 100)
-        mm([(code, a("ID"), a("ONE", 0, 12))] + swap("b0", 88, 3, "FZ", 0, 16), True, False)
-        mm(swap("b0", 88, 0, "KK", 0) + swap("b0", 88, 0, "KK", 24), False, False)
-        mm(swap("b0", 88, 1, "KK", 12) + swap("b0", 88, 3, "KK", 36) + ([] if t else swap("b0", 88, 3, "KK", 48)), False, True)
-        ts(co(4), code, 257.0, Op.min)
+        mm([zero("b0", 88, 12)] + swap("b0", 88, 1, "KK", 0) + swap("b0", 88, 0, "KK", 24), True, False)
+        mm(swap("b0", 88, 2, "KK", 12) + swap("b0", 88, 2, "KK", 36) + ([] if t else swap("b0", 88, 2, "KK", 48)), False, True)
+        ts(co(4), a("b0", 88, 100), 1.0 - 17 * 116, Op.add, 257.0, Op.min)
         act(a("M"), ind(a("MT"), co(4)))
         cp(a("EF"), a("b4", 192, 384))
         lowest("EQ", "EF", "b6", 0)
@@ -535,44 +555,43 @@ def rank_program(g, core, T, topo):
         ts(a("FL", 0, 192), a("b5", 0, 192), -255.5, Op.is_lt)
         either()
         tr(a("TZ"), a("FL", 0, 192))
+        tt(sm(7, 2), a("TZ", 0, 192, 8), a("NZ", 2, 192, 8), Op.mult)
+        tt(a("BO", ao, ao + 24), sm(7, 2), a("BI", ao, ao + 24), Op.add)
         tt(a("UU"), a("b2", 192, 384), a("FL", 0, 192), Op.mult)
         mm([(a("b0", 256, 448), a("ID"), a("WH", 0, 192)), (a("b0", 256, 448), a("ID"), a("UU"))])
-        act(a("OUT", MW * t, MW * t + 192), a("b0", 256, 448))
-        tt(sm(7), rowz("TZ", 0), sm(6), Op.mult)
-        tt(sm(8), rowz("TZ", 0), rowz("NZ", 2), Op.mult)
-        tt(a("OUT", MW * t + 192, MW * t + 216), sm(7, 2), a("D", ao, ao + 24), Op.add)
+        act(a("OUT", NT * t, NT * t + 192), a("b0", 256, 448), bias=0.0 if last else LIFT)
         dst = T.cores[(rank + 1) % N if not last else (rank - t) % N]
         rid, pid = topo.addr(dst, core)
         eng = topo.engines(core, dst)[:8]
-        for lo, hi, arr in ((192, MW, "arr%d" % t), (0, 192, "arz%d" % t)):
-            src, land = a("OUT", MW * t + lo, MW * t + hi), a("D", zo + MW + lo, zo + MW + hi)
+        for src, land, arr in ((a("BO", ao, ao + 24), a("BI", ao + 24, ao + 48), "arr%d" % t),
+                               (a("OUT", NT * t, NT * t + 192), zof(t + 1), "arz%d" % t)):
             put("g", [src], [land], lambda src=src, land=land, arr=arr, pid=pid, rid=rid, eng=eng: g.remote_dma(
                 land[0], src[0], T.sem[arr], T.sem.snt, pid, rid, sum(1 << e for e in eng)), 500.0, arr, len(eng), lat=REM - 500)
         sg = a("FL", 192, 384)
-        mm([(a("b6", 256, 448), a("BD"), a("WH", 384, 576)), (a("b6", 256, 448), a("BDN"), a("M"))])
-        sact(sg, a("b6", 256, 448), Fn.Sign, bias=a("LIM", 1, 2), scale=-1.0, acc=a("LIM", 4, 5))
-        mm([(a("b1", 256, 448), a("I13"), a("M"))], False, False)
-        mm([(a("b1", 256, 448), a("I12"), sg)], False, True)
-        act(a("Q1"), a("b1", 256, 448), Fn.Relu, bias=float(wide - 20480))
+        fill(a("LT"), lim(1))
+        near = [("BDP", a("LT")), ("BDN", a("WH", 384, 576))]
+        mm([(a("b4", 0, 192), a(w), x) for (w, x) in near])
+        mm([(a("b1", 256, 448), a("I13"), a("M"))], False, True)
+        act(a("Q1", 192, 384), a("b1", 256, 448), bias=float(wide - 16384))
+        tt(a("Q1", 0, 192), a("b4", 0, 192), a("Q1", 192, 384), Op.min)
         if t:
             act(a("VF"), key, Fn.Relu, bias=-VOID - SOME)
-            mm([(a("b3", 192, 384), a("ID"), a("VF")), (a("b3", 192, 384), a("I13"), a("M"))])
+            mm([(a("b3", 192, 384), a("I9"), a("VF")), (a("b3", 192, 384), a("I13"), a("M"))])
             tt(a("U1"), a("b3", 192, 384), a("OD"), Op.min)
-            tt(ind(a("CH", 0, 448), a("BL", 12, 24)), a("U1"), a("Q1"), Op.max)
-        else:
-            cp(ind(a("CH", 0, 448), a("BL", 12, 24)), a("Q1"))
-        act(a("CHH"), a("CH", 0, 256))
-        dma("y", a("JF", 0, 4096, p=row(0)), a("CHH"), "d46")
-        if LOV:
-            tt(a("CHL"), a("CH", 0, 256), a("CHH"), Op.subtract)
-        else:
-            mm([(a("b3", 256, 512), a("IDF"), a("CH", 0, 256))], True, False)
-            mm([(a("b3", 256, 512), a("NID"), a("CHH"))], False, True)
-            act(a("CHL"), a("b3", 256, 512))
-        dma("y", a("JF", 0, 4096, p=row(1)), a("CHL"), "d47")
+        tt(ind(a("CH", 0, 448), a("BL", 12, 24)), a("U1") if t else a("YB", 192, 384), a("Q1", 0, 192), Op.max)
+        for lo, hi in ((0, LOW), (LOW, 256)):
+            act(a("CHH", lo, hi), a("CH", lo, hi))
+        dma("y", a("JF", 0, 4096, p=row(0)), a("CHH"), "dh")
+        tt(a("CHL", 0, LOW), a("CH", 0, LOW), a("CHH", 0, LOW), Op.subtract)
+        mm([(a("b3", 256 + LOW, 512), a("IDF"), a("CH", LOW, 256))], True, False)
+        mm([(a("b3", 256 + LOW, 512), a("NID"), a("CHH", LOW, 256))], False, True)
+        act(a("CHL", LOW, 256), a("b3", 256 + LOW, 512))
+        dma("y", a("JF", 0, 4096, p=row(1)), a("CHL"), "dl")
+        mm([(a("b6", 256, 448), a(w), x) for (w, x) in near + [("BDM", a("M")), ("INF", a("NF"))]])
+        sact(sg, a("b6", 256, 448), Fn.Sign, bias=-18 * 2.0 ** 22 - 2048, acc=lim(4))
         mm([(a("b4", 0, 192), a(w), x) for (w, x) in (
-            ("ID", z), ("ID", de), ("IDH", df), ("IDH", a("WH", 384, 576)), ("I8", sg))])
-        act(a("X", 192 + wide, 192 + wide + 192), a("b4", 0, 192), Fn.Relu, bias=-256.0)
+            ("ID", z), ("ID", de), ("IDH", df), ("IDH", a("WH", 384, 576)), ("I9", sg))])
+        act(a("XO" if last else "X", 192 + wide, 384 + wide), a("b4", 0, 192), Fn.Relu, bias=-512.0 - 2 * LIFT * last)
         if not last:
             if t:
                 mm([(a("b4", 192, 384), a("LN%d" % j), a("GE", 192 * j, 192 * j + 192)) for j in range(2)])
@@ -580,53 +599,57 @@ def rank_program(g, core, T, topo):
                 mm([(a("b4", 192, 384), w, a("NE", 192 * j, 192 * j + 192))
                     for (w, j) in ((band("B0", 0), 0), (band("BM", 3), 0), (band("B0", 3), 1))])
             act(a("EN", wide, wide + 192), a("b4", 192, 384), bias=col(11))
-            act(a("LIM", 3, 4), a("LIM", 4, 5), bias=a("LIM", 3, 4), scale=4.0)
-            act(a("IB", 12, 13), a("LIM", 3, 4), bias=a("LIM", 5, 6), scale=1.0 / 256)
-            act(a("LIM", 1, 2), a("IB", 12, 13), bias=a("LIM", 3, 4), scale=-256.0)
-        else:
-            kind[0] += 5
+            act(lim(3), lim(4), bias=lim(3), scale=col(15))
+            act(a("IB", 12, 13), lim(3), bias=1.0 / 64 - 0.5, scale=1.0 / 256)
+            act(lim(1), a("IB", 12, 13), bias=lim(3), scale=col(16))
         mm([zero("b6", 12, 12)] + swap("b6", 12, 0, "TZ", 0, 16))
         tt(sm(11), a("b6", 12, 24), sm(2), Op.mult)
         tt(sm(12), sm(11), a("II", 0, 12), Op.add)
         cp(a("LX", 12 * t, 12 * t + 12), sm(12))
-        if 1 <= t < NS - 2:
-            ts(a("LW"), a("EF"), 2047.5, Op.is_gt, MARK, Op.mult)
-        elif t:
-            kind[0] += 1
-        if t >= 1:
-            numbers(t - 1, t, "LW" if 2 <= t < NS - 1 else None, FREE)
-        if t >= 3:
-            numbers(t - 2, t, None, FREE)
-        elif t:
-            kind[0] += len(FREE) - 1
-        numbers(t, t, None if last else "CM", (0, 12))
+        if t < NS - 2:
+            mm([(a("b7", 256, 448), a("ID"), z), (a("b7", 256, 448), a("BDS"), a("NE", 0, 192))])
+            act(a("ZL"), a("b7", 256, 448))
+        if 1 <= t and not last:
+            numbers(t - 1, wide, "ZL", 0, 1, FREE)
+        if 3 <= t and not last:
+            act(a("ZM", 192, 384), zof(t - 2), bias=LIFT)
+            numbers(t - 2, wide, "ZM", 192, 0, FREE)
+        if not last:
+            act(a("ZM", 0, 192), z, bias=2 * LIFT)
+            numbers(t, wide, "ZM", 0, 0, (0, 12))
         if t == 0:
-            mm(pick("b7", 256, "B03", "GH", 0, 256))
-            act(a("HSK"), a("b7", 256, 512))
-            mm([(a("b1", 0, 256), a("DUP", 0, 128), a("HSK"))])
-            mm([(a("b1", 256, 512), a("DUP", 128, 256), a("HSK"))])
-            act(a("HS2"), a("b1"))
             act(a("OWN"), a("OWN"), bias=col(6))
-            tt(a("OWN"), a("b7", 256, 512), a("OWN"), Op.not_equal)
-            mm([(a("b7", 256, 512), a("IDF"), a("SBF")), (a("b7", 256, 512), a("I13F"), a("OWN"))])
-            act(a("SKT", 0, 256), a("b7", 256, 512))
-            mm(pick("b4", 0, "B5", "GH", 0, 256))
-            act(a("PK"), a("b4", 0, 256))
+            for lo in (0, 128):
+                mm(pick("b6", 128 + lo, "B03", "GH", 16 * lo, 128))
+                act(a("HSK", lo, lo + 128), a("b6", 128 + lo, 256 + lo))
+                for be in range(2):
+                    mm([(a("b7", 256 + 128 * be, 384 + 128 * be), a("DUP", 128 * be, 128 * be + 128), a("HSK", lo, lo + 128))])
+                    act(a("HS2", 256 * be + lo, 256 * be + lo + 128), a("b7", 256 + 128 * be, 384 + 128 * be))
+                mm(pick("b4", lo, "B5", "GH", 16 * lo, 128))
+                act(a("PK", lo, lo + 128), a("b4", lo, lo + 128))
             dma("y", a("JF", 0, 4096, p=row(5)), a("PK"))
+            tt(a("MA", 0, 256), a("b6", 128, 384), a("OWN"), Op.not_equal)
+            mm([(a("b7", 256, 512), a(w), x) for (w, x) in (("ID", a("SBH")), ("ID", a("SBL")), ("I13", a("MA", 0, 256)))])
+            act(a("SKT", 0, 256), a("b7", 256, 512))
 
+    for lo in range(192, 192 + wide, 400):
+        act(a("XT", lo, lo + 400), a("X", lo, lo + 400), bias=128 - 2 * LIFT)
+        act(a("XO", lo, lo + 400), a("XT", lo, lo + 400), Fn.Relu, bias=-128.0)
+    for t in range(NS - 3, NS):
+        tt(ind(a("XO", 0, 192 + wide), a("LX", 12 * t, 12 * t + 12)), zof(t), a("CM"), Op.add)
+    for h in range(4):
+        dma("y", hbm(T.yx[:, 848 * h:848 * h + 848]), a("XO", 192 + 848 * h, 192 + 848 * h + 848), None, 3000.0)
     mm([(a("b7", 256, 384), band("B03", r), a("HT", 128 * r, 128 * r + 128)) for r in range(16)])
     cp(a("HL"), a("b7", 256, 384))
     for h in range(4):
-        dma("y", hbm(T.yx[:, 848 * h:848 * h + 848]), a("X", 192 + 848 * h, 192 + 848 * h + 848), None, 3000.0)
-    act(a("G", 0, 1024), ind(a("JF"), a("HL", 0, 64)))
-    cp(a("G", 1024, 2048), ind(a("JF"), a("HL", 64, 128)))
-    fin = NR + MW * NS
-    dma("y", hbm(T.yz[:]), a("D", fin, fin + 192))
-    tt(rowz("YB", 0, 192), a("D", fin + 192, fin + 204), a("CZ"), Op.add)
-    mm(pick("b1", 0, "B03", "G", 0, 128))
+        act(a("G", 512 * h, 512 * h + 512), ind(a("JF"), a("HL", 32 * h, 32 * h + 32)))
+    dma("y", hbm(T.yz[:]), zof(NS))
+    tt(rowz("YB", 0, 192), a("BI", 24 * NS + 1, 24 * NS + 24, 2), a("CZ"), Op.add)
+    for h in range(2):
+        mm(pick(("b4", "b6")[h], 0, "B03", "G", 1024 * h, 64))
+        act(a("YJ", 64 * h, 64 * h + 64), a(("b4", "b6")[h], 0, 64))
     tr(a("YB", 0, 192), a("YB", 192, 384))
     dma("s", hbm(T.yb[:]), a("YB", 0, 192, p=row(0)))
-    cp(a("YJ"), a("b1", 0, 128))
     dma("y", hbm(T.yj[:]), a("YJ"))
 
     def clash(r, s):
@@ -664,36 +687,32 @@ def rank_program(g, core, T, topo):
     for i in range(n):
         for j in deps[i]:
             kids[j].append(i)
-    kd = [o["k"] for o in ops]
-    full = [o["c"] + o["lat"] + LAT for o in ops]
+
+    names, count, kd = {}, {}, []
+    for i, o in enumerate(ops):
+        t = sum(i >= b for b in begin) - 1
+        what = (o["e"], "alt" in o, tuple(r[0] for r in o["w"][:1] + o["r"][:2]))
+        count[t, what] = count.get((t, what), 0) + 1
+        kd.append(names.setdefault((min(max(t, 0), 1) + (t == NS - 1), what, count[t, what] if t > 0 else i), len(names)))
+    kinds = len(names)
     tail = [o["lat"] + LAT for o in ops]
     forms = [[(o["e"], o["c"])] + ([(o["alt"]["e"], o["alt"]["c"])] if "alt" in o else []) for o in ops]
     banks = [o["bk"] for o in ops]
     cont = [o["cont"] for o in ops]
     pad = LAT + 70.0
 
-    kinds = max(kd) + 1
-    way = [0.0] * n
-
-    def lay(lean, lo, hi, goal, bound):
-        for i in range(hi - 1, lo - 1, -1):
-            w = 0.0
-            for k in kids[i]:
-                if way[k] > w:
-                    w = way[k]
-            way[i] = w + full[i] + lean[kd[i]]
-        order = sorted(range(lo, hi), key=lambda i: -way[i] - lean[kinds + kd[i]])
-        left = [0] * n
-        for i in range(lo, hi):
-            for k in kids[i]:
-                left[k] += 1
+    def lay(lean):
+        way = [0.0] * n
+        for i in range(n - 1, -1, -1):
+            way[i] = max([way[k] for k in kids[i]], default=0.0) + forms[i][0][1] + tail[i] + lean[kd[i]]
+        order = sorted(range(n), key=lambda i: -way[i])
+        left = [len(p) for p in deps]
         at = [0.0] * n
-        st = [0.0] * n
         form = [0] * n
         busy = {k: [] for k in list(Q) + ["b%d" % b for b in range(8)]}
         done = [False] * n
         low, span = 0, 0.0
-        for turn in range(lo, hi):
+        for turn in range(n):
             while done[order[low]]:
                 low += 1
             j = low
@@ -706,144 +725,137 @@ def rank_program(g, core, T, topo):
                 s0 = at[i]
                 moved = True
                 while moved:
-                    lst = busy[e]
-                    j = len(lst)
-                    while j and lst[j - 1][1] > s0:
-                        j -= 1
-                    while j < len(lst) and lst[j][0] < s0 + c:
-                        s0 = lst[j][1]
-                        j += 1
                     moved = False
-                    for b in banks[i]:
+                    for (b, gap) in [(e, 0.0)] + [(b, pad) for b in banks[i]]:
                         lst = busy[b]
                         j = len(lst)
-                        while j and lst[j - 1][1] + pad > s0:
+                        while j and lst[j - 1][1] + gap > s0:
                             j -= 1
-                        while j < len(lst) and lst[j][0] - pad < s0 + c:
-                            if lst[j][2] != e and s0 < lst[j][1] + pad:
-                                s0 = lst[j][1] + pad
+                        while j < len(lst) and lst[j][0] - gap < s0 + c:
+                            if (b == e or lst[j][2] != e) and s0 < lst[j][1] + gap:
+                                s0 = lst[j][1] + gap
                                 moved = True
                             j += 1
-                w = s0 + c + (lean[2 * kinds + kd[i]] if f else 0.0)
-                if found is None or w < found[0]:
-                    found = (w, s0, f, e, c)
-            w, s0, f, e, c = found
-            st[i], form[i] = s0, f
-            for key in [e] + banks[i]:
-                lst = busy[key]
+                if found is None or s0 + c + WISH < found[0] + found[3]:
+                    found = (s0, f, e, c)
+            s0, f, e, c = found
+            at[i], form[i] = s0, f
+            for b in [e] + banks[i]:
+                lst = busy[b]
                 j = len(lst)
                 while j and lst[j - 1][0] > s0:
                     j -= 1
                 lst.insert(j, (s0, s0 + c, e))
-            end = s0 + c + tail[i]
-            if i == goal:
-                return (end, st, form) if end <= bound else None
-            if end > span:
-                span = end
-                if span > bound and goal < 0:
-                    return None
+            span = max(span, s0 + c + tail[i])
             for k in kids[i]:
-                w = s0 + c if e == "t" and cont[k] else end
-                if at[k] < w:
-                    at[k] = w
+                at[k] = max(at[k], s0 + c + (0.0 if e == "t" and cont[k] else tail[i]))
                 left[k] -= 1
-        return span, st, form
+        return span, at, form
 
-    def seek(lean, lo, hi, goal, some, turns, rng):
-        lay(lean, 0, n, 0, 1e9)
-        now = best = (lay(lean, lo, hi, goal, 1e9)[0], lean)
-        for turn in range(turns):
-            new = list(now[1])
-            for j in range(1 + turn % 4):
-                new[some[rng.randint(len(some))] + kinds * rng.randint(3)] += float(rng.normal()) * SIG * (0.1 + rng.rand() ** 2)
-            got = lay(new, lo, hi, goal, now[0] - HEAT * (1 - turn / turns) ** 2 * float(np.log(rng.rand())))
-            if got:
-                now = (got[0], new)
-                if now[0] < best[0]:
-                    best = now
-        return best[1]
+    rooms = list(Q) + ["b%d" % b for b in range(8)]
+    job = [[(rooms.index(e), c, [rooms.index(b) for b in banks[i]], c + tail[i],
+             [(k, c if e == "t" and cont[k] else c + tail[i]) for k in kids[i]]) for (e, c) in forms[i]] for i in range(n)]
+    kda = np.array(kd)
 
-    def run(rank, alt, base):
-        order = sorted(range(n), key=lambda i: base[i] + rank[kd[i]])
-        left = [len(p) for p in deps]
+    def run(place, alt, base, lo, hi, left):
+        order = (np.argsort(base[lo:hi] + place[kda[lo:hi]], kind="stable") + lo).tolist()
+        left = list(left)
         at = [0.0] * n
         why = [-1] * n
-        held = [False] * n
-        free = {k: (0.0, -1, k) for k in list(Q) + ["b%d" % b for b in range(8)]}
+        held = set()
+        till, who, by = [0.0] * len(rooms), [-1] * len(rooms), [-1] * len(rooms)
         wait = []
         span = tip = 0
-        for i0 in order:
-            wait.append(i0)
-            j = len(wait) - 1
-            while j >= 0:
-                i = wait[j]
-                if left[i]:
-                    j -= 1
-                    continue
-                del wait[j]
-                e, c = forms[i][alt[kd[i]]]
+        for i in order:
+            if left[i]:
+                wait.append(i)
+                continue
+            while i >= 0:
+                e, c, bks, full, after = job[i][alt[kd[i]]]
                 s0 = at[i]
-                f = free[e]
-                if f[0] > s0:
-                    s0, why[i], held[i] = f[0], f[1], True
-                for b in banks[i]:
-                    f = free[b]
-                    if f[2] != e and f[0] + pad > s0:
-                        s0, why[i], held[i] = f[0] + pad, f[1], True
+                if till[e] > s0:
+                    s0, why[i] = till[e], who[e]
+                    held.add(i)
+                for b in bks:
+                    if by[b] != e and till[b] + pad > s0:
+                        s0, why[i] = till[b] + pad, who[b]
+                        held.add(i)
                 at[i] = s0
-                f = free[e] = (s0 + c, i, e)
-                for b in banks[i]:
-                    free[b] = f
-                end = s0 + c + tail[i]
-                if end > span:
-                    span, tip = end, i
-                for k in kids[i]:
-                    w = s0 + c if e == "t" and cont[k] else end
-                    if at[k] < w:
-                        at[k], why[k] = w, i
+                till[e], who[e] = s0 + c, i
+                for b in bks:
+                    till[b], who[b], by[b] = s0 + c, i, e
+                if s0 + full > span:
+                    span, tip = s0 + full, i
+                for k, w in after:
+                    if at[k] < s0 + w:
+                        at[k], why[k] = s0 + w, i
                     left[k] -= 1
-                j = len(wait) - 1
+                i = -1
+                for j in range(len(wait)):
+                    if not left[wait[j]]:
+                        i = wait.pop(j)
+                        break
         pairs = []
         while tip >= 0:
-            if held[tip]:
+            if tip in held:
                 pairs.append((tip, why[tip]))
             tip = why[tip]
-        return span, at, [alt[k] for k in kd], pairs
+        return span, at, place, alt, pairs
 
-    def tune(got, turns, rng):
-        sends = [0.0] + [got[1][i] for i in range(n) if ops[i]["sem"][:3] == "arr"]
-        base = [0.0] * n
-        for t in range(1, NS):
-            for i in range(begin[t], begin[t + 1] if t + 1 < NS else n):
-                base[i] = sends[t]
-        rank, alt = [0.0] * kinds, [0] * kinds
-        for i in list(range(n)) + list(range(begin[4], begin[5])):
-            rank[kd[i]], alt[kd[i]] = got[1][i] - base[i], got[2][i]
-        now = best = run(rank, alt, base)
-        for turn in range(turns):
-            i, j = now[3][rng.randint(len(now[3]))]
-            r, f, how = list(rank), list(alt), rng.randint(6)
-            if how == 0 and len(forms[i]) > 1:
+    def tune(place, alt, base, lo, hi, some, turns, heat, rng):
+        left = [sum(j >= lo for j in p) for p in deps]
+        now = best = run(place, alt, base, lo, hi, left)
+        for turn, u in enumerate(rng.rand(turns, 5).tolist()):
+            i, j = now[4][int(u[0] * len(now[4]))]
+            way = 1.0
+            if u[1] < 0.5:
+                i, j, way = j, i, -1.0
+            r, f = now[2].copy(), now[3]
+            to = base[j] + r[kd[j]] - way * (1.0 + SIG * u[2] ** 4)
+            if turn % 3 == 0:
+                i = lo + int(u[0] * (hi - lo))
+                to = base[i] + r[kd[i]] - way * 4 * SIG * u[2] ** 2
+            if kd[i] not in some:
+                continue
+            if len(forms[i]) > 1 and u[3] < 0.3:
+                f = list(f)
                 f[kd[i]] ^= 1
-            elif how == 1 and len(forms[j]) > 1:
-                f[kd[j]] ^= 1
-            elif how % 2:
-                r[kd[i]] = base[j] + rank[kd[j]] - base[i] - 1.0 - SIG * rng.rand() ** 4
             else:
-                r[kd[j]] = base[i] + rank[kd[i]] - base[j] + 1.0 + SIG * rng.rand() ** 4
-            new = run(r, f, base)
-            if new[0] <= now[0] - HEAT * (1 - turn / turns) ** 2 * float(np.log(rng.rand())):
-                now, rank, alt = new, r, f
+                more = [(i, to)]
+                while more:
+                    i, to = more.pop()
+                    r[kd[i]] = to - base[i]
+                    more += [(j, to - way) for j in (deps if way > 0 else kids)[i]
+                             if lo <= j < hi and kd[j] in some and (base[j] + r[kd[j]] - to) * way > 0 and base[i] == base[j]]
+            new = run(r, f, base, lo, hi, left)
+            if new[0] <= now[0] - heat * (1 - turn / turns) ** 2 * float(np.log(u[4])):
+                now = new
                 if now[0] < best[0]:
                     best = now
         return best
 
     if not PLAN:
         rng = np.random.RandomState(SEED)
-        lean = seek([0.0] * (2 * kinds) + [WISH] * kinds, 0, n, -1, list(range(kinds)), TURNS // 20, rng)
-        best = tune(lay(lean, 0, n, -1, 1e9), TURNS, rng)
+        lean = [0.0] * kinds
+        best = lay(lean)
+        for turn in range(TURNS // 200):
+            new = list(lean)
+            for k in rng.randint(0, kinds, 1 + turn % 4):
+                new[k] += float(rng.normal()) * SIG
+            got = lay(new)
+            if got[0] <= best[0]:
+                best, lean = got, new
+        sends = [0.0] + [best[1][i] for i in range(n) if ops[i]["sem"][:3] == "arr"]
+        base = np.array([sends[max(sum(i >= b for b in begin) - 1, 0)] for i in range(n)])
+        place, alt = np.zeros(kinds), [0] * kinds
+        for i in list(range(n)) + list(range(begin[3], begin[5])):
+            place[kd[i]], alt[kd[i]] = best[1][i] - base[i], best[2][i]
+        for lo, hi, k0, k1, turns, heat in ((begin[2], begin[6], begin[1], begin[6], TURNS, HEAT), (0, begin[2], 0, begin[1], TURNS, HEAT),
+                                            (begin[5], n, begin[6], n, TURNS // 3, HEAT / 2), (0, n, 0, n, TURNS // 4, HEAT / 4)):
+            best = tune(place, alt, base, lo, hi, set(kd[k0:k1]), turns, heat, rng)
+            place, alt = best[2], best[3]
         PLAN.append(sorted(range(n), key=lambda i: (best[1][i], i)))
-        PLAN.append(best[2])
+        PLAN.append([alt[k] for k in kd])
         PLAN.append(best[0])
     for i in range(n):
         if PLAN[1][i]:

import numpy as np
from concourse.mybir import AluOpType as Op, ActivationFunctionType as Fn

NV, NB, NT, NS = 2048, 256, 192, 7
NR = 16 * NT
NX = 192 + NV + NT * NS
F32, BF, I32, U16 = "float32", "bfloat16", "int32", "uint16"
_S = {
    "X": (NX, F32), "XO": (NX, BF), "XT": (NX, BF), "JF": (6144, BF), "EN": (3392, BF), "CH": (456, F32), "CHH": (256, BF), "CHL": (256, BF),
    "SBI": (256, I32), "SBF": (256, F32), "SBU": (256, U16), "SB2": (512, F32), "HS2": (512, F32), "SKT": (456, F32),
    "HSK": (256, F32), "HT": (2048, BF), "SIO": (2048, F32), "GH": (4096, BF), "HEL": (128, U16), "HL": (128, U16),
    "OH": (2048, BF), "SBH": (256, BF), "SBL": (256, BF), "PK": (256, BF), "OWN": (256, F32),
    "OUT": (7 * NT, BF), "BI": (8 * 24, BF), "BO": (7 * 24, BF), "LX": (7 * 12, U16), "MT": (272, BF), "MA": (512, BF),
    "G": (NR + 7 * NT, BF), "D": (NR + 8 * NT, BF), "AB": (NR, BF), "EQ": (2304, BF), "ES": (2304, BF),
    "PI": (2, I32), "PJ": (2, I32), "COL": (24, F32), "IM": (144, F32), "IMP": (128, F32), "IG": (128, F32),
    "BD": (128, BF), "BDF": (128, F32), "ID": (128, BF), "IDS": (6 * 128, BF), "IFS": (4 * 128, F32),
    "ZR": (256, BF), "ONE": (192, BF), "BB": (144, BF), "BND": (13 * 144, BF), "MX": (11 * 128, BF), "W1": (128, BF),
    "IO": (456, BF), "DG": (2048, BF), "RC": (192, BF), "LT": (192, BF),
    "R16": (16, F32), "WD": (32, F32), "SW": (4 * 512, BF), "DUP": (256, F32), "IB": (16, BF), "CZ": (12, BF),
    "RO": (12, U16), "RS": (384, F32), "NI": (192, BF), "II": (36, F32), "CM": (192, BF),
    "T1": (60, F32), "T2": (12, I32), "PEI": (128, I32), "HEI": (128, I32), "DQ": (128, BF),
    "PEB": (128, BF), "HEB": (128, BF), "HIC": (128, BF), "LOC": (128, BF), "BXI": (192, I32), "BXB": (192, BF),
    "LMI": (2, I32), "LMF": (2, F32), "LIM": (8, F32), "AI": (8, I32),
    "LM": (12, U16), "HK": (192, F32), "HR": (192, F32), "L1": (192, U16), "CL": (192, U16), "KR": (192, F32),
    "TM": (192, F32), "A32": (72, I32), "U1": (192, F32), "Q1": (384, F32), "VF": (192, BF), "ZZ": (768, BF),
    "YJ": (128, F32), "YB": (384, F32), "GE": (384, BF), "AF": (192, BF), "EF": (192, U16),
    "NZ": (384, BF), "TZ": (192, BF), "FZ": (192, BF), "ZM": (384, F32),
    "NF": (192, BF), "CO": (60, U16), "DE": (384, BF), "EL": (24, U16), "BL": (24, U16), "NE": (384, BF), "SM": (192, F32),
    "KK": (120, BF), "WH": (576, BF), "FL": (384, BF), "UU": (192, BF), "OD": (192, F32), "SK": (192, F32), "ZL": (192, F32),
    "M": (192, BF), "BX": (12, BF),
}
TWICE = ("NF", "CO", "DE", "EL", "BL", "NE", "SM", "KK", "WH", "FL", "UU", "OD", "SK", "ZL", "M", "BX")
SCRATCH = {k: ("sbuf", [128, w * (2 if k in TWICE else 1)], d) for k, (w, d) in _S.items()}
for _b in range(8):
    SCRATCH["b%d" % _b] = ("psum", [128, 512], F32)
SEMAPHORES = (["cv", "cs", "ct", "cg", "snt", "dh", "dl"] + ["ar%s%d" % (k, i) for k in "rz" for i in range(NS)]
              + ["d%d" % i for i in range(56)])
CHAINED = ("b0", "b1", "b2", "b3", "b5")

LIFT = 192.0
SPLIT, SOME, VOID = 1023.5, 2048.0, 8192.0
IDS = {"NID": -1.0, "IDH": 0.5, "E01": -2 * LIFT, "I13": 8192.0, "I9": 512.0, "INF": -2.0 ** 23}
IFS = {"IDF": 1.0, "NIF": -1.0, "IDQ": 2.0 ** -21}
MXS = ("LO", "LE", "LN0", "LN1", "BD3", "BDN", "BDP", "BDM", "BDS", "WC")
BANDS = ("B0", "B1", "B03", "BAL", "BK", "BN", "BP", "BC", "BE", "BEP", "B5", "BM")
SCALES = (1.0, 32.0, 512.0, 6144.0)
CY, GA, SCA, PE, LAT, DMA, REM = 0.95, 1.56, 3.8, 0.5, 130.0, 2300.0, 2500.0
TURN = (0, 4, 12)
FREE = (0, 6, 12)
LOOKS = (0, 2, 4, 6, 8, 12, 16)
PICKS = (0, 2, 8, 12, 16)
DIFF = (0, 2, 4, 8, 12, 15, 16)
ABS = (0, 2, 4, 8, 12, 14, 15, 16)
LOW = 160
WIDE = max(k1 - k0 for k0, k1 in zip(DIFF, DIFF[1:]))
TURNS, SIG, SEED = 65000, 1500.0, 1
WISH, HEAT = 800.0, 100.0
PLAN = []


def rank_program(g, core, T, topo):
    rank = T.rank_of(core)
    if rank is None:
        return
    N = len(T.cores)
    Q = {"v": g.vector, "s": g.scalar, "t": g.tensor, "g": g, "y": g.sync}
    own = {"v": "cv", "s": "cs", "t": "ct", "g": "cg"}
    ops = []
    nd = [0]
    par = [0]

    def a(name, lo=0, hi=None, st=1, p=None, old=0):
        for (buf, names) in (("IDS", list(IDS)), ("IFS", list(IFS)), ("MX", MXS)):
            if name in names:
                j = names.index(name)
                return a(buf, 128 * j, 128 * j + 128)
        if name in BANDS:
            j = BANDS.index(name)
            return a("BND", 144 * j + lo, 144 * j + (144 if hi is None else hi))
        w = _S[name][0] if name in _S else 512
        if hi is None:
            hi = w
        if name in TWICE:
            lo, hi = lo + w * (par[0] ^ old), hi + w * (par[0] ^ old)
        ps = slice(None) if p is None else p
        ap = T[name][ps, lo:hi] if st == 1 else T[name][ps, lo:hi:st]
        reg = (name, 0, 512, None) if name in CHAINED else (name, lo, hi, None if p is None else p.start)
        return (ap, [reg], [], (hi - lo + st - 1) // st)

    def ind(win, off):
        return (win[0].indirect(off[0]), win[1], off[1], 16 * off[3])

    def val(x):
        return x[0] if isinstance(x, tuple) else x

    def psum(x):
        return x[1][0][0][0] == "b"

    def two(x):
        return not psum(x) and _S[x[1][0][0]][1] in (BF, U16)

    def put(e, reads, writes, call, cost, sem=None, n=1, cont=False, lat=0.0):
        rs, ws = [], []
        for x in reads:
            if isinstance(x, tuple):
                rs += x[1] + x[2]
        for x in writes:
            ws += x[1]
            rs += x[2]
        ops.append({"e": e, "r": rs, "w": ws, "call": call, "c": cost, "sem": sem or own[e], "n": n, "cont": cont, "lat": lat})

    def vcost(out, x, per):
        if out[2]:
            return 50 + out[3] * SCA * CY
        if x[2]:
            return 60 + out[3] * GA * CY
        return max(64, out[3] * per) * CY

    def cp(out, x):
        put("v", [x], [out], lambda: g.vector.tensor_copy(out[0], x[0]), vcost(out, x, 0.5 if two(out) and two(x) else 1))

    def tt(out, x, y, o):
        put("v", [x, y], [out], lambda: g.vector.tensor_tensor(out[0], x[0], y[0], o), vcost(out, x, 1 if psum(x) or psum(y) else 2))

    def ts(out, x, s1, o1, s2=None, o2=None):
        c = vcost(out, x, 0.5 if two(out) and two(x) else 1)
        if o2 is None:
            put("v", [x, s1], [out], lambda: g.vector.tensor_scalar(out[0], x[0], val(s1), None, o1), c)
        else:
            put("v", [x, s1, s2], [out], lambda: g.vector.tensor_scalar(out[0], x[0], val(s1), val(s2), o1, o2), c)

    def ms(out, c):
        put("v", [], [out], lambda: g.vector.memset(out[0], c), vcost(out, out, 0.5 if two(out) else 1))

    def tr(out, x):
        put("v", [x], [out], lambda: g.vector.transpose(out[0], x[0]), vcost(out, x, 0.5 if two(out) else 1))

    def scan(out, d0, d1):
        put("v", [d0, d1], [out], lambda: g.vector.tensor_tensor_scan(out[0], d0[0], d1[0], 0.0, Op.max, Op.min), vcost(out, d1, 1))

    def sact(out, x, f=Fn.Identity, bias=0.0, scale=1.0, acc=None):
        if out[2]:
            put("s", [x], [out], lambda: g.scalar.activation(out[0], x[0], f), vcost(out, x, 1) + 15)
        elif acc is None:
            put("s", [x, bias, scale], [out], lambda: g.scalar.activation(out[0], x[0], f, bias=val(bias), scale=val(scale)), vcost(out, x, 1))
        else:
            put("s", [x, bias, scale], [out, acc], lambda: g.scalar.activation(
                out[0], x[0], f, bias=val(bias), scale=val(scale), accum_out=acc[0]), vcost(out, x, 1) + 20)

    def either():
        o = ops.pop()
        ops[-1]["alt"] = {k: o[k] for k in ("e", "call", "c", "sem")}
        ops[-1]["r"] = ops[-1]["r"] + o["r"]

    def act(out, x, f=Fn.Identity, bias=0.0, scale=1.0):
        sact(out, x, f, bias, scale)
        if f == Fn.Identity and bias == 0.0 and scale == 1.0:
            cp(out, x)
        elif f == Fn.Identity:
            ts(out, x, scale, Op.mult, bias, Op.add)
        elif f == Fn.Relu and scale == 1.0:
            ts(out, x, bias, Op.add, 0.0, Op.max)
        else:
            return
        either()

    def over(out, x, c):
        sact(out, x, Fn.Sign, -c)
        ts(out, x, c + 0.5, Op.is_gt)
        either()

    def gcp(out, x):
        put("g", [x], [out], lambda: g.affine_select(out[0], x[0], [[0, x[3]]], Op.is_ge, 0.0, 0, 0), 170 + 2 * CY * out[3])

    def diag(out, c):
        act(out, a("ID"), scale=c)
        o = ops.pop()
        x = a("ZR", 0, 128)
        put("g", [x], [out], lambda: g.affine_select(out[0], x[0], [[-1, 128]], Op.not_equal, c, 0, 1), 170 + 2 * CY * 128)
        ops.append({**o, **o["alt"]})
        either()

    def iota(out, pat, base=0, ch=0):
        if _S[out[1][0][0]][1] == I32:
            put("g", [], [out], lambda: g.iota(out[0], pat, base, ch), 130 + 2 * CY * out[3])
        else:
            put("g", [], [out], lambda: g.iota(out[0], pat, base, ch, allow_small_or_imprecise_dtypes=True), 130 + 2 * CY * out[3])

    def mm(items, start=True, stop=True):
        def call():
            for i, it in enumerate(items):
                ins = g.tensor.matmul(it[0][0], it[1][0], it[2][0], start and i == 0, stop and i == len(items) - 1)
            return ins
        c = sum(max(64, it[2][3]) * PE * (1 if two(it[1]) else 4) for it in items)
        put("t", [x for it in items for x in it[1:]], [it[0] for it in items], call, c, cont=not start, lat=70.0)

    def dma(e, out, x, sem=None, extra=0.0):
        if sem is None:
            sem = "d%d" % nd[0]
            nd[0] += 1
        put(e, [x], [out], lambda: Q[e].dma_start(out[0], x[0]), 60.0, sem, 16, lat=DMA + extra)

    def hbm(ap):
        return (ap, [], [], 0)

    def row(j):
        return slice(j, 128, 16)

    def band(name, r):
        return a(name, 15 - r, 143 - r)

    def zero(bank, lo, n):
        return (a(bank, lo, lo + n), a("ZR", 0, 128), a("ZR", 0, n))

    def pick(bank, lo, bnd, src, slo, n):
        return [(a(bank, lo, lo + n), band(bnd, r), a(src, slo + r, slo + 16 * n, 16)) for r in range(16)]

    def swap(bank, lo, w, src, slo, st=1):
        return [(a(bank, lo + be, lo + 12, 2), a("SW", 512 * w + 256 * be + 128 * ga, 512 * w + 256 * be + 128 * ga + 128),
                 a(src, slo + st * ga, slo + st * 11 + 1, 2 * st)) for be in range(2) for ga in range(2)]

    def lowest(eq, src, sc, cl):
        for c in range(12):
            ts(a(eq, 208 * c, 192 * c + 192), a(src, 16 * c, 192), a(sc, cl + c, cl + c + 1), Op.is_equal)

        def off(cs):
            return [(a("b5", 16 * c + 16, 192), a("BD"), a(eq, 208 * c + 16, 192 * c + 192)) for c in cs]
        mm([zero("b5", 0, 192)], True, False)
        for c0, c1 in ((0, 3), (3, 7), (7, 11)):
            mm(off(range(c0, c1)), False, False)
        mm([(a("b5", r, 192, 16), a("DG", 128 * r, 128 * r + 128), a(eq, r, 208 * 11 + r + 1, 208)) for r in range(16)], False, True)

    def fill(out, c):
        act(out, a("ZR", 0, out[3]), bias=c)

    def msum(out, terms):
        mm([(a("b7", 0, 128), a(w), x) for (w, x) in terms])
        act(out, a("b7", 0, 128))

    def col(j):
        return a("COL", j, j + 1)

    def unit(j):
        return a("R16", j, j + 1)

    def lim(j):
        return a("LIM", j, j + 1)

    def ai(j):
        return a("AI", j, j + 1)

    def sm(j, n=1):
        return a("SM", 12 * j, 12 * (j + n))

    def kk(j, n=1):
        return a("KK", 12 * j, 12 * (j + n))

    def a32(j, n=1):
        return a("A32", 12 * j, 12 * (j + n))

    def co(j):
        return a("CO", 12 * j, 12 * j + 12)

    def rowz(name, k, lo=0):
        return a(name, lo + k, lo + 192, 16)

    def zof(t):
        return a("D", NR + NT * t, NR + NT * t + 192)

    ms(a("BXI"), 0)
    iota(a("LMI"), [[0, 2]])
    dma("y", a("SBI"), hbm(T.sb[:]))
    dma("s", a("HEI"), hbm(T.he[:]))
    dma("y", a("BXI", p=row(0)), hbm(T.bx[:]))
    dma("s", a("PEI"), hbm(T.pe[:]))
    dma("y", a("LMI", p=row(0)), hbm(T.lim[:]))
    dma("y", zof(0), hbm(T.zs[:]))
    for h in range(2):
        dma("y", a("XO", 192 + 1024 * h, 1216 + 1024 * h), hbm(T.xs[:, 1024 * h:1024 * h + 1024]), None, 1200.0 + 1200.0 * h)
    for h in range(4):
        act(a("X", 192 + 512 * h, 704 + 512 * h), a("XO", 192 + 512 * h, 704 + 512 * h), bias=2 * LIFT)
    act(zof(0), zof(0), bias=LIFT)
    ms(a("EN", 0, NV), 1.0)
    for h in range(3):
        dma("y", a("JF", 2048 * h, 2048 * h + 2048), a("XO", 192, 192 + NV), None, 2500.0)

    iota(a("ZR"), [[0, 256]])
    iota(a("ONE"), [[0, 192]], 1)
    iota(a("PI", 0, 1), [[0, 1]], 0, 1)
    iota(a("IM"), [[1, 144]])
    iota(a("IG"), [[1, 8], [0, 16]])
    iota(a("IMP"), [[1, 128]], 0, -1)
    iota(a("II"), [[0, 3], [16, 12]])
    iota(a("W1"), [[0, 8], [1, 16]], -12)
    iota(a("NI"), [[1, 192]])
    iota(a("IO"), [[1, 456]])
    for lo in range(0, NV, 512):
        iota(a("SIO", lo, lo + 512), [[1, 512]], lo)
    iota(a("OWN"), [[1, 256]])
    iota(a("MA", 0, 256), [[0, 16], [1, 16]])
    iota(a("MA", 256, 512), [[1, 16], [0, 16]])
    iota(a("G", NR, NR + 7 * NT), [[0, 7 * NT]], 1)
    ts(a("PJ", 0, 1), a("PI", 0, 1), 15, Op.bitwise_and)
    ts(a("PJ", 1, 2), a("PI", 0, 1), 4, Op.logical_shift_right)
    cp(a("COL", 0, 2), a("PJ"))
    ts(a("PI", 1, 2), a("PJ", 1, 2), 1, Op.bitwise_and)
    cp(col(3), a("PI", 1, 2))
    act(col(2), col(3), bias=1.0, scale=-1.0)
    act(col(4), col(1), bias=15.0, scale=16.0)
    act(col(10), col(0), scale=128.0)
    fill(a("HIC"), col(10))
    iota(a("LOC"), [[1, 128]])
    dma("y", a("JF", 4096, 6144, p=row(0)), a("HIC"))
    dma("y", a("JF", 4096, 6144, p=row(2)), a("LOC"))
    for j in (1, 3, 4):
        dma("y", a("JF", 4096, 6144, p=row(j)), a("ZR", 0, 128))
    ts(a("R16"), a("IM", 0, 16), col(0), Op.is_equal)
    ts(col(5), col(0), 3.5, Op.is_lt)
    act(col(6), col(0), scale=256.0)
    act(col(7), unit(4), bias=col(5), scale=8192.0)
    act(col(14), col(2), scale=256.0)
    for j, w in ((11, 2.0), (15, 4.0), (16, -256.0), (17, 1.0 / 32), (18, LIFT)):
        act(col(j), unit(2), scale=w)
    ts(a("BD"), a("IG"), col(1), Op.is_equal)
    act(a("BDF"), a("BD"))
    ts(a("ID"), a("IMP"), 0.0, Op.is_equal)
    for nm, w in list(IFS.items()) + list(IDS.items()):
        diag(a(nm), w)
    for nm, w in (("BD3", col(5)), ("BDN", -4096.0), ("BDP", 4096.0), ("BDM", 2.0 ** 22), ("BDS", col(18))):
        act(a(nm), a("BD"), scale=w)
    ts(a("BB"), a("IM"), col(4), Op.is_equal)
    for nm, w in (("B0", unit(0)), ("B03", col(5)), ("B1", unit(1)), ("BAL", 1.0), ("BK", col(6)), ("BN", -8192.0),
                  ("BP", 8192.0), ("BEP", col(7)), ("B5", unit(5))):
        act(a(nm), a("BB"), scale=w)
    act(col(19), unit(2), bias=unit(4), scale=4096.0)
    act(col(20), unit(2), bias=unit(1), scale=-8192.0)
    act(a("BC"), a("BB"), scale=col(19))
    act(a("BE"), a("BB"), scale=col(20))
    act(a("BM"), a("B0"), scale=-1.0)
    for be in range(2):
        for ga in range(2):
            ts(a("SW", 256 * be + 128 * ga, 256 * be + 128 * ga + 128), a("IMP"), 16.0 * (ga - be), Op.is_equal, col(2 + be), Op.mult)
        msum(a("DUP", 128 * be, 128 * be + 128), [("ID", a("SW", 256 * be + 128 * ga, 256 * be + 128 * ga + 128)) for ga in range(2)])
    for w in range(1, 4):
        act(a("SW", 512 * w, 512 * w + 512), a("SW", 0, 512), scale=SCALES[w])
    cp(a("SBF"), a("SBI"))
    cp(a("HEB"), a("HEI"))
    cp(a("PEB"), a("PEI"))
    tt(a("DQ"), a("HEI"), a("PEI"), Op.subtract)
    for j, x in ((1, a("HEB")), (0, a("PEB")), (3, a("DQ")), (4, a("HIC")), (5, a("LOC"))):
        dma("y", a("EN", 0, NV, p=row(j)), x)
    mm([(a("b1", 0, 256), a("DUP", 0, 128), a("SBF"))])
    mm([(a("b1", 256, 512), a("DUP", 128, 256), a("SBF"))])
    act(a("SB2"), a("b1"))
    cp(a("BXB"), a("BXI"))
    tr(a("TZ"), a("BXB"))
    iota(a("CZ"), [[0, 6], [-256, 2]], 256)
    tt(a("BI", 1, 24, 2), rowz("TZ", 0), a("CZ"), Op.subtract)
    ms(a("BI", 0, 24, 2), 0.0)
    act(a("II"), a("II"), bias=col(0))
    act(a("IB", 0, 12), a("II", 0, 12))
    act(a("II", 12, 24), a("II", 12, 24), bias=256.0)
    act(a("II", 24, 36), a("II", 24, 36), bias=-192.0)
    ts(a("T2"), a("II", 0, 12), -5.5, Op.add, 1.0 / 12, Op.mult)
    ts(a("T1", 48, 60), a("T2"), -191.0, Op.mult)
    act(a("T1", 16, 28), a("II", 0, 12), scale=16.0)
    tt(a("T1", 32, 44), a("T1", 16, 28), a("T1", 48, 60), Op.add)
    cp(a("RO"), a("T1", 32, 44))
    ts(a("WD", 0, 16), a("IM", 0, 16), col(0), Op.is_gt)
    act(a("WD", 16, 32), a("R16"), scale=-256.0)
    tt(a("WD", 0, 16), a("WD", 0, 16), a("WD", 16, 32), Op.add)
    for r in range(16):
        act(a("DG", 128 * r, 128 * r + 128), a("BD"), scale=a("WD", r, r + 1))
    iota(a("RS"), [[0, 384]])
    fill(a("RS", 193, 384, 16), SOME + 4.0 / 32)
    iota(a("TM", 0, 1), [[0, 1]])
    iota(a("CH", 0, 448), [[0, 448]])
    iota(a("CH", 448, 456), [[0, 8]], 1)
    iota(a("SKT", 256, 456), [[0, 200]])
    iota(a("YB", 192, 384), [[0, 192]])
    iota(a("CM"), [[0, 192]], -int(LIFT))
    ts(a("MA"), a("MA"), col(0), Op.is_equal)
    mm([(a("b7", 256, 512), a("ID"), a("MA", 256 * j, 256 * j + 256)) for j in range(2)])
    act(a("MT", 1, 257), a("b7", 256, 512), bias=1.0)
    iota(a("MT", 0, 1), [[0, 1]])
    iota(a("MT", 257, 272), [[0, 15]], 1)
    cp(a("LMF"), a("LMI"))
    mm([(a("b6", 16, 18), a("BDF"), a("LMF"))])
    cp(ai(5), a("b6", 16, 17))
    ts(ai(6), ai(5), 992, Op.bitwise_and)
    ts(ai(7), ai(5), 31, Op.bitwise_and)
    ts(lim(1), ai(6), unit(0), Op.mult)
    ts(lim(1), ai(7), unit(1), Op.mult, lim(1), Op.add)
    act(lim(3), unit(2), bias=lim(1), scale=160.0 * 256)
    ts(lim(2), a("b6", 17, 18), 1008.0, Op.min, -1.0, Op.mult)
    ts(ai(2), lim(2), 1023.0, Op.add)
    ts(ai(3), ai(2), 992, Op.bitwise_and)
    ts(ai(4), ai(2), 31, Op.bitwise_and)
    ts(col(12), ai(3), unit(0), Op.mult, unit(2), Op.add)
    ts(col(12), ai(4), unit(1), Op.mult, col(12), Op.add)
    fill(a("RC"), col(12))
    act(col(13), unit(0), bias=unit(1))
    act(a("W1"), a("W1"), bias=col(13), scale=col(17))
    tt(a("WC"), a("W1"), a("BD"), Op.mult)
    act(a("SBH"), a("SBF"))
    dma("y", a("JF", 0, 4096, p=row(2)), a("SBH"))
    mm([(a("b7", 0, 256), a("IDF"), a("SBF")), (a("b7", 0, 256), a("NID"), a("SBH"))])
    act(a("SBL"), a("b7", 0, 256))
    dma("y", a("JF", 0, 4096, p=row(3)), a("SBL"))
    for j in (0, 1, 4):
        dma("y", a("JF", 0, 4096, p=row(j)), a("ZR", 0, 256))
    mm(pick("b6", 128, "B1", "EN", 0, 128))
    msum(a("LO"), [("ID", band("BN", 0)), ("ID", band("BN", 1)), ("ID", band("BK", 2)), ("ID", band("BP", 3))])
    msum(a("LE"), [("ID", band("BE", 3)), ("ID", band("B0", 5)), ("ID", band("BC", 0)), ("ID", band("B5", 1))])
    msum(a("LN0"), [("ID", band("B5", 0)), ("NID", band("B5", 3))])
    act(a("LN1"), band("B5", 3))
    cp(a("SBU"), a("SBI"))
    cp(a("HEL"), a("b6", 128, 256))
    for h in range(4):
        bk = ("b1", "b7")[h % 2]
        tt(a("OH", 512 * h, 512 * h + 512), ind(a("SBF"), a("HEL", 32 * h, 32 * h + 32)), a("SIO", 512 * h, 512 * h + 512), Op.is_equal)
        mm([(a(bk), a("LE"), a("EN", 512 * h, 512 * h + 512)), (a(bk), a("LO"), a("OH", 512 * h, 512 * h + 512))])
        act(a("HT", 512 * h, 512 * h + 512), a(bk), Fn.Relu)
    for h in range(8):
        act(a("GH", 512 * h, 512 * h + 512), ind(a("HT"), a("SBU", 32 * h, 32 * h + 32)))

    def numbers(t, wide, name, lo, old, cut):
        for j0, j1 in zip(cut, cut[1:]):
            out = ind(a("X", 0, 192 + wide), a("LX", 12 * t + j0, 12 * t + j1))
            x = a(name, lo + 16 * j0, lo + 16 * j1, old=old)
            sact(out, x, Fn.Silu)
            cp(out, x)
            either()

    begin = []
    for t in range(NS):
        par[0] = t % 2
        last = t == NS - 1
        begin.append(len(ops))
        z = zof(t)
        zo = NR + NT * t
        ao = 24 * t
        box = kk(9)
        rest = a("BI", ao, ao + 24, 2)
        wide = NV + NT * t
        ts(a("LM"), a("BI", ao + 1, ao + 24, 2), 256.0, Op.add)
        tt(box, a("BI", ao + 1, ao + 24, 2), a("CZ"), Op.add)
        act(a("HK"), ind(a("HS2" if t else "SB2"), a("LM")))
        tr(a("HR"), a("HK"))
        for j0, j1 in zip(TURN, TURN[1:]):
            cp(a("L1", 16 * j0, 16 * j1), ind(a("HR"), a("RO", j0, j1)))
        banks = [("b0", 0), ("b1", 0), ("b6", 64), ("b7", 0)]
        for k0, k1 in zip(LOOKS, LOOKS[1:] if t else ()):
            act(a("G", 192 * k0, 192 * k1), ind(a("JF"), a("L1", 12 * k0, 12 * k1)))
        for (bk, lo), k0, k1 in zip(banks, PICKS, PICKS[1:] if t else ()):
            w = 12 * (k1 - k0)
            mm(pick(bk, lo, "B03", "G", 192 * k0, w))
            cp(a("CL", 12 * k0, 12 * k1), a(bk, lo, lo + w))
        if t:
            over(kk(6), rest, 0.0)
            act(rest, rest, Fn.Relu, bias=-1.0)
        mm([zero("b6", 32, 12)] + swap("b6", 32, 0, "BI", ao + 1, 2) + (swap("b6", 32, 2, "KK", 72) if t else []))
        ts(a("BX"), a("b6", 32, 44), col(14), Op.add, 448.0, Op.min)
        cp(a("BL", 0, 12), a("BX"))
        act(a("AF"), ind(a("IO"), a("BL", 0, 12)))
        lowest("ES", "AF", "BX", 0)
        over(a("NF"), a("b5", 0, 192), -256.0)
        tr(a("FZ"), a("NF"))
        mm([(a("b7", 192, 204), a("ID"), a("BX"))] + swap("b7", 192, 2, "FZ", 0, 16))
        tt(sm(1), a("b7", 192, 204), a("II", 12, 24), Op.min)
        cp(a("BL", 12, 24), sm(1))
        act(a("SK"), ind(a("SKT" if t else "SBF"), a("BL", 0, 12)))
        mm([(a("b1", 256, 448), a("ID"), a("NI")), (a("b1", 256, 448), a("NIF"), a("SK"))], True, False)
        key = a("b3", 0, 192)
        mm([(key, a("WC"), a("RC"))], True, False)
        if t:
            act(a("OD"), ind(a("CH"), a("BL", 0, 12)))
            over(a("VF"), a("OD"), 0.0)
            mm([(key, a("IDQ"), a("SK"))], False, False)
            mm([(key, a("I13"), a("VF"))], False, False)
        cl = "CL" if t else "L1"
        if t:
            gcp(a("ZZ", 0, 192), z)
        else:
            act(a("ZZ", 0, 192), z, bias=-2 * LIFT)
        gcp(a("ZZ", 192, 384), z if t else a("ZZ", 0, 192))
        gcp(a("ZZ", 384, 192 * WIDE), a("ZZ", 0, 192 * WIDE - 384))
        for k0, k1 in zip(DIFF, DIFF[1:]):
            tt(a("D", 192 * k0, 192 * k1), ind(a("X" if t else "XO", 192, 192 + wide), a(cl, 12 * k0, 12 * k1)),
               a("ZZ", 0, 192 * (k1 - k0)), Op.subtract)
        for k0, k1 in zip(ABS, ABS[1:]):
            act(a("AB", 192 * k0, 192 * k1), a("D", 192 * k0, 192 * k1), Fn.Abs, bias=-LIFT)
            mm([(key, band("BAL", k), a("AB", 192 * k, 192 * k + 192)) for k in range(k0, k1)], False, k1 == 16)
        fill(a("RS", 0, 192, 16), SOME + (4.0 + t) / 32)
        tr(a("KR"), key)
        m1, m2 = a("b2", 15, 192, 16), a("b2", 207, 384, 16)
        scan(a("b2", 0, 192), a("RS", 0, 192), a("KR"))
        ts(a32(0), m1, -4.0, Op.add)
        tt(kk(0), m1, a32(0), Op.subtract)
        mm([(a("b7", 64, 76), a("ID"), a("IB", 0, 12))] + swap("b7", 64, 3, "KK", 0))
        ts(co(0), a("b7", 64, 76), -192.0 * 116, Op.add)
        ts(kk(2), m1, SPLIT, Op.is_ge, -32768.0, Op.mult)
        tt(a("TM", 1, 192), a("b2", 0, 191), a("KR", 1, 192), Op.max)
        scan(a("b2", 192, 384), a("RS", 192, 384), a("TM"))
        ts(a32(1), m2, -4.0, Op.add)
        tt(kk(1), m2, a32(1), Op.subtract)
        if t:
            ts(a32(2, 2), a("b2", 15, 384, 16), 1024.0, Op.mult)
            ts(a32(4, 2), a32(2, 2), 4, Op.bitwise_and)
            tt(kk(3), a32(4), a32(5), Op.add)
        mm([(a("b7", 76, 88), a("ID"), a("IB", 0, 12))] + swap("b7", 76, 3, "KK", 12))
        ts(co(1), a("b7", 76, 88), -192.0 * 116, Op.add)
        for j in range(2):
            if t:
                act(a("GE", 192 * j, 192 * j + 192), ind(a("G", 0, zo + 192), co(j)))
            else:
                act(kk(7 + j), kk(j), scale=256.0)
                mm([(a("b0", 32 + 12 * j, 44 + 12 * j), a("ID"), a("BX"))] + swap("b0", 32 + 12 * j, 1, "KK", 84 + 12 * j))
                ts(co(2 + j), a("b0", 32 + 12 * j, 44 + 12 * j), -256.0 * 116, Op.add)
                act(a("GE", 192 * j, 192 * j + 192), ind(a("JF", 0, 4096), co(2 + j)))
        ne = 1 if t else 2
        e = a("b6", 0, 12)
        mm([(a("b4", 192, 384), a("BD3"), a("GE", 0, 192))])
        mm(pick("b6", 0, "BEP", "GE", 0, 12))
        de, df = a("DE", 0, 192), a("DE", 192, 384)
        act(de, ind(a("D", 0, zo + 192), co(0)))
        tt(df, ind(a("D", 0, zo + 192), co(1)), de, Op.subtract)
        ts(a("EL", 0, 12), e, float(wide - 1), Op.min)
        tt(sm(2), e, a("II", 24, 36), Op.subtract)
        if not t:
            mm(pick("b7", 160, "BEP", "GE", 192, 12))
            cp(a("EL", 12, 24), a("b7", 160, 172))
        for j in range(ne):
            act(a("NE", 192 * j, 192 * j + 192), ind(a("EN", 0, wide), a("EL", 12 * j, 12 * j + 12)))
        act(a("WH", 0, 192), de, Fn.Abs, bias=-LIFT)
        act(a("WH", 192, 384), de, bias=191.75 - LIFT / 2, scale=0.5)
        act(a("WH", 384, 576), df, Fn.Abs)
        tr(a("NZ", 0, 192 * ne), a("NE", 0, 192 * ne))
        tt(sm(4), rowz("NZ", 0), box, Op.is_equal)
        tt(sm(3), rowz("NZ", 0), box, Op.subtract)
        tt(sm(5), sm(4), rowz("NZ", 3), Op.mult)
        tt(rowz("NZ", 10), sm(5), sm(3), Op.add)
        mm([(a("b2", 192, 384), a(w), x) for (w, x) in (
            ("ID", z), ("E01", a("ONE", 0, 192)), ("ID", a("WH", 192, 384)), ("NID", a("WH", 0, 192)))])
        if not t:
            for j in range(2):
                tt(kk(3 + j), rowz("NZ", 1, 192 * j), box, Op.not_equal)
        mm([zero("b0", 88, 12)] + swap("b0", 88, 1, "KK", 0) + swap("b0", 88, 0, "KK", 24), True, False)
        mm(swap("b0", 88, 2, "KK", 12) + swap("b0", 88, 2, "KK", 36) + ([] if t else swap("b0", 88, 2, "KK", 48)), False, True)
        ts(co(4), a("b0", 88, 100), 1.0 - 17 * 116, Op.add, 257.0, Op.min)
        act(a("M"), ind(a("MT"), co(4)))
        cp(a("EF"), a("b4", 192, 384))
        lowest("EQ", "EF", "b6", 0)
        sact(a("FL", 0, 192), a("b5", 0, 192), Fn.Relu, bias=-255.0, scale=-1.0)
        ts(a("FL", 0, 192), a("b5", 0, 192), -255.5, Op.is_lt)
        either()
        tr(a("TZ"), a("FL", 0, 192))
        tt(sm(7, 2), a("TZ", 0, 192, 8), a("NZ", 2, 192, 8), Op.mult)
        tt(a("BO", ao, ao + 24), sm(7, 2), a("BI", ao, ao + 24), Op.add)
        tt(a("UU"), a("b2", 192, 384), a("FL", 0, 192), Op.mult)
        mm([(a("b0", 256, 448), a("ID"), a("WH", 0, 192)), (a("b0", 256, 448), a("ID"), a("UU"))])
        act(a("OUT", NT * t, NT * t + 192), a("b0", 256, 448), bias=0.0 if last else LIFT)
        dst = T.cores[(rank + 1) % N if not last else (rank - t) % N]
        rid, pid = topo.addr(dst, core)
        eng = topo.engines(core, dst)[:8]
        for src, land, arr in ((a("BO", ao, ao + 24), a("BI", ao + 24, ao + 48), "arr%d" % t),
                               (a("OUT", NT * t, NT * t + 192), zof(t + 1), "arz%d" % t)):
            put("g", [src], [land], lambda src=src, land=land, arr=arr, pid=pid, rid=rid, eng=eng: g.remote_dma(
                land[0], src[0], T.sem[arr], T.sem.snt, pid, rid, sum(1 << e for e in eng)), 500.0, arr, len(eng), lat=REM - 500)
        sg = a("FL", 192, 384)
        fill(a("LT"), lim(1))
        near = [("BDP", a("LT")), ("BDN", a("WH", 384, 576))]
        mm([(a("b4", 0, 192), a(w), x) for (w, x) in near])
        mm([(a("b1", 256, 448), a("I13"), a("M"))], False, True)
        act(a("Q1", 192, 384), a("b1", 256, 448), bias=float(wide - 16384))
        tt(a("Q1", 0, 192), a("b4", 0, 192), a("Q1", 192, 384), Op.min)
        if t:
            act(a("VF"), key, Fn.Relu, bias=-VOID - SOME)
            mm([(a("b3", 192, 384), a("I9"), a("VF")), (a("b3", 192, 384), a("I13"), a("M"))])
            tt(a("U1"), a("b3", 192, 384), a("OD"), Op.min)
        tt(ind(a("CH", 0, 448), a("BL", 12, 24)), a("U1") if t else a("YB", 192, 384), a("Q1", 0, 192), Op.max)
        for lo, hi in ((0, LOW), (LOW, 256)):
            act(a("CHH", lo, hi), a("CH", lo, hi))
        dma("y", a("JF", 0, 4096, p=row(0)), a("CHH"), "dh")
        tt(a("CHL", 0, LOW), a("CH", 0, LOW), a("CHH", 0, LOW), Op.subtract)
        mm([(a("b3", 256 + LOW, 512), a("IDF"), a("CH", LOW, 256))], True, False)
        mm([(a("b3", 256 + LOW, 512), a("NID"), a("CHH", LOW, 256))], False, True)
        act(a("CHL", LOW, 256), a("b3", 256 + LOW, 512))
        dma("y", a("JF", 0, 4096, p=row(1)), a("CHL"), "dl")
        mm([(a("b6", 256, 448), a(w), x) for (w, x) in near + [("BDM", a("M")), ("INF", a("NF"))]])
        sact(sg, a("b6", 256, 448), Fn.Sign, bias=-18 * 2.0 ** 22 - 2048, acc=lim(4))
        mm([(a("b4", 0, 192), a(w), x) for (w, x) in (
            ("ID", z), ("ID", de), ("IDH", df), ("IDH", a("WH", 384, 576)), ("I9", sg))])
        act(a("XO" if last else "X", 192 + wide, 384 + wide), a("b4", 0, 192), Fn.Relu, bias=-512.0 - 2 * LIFT * last)
        if not last:
            if t:
                mm([(a("b4", 192, 384), a("LN%d" % j), a("GE", 192 * j, 192 * j + 192)) for j in range(2)])
            else:
                mm([(a("b4", 192, 384), w, a("NE", 192 * j, 192 * j + 192))
                    for (w, j) in ((band("B0", 0), 0), (band("BM", 3), 0), (band("B0", 3), 1))])
            act(a("EN", wide, wide + 192), a("b4", 192, 384), bias=col(11))
            act(lim(3), lim(4), bias=lim(3), scale=col(15))
            act(a("IB", 12, 13), lim(3), bias=1.0 / 64 - 0.5, scale=1.0 / 256)
            act(lim(1), a("IB", 12, 13), bias=lim(3), scale=col(16))
        mm([zero("b6", 12, 12)] + swap("b6", 12, 0, "TZ", 0, 16))
        tt(sm(11), a("b6", 12, 24), sm(2), Op.mult)
        tt(sm(12), sm(11), a("II", 0, 12), Op.add)
        cp(a("LX", 12 * t, 12 * t + 12), sm(12))
        if t < NS - 2:
            mm([(a("b7", 256, 448), a("ID"), z), (a("b7", 256, 448), a("BDS"), a("NE", 0, 192))])
            act(a("ZL"), a("b7", 256, 448))
        if 1 <= t and not last:
            numbers(t - 1, wide, "ZL", 0, 1, FREE)
        if 3 <= t and not last:
            act(a("ZM", 192, 384), zof(t - 2), bias=LIFT)
            numbers(t - 2, wide, "ZM", 192, 0, FREE)
        if not last:
            act(a("ZM", 0, 192), z, bias=2 * LIFT)
            numbers(t, wide, "ZM", 0, 0, (0, 12))
        if t == 0:
            act(a("OWN"), a("OWN"), bias=col(6))
            for lo in (0, 128):
                mm(pick("b6", 128 + lo, "B03", "GH", 16 * lo, 128))
                act(a("HSK", lo, lo + 128), a("b6", 128 + lo, 256 + lo))
                for be in range(2):
                    mm([(a("b7", 256 + 128 * be, 384 + 128 * be), a("DUP", 128 * be, 128 * be + 128), a("HSK", lo, lo + 128))])
                    act(a("HS2", 256 * be + lo, 256 * be + lo + 128), a("b7", 256 + 128 * be, 384 + 128 * be))
                mm(pick("b4", lo, "B5", "GH", 16 * lo, 128))
                act(a("PK", lo, lo + 128), a("b4", lo, lo + 128))
            dma("y", a("JF", 0, 4096, p=row(5)), a("PK"))
            tt(a("MA", 0, 256), a("b6", 128, 384), a("OWN"), Op.not_equal)
            mm([(a("b7", 256, 512), a(w), x) for (w, x) in (("ID", a("SBH")), ("ID", a("SBL")), ("I13", a("MA", 0, 256)))])
            act(a("SKT", 0, 256), a("b7", 256, 512))

    for lo in range(192, 192 + wide, 400):
        act(a("XT", lo, lo + 400), a("X", lo, lo + 400), bias=128 - 2 * LIFT)
        act(a("XO", lo, lo + 400), a("XT", lo, lo + 400), Fn.Relu, bias=-128.0)
    for t in range(NS - 3, NS):
        tt(ind(a("XO", 0, 192 + wide), a("LX", 12 * t, 12 * t + 12)), zof(t), a("CM"), Op.add)
    for h in range(4):
        dma("y", hbm(T.yx[:, 848 * h:848 * h + 848]), a("XO", 192 + 848 * h, 192 + 848 * h + 848), None, 3000.0)
    mm([(a("b7", 256, 384), band("B03", r), a("HT", 128 * r, 128 * r + 128)) for r in range(16)])
    cp(a("HL"), a("b7", 256, 384))
    for h in range(4):
        act(a("G", 512 * h, 512 * h + 512), ind(a("JF"), a("HL", 32 * h, 32 * h + 32)))
    dma("y", hbm(T.yz[:]), zof(NS))
    tt(rowz("YB", 0, 192), a("BI", 24 * NS + 1, 24 * NS + 24, 2), a("CZ"), Op.add)
    for h in range(2):
        mm(pick(("b4", "b6")[h], 0, "B03", "G", 1024 * h, 64))
        act(a("YJ", 64 * h, 64 * h + 64), a(("b4", "b6")[h], 0, 64))
    tr(a("YB", 0, 192), a("YB", 192, 384))
    dma("s", hbm(T.yb[:]), a("YB", 0, 192, p=row(0)))
    dma("y", hbm(T.yj[:]), a("YJ"))

    def clash(r, s):
        return r[1] < s[2] and s[1] < r[2] and (r[3] is None or s[3] is None or r[3] == s[3])

    def covers(r, s):
        return r[1] <= s[1] and s[2] <= r[2] and r[3] in (None, s[3])

    seen = {}
    for i, o in enumerate(ops):
        dep = set()
        for r in o["r"]:
            dep.update(j for (s, w, j) in seen.get(r[0], []) if w and clash(r, s))
        for r in o["w"]:
            dep.update(j for (s, w, j) in seen.get(r[0], []) if clash(r, s))
        o["dep"] = dep
        for r in o["w"]:
            seen[r[0]] = [x for x in seen.get(r[0], []) if not covers(r, x[0])] + [(r, True, i)]
        for r in set(o["r"]):
            seen.setdefault(r[0], []).append((r, False, i))
        o["bk"] = sorted(set(r[0] for r in o["r"] + o["w"] if r[0][0] == "b"))
    n = len(ops)
    deps = [sorted(o["dep"]) for o in ops]
    above = []
    for i in range(n):
        m = 0
        for j in deps[i]:
            m |= above[j]
        keep = [j for j in deps[i] if not m >> j & 1]
        for j in deps[i]:
            m |= 1 << j
        above.append(0 if ops[i]["sem"][:2] == "ar" else m)
        deps[i] = keep
    kids = [[] for o in ops]
    for i in range(n):
        for j in deps[i]:
            kids[j].append(i)

    names, count, kd = {}, {}, []
    for i, o in enumerate(ops):
        t = sum(i >= b for b in begin) - 1
        what = (o["e"], "alt" in o, tuple(r[0] for r in o["w"][:1] + o["r"][:2]))
        count[t, what] = count.get((t, what), 0) + 1
        kd.append(names.setdefault((min(max(t, 0), 1) + (t == NS - 1), what, count[t, what] if t > 0 else i), len(names)))
    kinds = len(names)
    tail = [o["lat"] + LAT for o in ops]
    forms = [[(o["e"], o["c"])] + ([(o["alt"]["e"], o["alt"]["c"])] if "alt" in o else []) for o in ops]
    banks = [o["bk"] for o in ops]
    cont = [o["cont"] for o in ops]
    pad = LAT + 70.0

    def lay(lean):
        way = [0.0] * n
        for i in range(n - 1, -1, -1):
            way[i] = max([way[k] for k in kids[i]], default=0.0) + forms[i][0][1] + tail[i] + lean[kd[i]]
        order = sorted(range(n), key=lambda i: -way[i])
        left = [len(p) for p in deps]
        at = [0.0] * n
        form = [0] * n
        busy = {k: [] for k in list(Q) + ["b%d" % b for b in range(8)]}
        done = [False] * n
        low, span = 0, 0.0
        for turn in range(n):
            while done[order[low]]:
                low += 1
            j = low
            while done[order[j]] or left[order[j]]:
                j += 1
            i = order[j]
            done[i] = True
            found = None
            for f, (e, c) in enumerate(forms[i]):
                s0 = at[i]
                moved = True
                while moved:
                    moved = False
                    for (b, gap) in [(e, 0.0)] + [(b, pad) for b in banks[i]]:
                        lst = busy[b]
                        j = len(lst)
                        while j and lst[j - 1][1] + gap > s0:
                            j -= 1
                        while j < len(lst) and lst[j][0] - gap < s0 + c:
                            if (b == e or lst[j][2] != e) and s0 < lst[j][1] + gap:
                                s0 = lst[j][1] + gap
                                moved = True
                            j += 1
                if found is None or s0 + c + WISH < found[0] + found[3]:
                    found = (s0, f, e, c)
            s0, f, e, c = found
            at[i], form[i] = s0, f
            for b in [e] + banks[i]:
                lst = busy[b]
                j = len(lst)
                while j and lst[j - 1][0] > s0:
                    j -= 1
                lst.insert(j, (s0, s0 + c, e))
            span = max(span, s0 + c + tail[i])
            for k in kids[i]:
                at[k] = max(at[k], s0 + c + (0.0 if e == "t" and cont[k] else tail[i]))
                left[k] -= 1
        return span, at, form

    rooms = list(Q) + ["b%d" % b for b in range(8)]
    job = [[(rooms.index(e), c, [rooms.index(b) for b in banks[i]], c + tail[i],
             [(k, c if e == "t" and cont[k] else c + tail[i]) for k in kids[i]]) for (e, c) in forms[i]] for i in range(n)]
    kda = np.array(kd)

    def run(place, alt, base, lo, hi, left):
        order = (np.argsort(base[lo:hi] + place[kda[lo:hi]], kind="stable") + lo).tolist()
        left = list(left)
        at = [0.0] * n
        why = [-1] * n
        held = set()
        till, who, by = [0.0] * len(rooms), [-1] * len(rooms), [-1] * len(rooms)
        wait = []
        span = tip = 0
        for i in order:
            if left[i]:
                wait.append(i)
                continue
            while i >= 0:
                e, c, bks, full, after = job[i][alt[kd[i]]]
                s0 = at[i]
                if till[e] > s0:
                    s0, why[i] = till[e], who[e]
                    held.add(i)
                for b in bks:
                    if by[b] != e and till[b] + pad > s0:
                        s0, why[i] = till[b] + pad, who[b]
                        held.add(i)
                at[i] = s0
                till[e], who[e] = s0 + c, i
                for b in bks:
                    till[b], who[b], by[b] = s0 + c, i, e
                if s0 + full > span:
                    span, tip = s0 + full, i
                for k, w in after:
                    if at[k] < s0 + w:
                        at[k], why[k] = s0 + w, i
                    left[k] -= 1
                i = -1
                for j in range(len(wait)):
                    if not left[wait[j]]:
                        i = wait.pop(j)
                        break
        pairs = []
        while tip >= 0:
            if tip in held:
                pairs.append((tip, why[tip]))
            tip = why[tip]
        return span, at, place, alt, pairs

    def tune(place, alt, base, lo, hi, some, turns, heat, rng):
        left = [sum(j >= lo for j in p) for p in deps]
        now = best = run(place, alt, base, lo, hi, left)
        for turn, u in enumerate(rng.rand(turns, 5).tolist()):
            i, j = now[4][int(u[0] * len(now[4]))]
            way = 1.0
            if u[1] < 0.5:
                i, j, way = j, i, -1.0
            r, f = now[2].copy(), now[3]
            to = base[j] + r[kd[j]] - way * (1.0 + SIG * u[2] ** 4)
            if turn % 3 == 0:
                i = lo + int(u[0] * (hi - lo))
                to = base[i] + r[kd[i]] - way * 4 * SIG * u[2] ** 2
            if kd[i] not in some:
                continue
            if len(forms[i]) > 1 and u[3] < 0.3:
                f = list(f)
                f[kd[i]] ^= 1
            else:
                more = [(i, to)]
                while more:
                    i, to = more.pop()
                    r[kd[i]] = to - base[i]
                    more += [(j, to - way) for j in (deps if way > 0 else kids)[i]
                             if lo <= j < hi and kd[j] in some and (base[j] + r[kd[j]] - to) * way > 0 and base[i] == base[j]]
            new = run(r, f, base, lo, hi, left)
            if new[0] <= now[0] - heat * (1 - turn / turns) ** 2 * float(np.log(u[4])):
                now = new
                if now[0] < best[0]:
                    best = now
        return best

    if not PLAN:
        rng = np.random.RandomState(SEED)
        lean = [0.0] * kinds
        best = lay(lean)
        for turn in range(TURNS // 200):
            new = list(lean)
            for k in rng.randint(0, kinds, 1 + turn % 4):
                new[k] += float(rng.normal()) * SIG
            got = lay(new)
            if got[0] <= best[0]:
                best, lean = got, new
        sends = [0.0] + [best[1][i] for i in range(n) if ops[i]["sem"][:3] == "arr"]
        base = np.array([sends[max(sum(i >= b for b in begin) - 1, 0)] for i in range(n)])
        place, alt = np.zeros(kinds), [0] * kinds
        for i in list(range(n)) + list(range(begin[3], begin[5])):
            place[kd[i]], alt[kd[i]] = best[1][i] - base[i], best[2][i]
        for lo, hi, k0, k1, turns, heat in ((begin[2], begin[6], begin[1], begin[6], TURNS, HEAT), (0, begin[2], 0, begin[1], TURNS, HEAT),
                                            (begin[5], n, begin[6], n, TURNS // 3, HEAT / 2), (0, n, 0, n, TURNS // 4, HEAT / 4)):
            best = tune(place, alt, base, lo, hi, set(kd[k0:k1]), turns, heat, rng)
            place, alt = best[2], best[3]
        PLAN.append(sorted(range(n), key=lambda i: (best[1][i], i)))
        PLAN.append([alt[k] for k in kd])
        PLAN.append(best[0])
    for i in range(n):
        if PLAN[1][i]:
            ops[i].update(ops[i]["alt"])
    clock = {k: {} for k in Q}
    total = {}
    tok = {}
    user = {}
    for i in PLAN[0]:
        o = ops[i]
        e = o["e"]
        need = [j for j in deps[i] if not (o["cont"] and ops[j]["e"] == "t")]
        need += [user[b] for b in o["bk"] if b in user and ops[user[b]]["e"] != e]
        for j in sorted(need, key=lambda j: -tok[j][1]):
            sem, m, c = tok[j]
            if clock[e].get(sem, 0) < m:
                Q[e].wait_ge(T.sem[sem], m)
                for k, v in c.items():
                    if clock[e].get(k, 0) < v:
                        clock[e][k] = v
        ins = o["call"]()
        sem = o["sem"]
        total[sem] = total.get(sem, 0) + o["n"]
        if sem[:2] == "ar":
            total["snt"] = total.get("snt", 0) + o["n"]
            tok[i] = (sem, total[sem], {sem: total[sem]})
        else:
            ins.then_inc(T.sem[sem], o["n"])
            c = dict(clock[e])
            c[sem] = total[sem]
            tok[i] = (sem, total[sem], c)
        for b in o["bk"]:
            user[b] = i
    for s, m in total.items():
        g.wait_ge(T.sem[s], m)
